import numpy as np
import ml_dtypes


def mxq(x, axis, fmt="e4m3"):
    dtype, down = {"e4m3": (ml_dtypes.float8_e4m3fn, 7), "e5m2": (ml_dtypes.float8_e5m2, 14)}[fmt]
    v = np.moveaxis(np.asarray(x, np.float32).astype(ml_dtypes.bfloat16).astype(np.float64), axis, -1)
    blocks = v.reshape(v.shape[:-1] + (-1, 32))
    amax = np.abs(blocks).max(-1, keepdims=True)
    byte = np.maximum(np.where(amax > 0, np.frexp(amax)[1] - 1 + 127, 0) - down, 1)
    scale = np.exp2(byte - 127.0)
    codes = (blocks / scale).astype(np.float32).astype(dtype).astype(np.float64)
    return np.moveaxis((codes * scale).reshape(v.shape), -1, axis)


WIDE = False


def mx_kscale(k):
    if not WIDE:
        return np.ones(k)
    levels = np.array([10, -10, 5, -5, 0])
    if k % 512:
        return np.exp2(np.random.permutation(np.resize(levels, k // 32))).repeat(32)
    a = np.empty((k // 512, 16))
    for p in range(k // 512):
        a[p, :8] = np.random.permutation(np.resize(levels, 8))
        for g in range(8):
            far = levels[np.abs(levels - a[p, g]) >= 10]
            a[p, g + 8] = far[np.random.randint(len(far))]
    return np.exp2(a.ravel()).repeat(32)


BF16 = ml_dtypes.bfloat16


def bf(x):
    return np.asarray(x, np.float32).astype(BF16)


def f64(x):
    return np.asarray(x).astype(np.float64)


T, D, H, N = 4096, 512, 4, 32
TWO = 2
C = H * TWO * N
SLOTS = N * N


def draw0():
    s = mx_kscale(D)
    t = mx_kscale(SLOTS)
    return {
        "x": bf(np.random.standard_normal((T, D)) * s),
        "wk": bf(np.random.standard_normal((D, C)) * 1.5 / np.sqrt(D) / s[:, None]),
        "slot_gain": bf(np.random.standard_normal(SLOTS) * np.sqrt(SLOTS) * t),
        "values": bf(np.random.standard_normal((SLOTS, D)) * 2.0 / np.sqrt(SLOTS) / t[:, None]),
        "wg": bf(np.random.standard_normal((D, D)) * 1.5 / np.sqrt(D) / s[:, None]),
    }


def softmax(v):
    e = np.exp(v - v.max(-1, keepdims=True))
    return e / e.sum(-1, keepdims=True)


def product_key_weights(sc):
    p = softmax(sc)
    p1 = p[:, :, 0, :]
    p2 = p[:, :, 1, :]
    w = np.sum(p1[:, :, :, None] * p2[:, :, None, :], axis=1)
    return w.reshape(w.shape[0], SLOTS)


def core(x, wk, slot_gain, values, wg):
    xq = mxq(f64(x), 1, "e4m3")
    sc = (xq @ mxq(f64(wk), 0, "e4m3")).reshape(x.shape[0], H, TWO, N)
    w = product_key_weights(sc)
    wg_slots = w * f64(slot_gain)[None, :]
    mem = mxq(wg_slots, 1, "e4m3") @ mxq(f64(values), 0, "e4m3")
    a = xq @ mxq(f64(wg), 0, "e4m3")
    gate = a * (1.0 / (1.0 + np.exp(-a)))
    return mem * gate


def e4m3fn_bytes(y):
    return np.clip(np.asarray(y, np.float64), -448.0, 448.0).astype(np.float32).astype(ml_dtypes.float8_e4m3fn).view(np.uint8)


def e4m3fn_values(b):
    return np.asarray(b, np.uint8).view(ml_dtypes.float8_e4m3fn).astype(np.float64)


def setup_inputs():
    d = draw0()
    x0 = np.asarray(d['x']).astype(np.float64)
    s = (np.max(np.abs(x0), axis=(0,), keepdims=True) / 448.0).astype(np.float32)
    out = {}
    for k, v in d.items():
        if k == 'x':
            out['x_bytes'] = e4m3fn_bytes(x0 / s.astype(np.float64))
            out['x_scale'] = s
        else:
            out[k] = v
    return out


def reference(x_bytes, x_scale, wk, slot_gain, values, wg):
    return core(e4m3fn_values(x_bytes) * x_scale.astype(np.float64), wk, slot_gain, values, wg)

@@ -1,0 +1,417 @@
+from contextlib import ExitStack
+
+import concourse.mybir as mybir
+from concourse.masks import make_identity
+
+F32 = mybir.dt.float32
+BF16 = mybir.dt.bfloat16
+U32 = mybir.dt.uint32
+U8 = mybir.dt.uint8
+FP8 = mybir.dt.float8_e4m3fn
+FP8X4 = mybir.dt.float8_e4m3fn_x4
+ACT = mybir.ActivationFunctionType
+ALU = mybir.AluOpType
+AX = mybir.AxisListType
+
+T, D, H, N = 4096, 512, 4, 32
+C = H * 2 * N
+SLOTS = N * N
+P = 128
+NT = T // P
+
+FLOPS = 2 * T * D * C + 2 * T * SLOTS * D + 2 * T * D * D
+
+V_WHOLE = 0
+G_WHOLE = 3
+SHARED = (1, 0)
+S_HALVES = [(1, 1), (2, 0), (2, 1)]
+
+X_CHUNKS = [(0, 2), (2, 8), (8, 16), (16, 24), (24, 32)]
+
+
+def tile_productkeysoftmemoryplus_t_kernel(
+    tc, x_bytes, x_scale, wk, slot_gain, values, wg, out
+):
+    nc = tc.nc
+    x_view = x_bytes.rearrange("(p n) d -> p n d", n=NT)
+    out_view = out.rearrange("(p n) d -> p n d", n=NT)
+
+    with ExitStack() as ctx:
+        keep = ctx.enter_context(tc.tile_pool(name="keep", bufs=1))
+        work = ctx.enter_context(tc.tile_pool(name="work", bufs=2))
+        psum = ctx.enter_context(tc.psum_pool(name="psum", bufs=1))
+        ctx.enter_context(tc.manual_schedule())
+
+        xraw = []
+        for a, b in X_CHUNKS:
+            xr = keep.tile([P, b - a, D], U8, name="xraw%d" % a, align_bytes=64)
+            xraw.append(xr)
+        scale_sb = keep.tile([P, D], F32, name="scale_sb")
+        wg_raw = keep.tile([P, 4, D], BF16, name="wg_raw")
+        wk_raw = keep.tile([P, 4, C], BF16, name="wk_raw")
+        v_raw = keep.tile([P, 2, 4, D], BF16, name="v_raw")
+        gain_sb = keep.tile([P, 2, 4], BF16, name="gain_sb")
+
+        def load_x(i):
+            a, b = X_CHUNKS[i]
+            nc.sync.dma_start(out=xraw[i][:], in_=x_view[:, a:b, :])
+
+        nc.sync.dma_start(out=scale_sb[:], in_=x_scale.rearrange("o k -> (o k)").partition_broadcast(P))
+        load_x(0)
+        nc.sync.dma_start(out=wg_raw[:], in_=wg.rearrange("(p j) c -> p j c", j=4))
+        load_x(1)
+        nc.sync.dma_start(out=wk_raw[:], in_=wk.rearrange("(p j) c -> p j c", j=4))
+        load_x(2)
+        for g in range(2):
+            nc.sync.dma_start(
+                out=v_raw[:, g, :, :],
+                in_=values[512 * g : 512 * (g + 1), :].rearrange("(p j) c -> p j c", j=4),
+            )
+        nc.sync.dma_start(out=gain_sb[:], in_=slot_gain.rearrange("(g p t) -> p g t", p=P, t=4))
+        load_x(3)
+        load_x(4)
+
+        ident = keep.tile([P, P], F32, name="ident")
+        make_identity(nc, ident[:])
+        warm = keep.tile([P, 1], F32, name="warm")
+        nc.gpsimd.memset(warm[:], 0.0)
+        warm_out = keep.tile([P, 1], F32, name="warm_out")
+        nc.scalar.activation(out=warm_out[:], in_=warm[:], func=ACT.Silu)
+
+        x_codes = keep.tile([P, T], U32, name="x_codes", align_bytes=64)
+        x_planes = keep.tile([P, T], U8, name="x_planes", align_bytes=64)
+        wg_codes = keep.tile([P, D], U32, name="wg_codes", align_bytes=64)
+        wg_planes = keep.tile([P, D], U8, name="wg_planes", align_bytes=64)
+        wk_codes = keep.tile([P, C], U32, name="wk_codes", align_bytes=64)
+        wk_planes = keep.tile([P, C], U8, name="wk_planes", align_bytes=64)
+        v_codes = keep.tile([P, 2, D], U32, name="v_codes", align_bytes=64)
+        v_planes = keep.tile([P, 2, D], U8, name="v_planes", align_bytes=64)
+        gate = keep.tile([P, NT, D], F32, name="gate")
+
+        wg_il = keep.tile([P, D, 4], BF16, name="wg_il", align_bytes=64)
+
+        def wk_copy():
+            wk_il = keep.tile([P, C, 4], BF16, name="wk_il", align_bytes=64)
+            nc.vector.tensor_copy(out=wk_il[:], in_=wk_raw[:].rearrange("p j c -> p c j"))
+            state["wk_il"] = wk_il
+
+        def wk_quant():
+            nc.vector.quantize_mx(
+                out=wk_codes[:].bitcast(FP8X4),
+                scales=wk_planes[:],
+                in_=state["wk_il"][:].rearrange("p c j -> p (c j)"),
+            )
+
+        def v_copy(i):
+            g, b = divmod(i, 2)
+            v_il = work.tile([P, 256, 4], BF16, name="v_il", align_bytes=64)
+            nc.vector.tensor_copy(
+                out=v_il[:],
+                in_=v_raw[:, g, :, 256 * b : 256 * (b + 1)].rearrange("p j c -> p c j"),
+            )
+            state["v_il", i] = v_il
+
+        def v_quant(i):
+            g, b = divmod(i, 2)
+            cols = slice(256 * b, 256 * (b + 1))
+            nc.vector.quantize_mx(
+                out=v_codes[:, g, cols].bitcast(FP8X4),
+                scales=v_planes[:, g, cols],
+                in_=state["v_il", i][:].rearrange("p c j -> p (c j)"),
+            )
+
+        state = {}
+        prep = {5: [wk_copy], 6: [wk_quant]}
+        for i in range(4):
+            prep.setdefault(7 + 2 * i, []).append(lambda i=i: v_copy(i))
+            prep.setdefault(8 + 2 * i, []).append(lambda i=i: v_quant(i))
+
+        def x_product(q):
+            xb = work.tile([P, 2, D], BF16, name="xb", bufs=3, align_bytes=64)
+            for s in range(2):
+                n = 2 * q + s
+                i = [k for k, (a, b) in enumerate(X_CHUNKS) if a <= n < b][0]
+                nc.vector.tensor_tensor(
+                    out=xb[:, s, :],
+                    in0=xraw[i][:, n - X_CHUNKS[i][0], :].bitcast(FP8),
+                    in1=scale_sb[:],
+                    op=ALU.mult,
+                )
+            state["xb", q] = xb
+
+        def x_transpose(q):
+            words = state["xb", q][:].rearrange("p s d -> p (s d)").bitcast(F32)
+            xt = psum.tile([P, 2, 2, P], F32, name="xt", tag="sc", bufs=2)
+            for s in range(2):
+                for u in range(2):
+                    nc.tensor.transpose(
+                        xt[:, s, u, :], words[:, 256 * s + u : 256 * (s + 1) : 2], ident[:]
+                    )
+            state["xt", q] = xt
+
+        def x_copy(q):
+            xg = work.tile([P, 2 * P, 4], BF16, name="xg", bufs=4, align_bytes=64)
+            nc.scalar.copy(
+                out=xg[:].rearrange("p k t -> p (k t)").bitcast(F32).rearrange(
+                    "p (s k u) -> p s k u", s=2, u=2
+                ),
+                in_=state["xt", q][:].rearrange("p s u k -> p s k u"),
+            )
+            state["xg", q] = xg
+
+        def x_quant(q):
+            cols = slice(256 * q, 256 * (q + 1))
+            nc.vector.quantize_mx(
+                out=x_codes[:, cols].bitcast(FP8X4),
+                scales=x_planes[:, cols],
+                in_=state["xg", q][:].rearrange("p k t -> p (k t)"),
+            )
+
+        def mx_x(dst, n, codes, planes):
+            cols = slice(P * n, P * (n + 1))
+            nc.tensor.matmul_mx(
+                out=dst,
+                lhsT=x_codes[:, cols].bitcast(FP8X4),
+                lhsT_scale=x_planes[:, cols],
+                rhs=codes[:].bitcast(FP8X4),
+                rhs_scale=planes[:],
+                start=True,
+                stop=True,
+            )
+
+        def gate_matmul(q):
+            for s in range(2):
+                a_ps = psum.tile([P, D], F32, name="a_ps", tag="ub", bufs=3)
+                mx_x(a_ps[:], 2 * q + s, wg_codes, wg_planes)
+                state["a", 2 * q + s] = a_ps
+
+        def gate_silu(q):
+            for n in (2 * q, 2 * q + 1):
+                nc.scalar.activation(out=gate[:, n, :], in_=state["a", n][:], func=ACT.Silu)
+
+        NQ = NT // 2
+        for q in range(NQ + 5):
+            if 0 <= q - 4 < NQ:
+                gate_matmul(q - 4)
+            if 0 <= q - 1 < NQ:
+                x_transpose(q - 1)
+            if 0 <= q - 5 < NQ:
+                gate_silu(q - 5)
+            if 0 <= q - 2 < NQ:
+                x_copy(q - 2)
+            if q < NQ:
+                x_product(q)
+            if q == 1:
+                nc.vector.tensor_copy(out=wg_il[:], in_=wg_raw[:].rearrange("p j c -> p c j"))
+            if q == 2:
+                nc.vector.quantize_mx(
+                    out=wg_codes[:].bitcast(FP8X4),
+                    scales=wg_planes[:],
+                    in_=wg_il[:].rearrange("p c j -> p (c j)"),
+                )
+            for f in prep.get(q, []):
+                f()
+            if 0 <= q - 3 < NQ:
+                x_quant(q - 3)
+
+        def scores(n):
+            sc = psum.tile([P, C], F32, name="sc_ps", tag="sc", bufs=2)
+            mx_x(sc[:], n, wk_codes, wk_planes)
+            state["sc", n] = sc
+
+        def maxima(n):
+            nm = work.tile([P, 2 * H], F32, name="nm", bufs=3)
+            nc.vector.tensor_reduce(
+                out=nm[:],
+                in_=state["sc", n][:].rearrange("p (c k) -> p c k", k=N),
+                axis=AX.X,
+                op=ALU.max,
+                negate=True,
+            )
+            state["nm", n] = nm
+
+        def exps(n):
+            e = work.tile([P, 2, H, N], F32, name="e", bufs=4)
+            z = work.tile([P, 2 * H], F32, name="z", bufs=3)
+            sc, nm = state["sc", n], state["nm", n]
+            for half in range(2):
+                for h in range(H):
+                    c = 2 * h + half
+                    src = sc[:, N * c : N * (c + 1)]
+                    dst = e[:, half, h, :]
+                    if half == 1:
+                        src = src.rearrange("p (m t) -> p t m", t=4)
+                        dst = dst.rearrange("p (t m) -> p t m", t=4)
+                    nc.scalar.activation(
+                        out=dst,
+                        in_=src,
+                        func=ACT.Exp,
+                        bias=nm[:, c : c + 1],
+                        accum_out=z[:, H * half + h : H * half + h + 1],
+                    )
+            state["e", n], state["z", n] = e, z
+
+        def recips(n):
+            rz = work.tile([P, 2 * H], F32, name="rz", bufs=3)
+            nc.vector.reciprocal(out=rz[:], in_=state["z", n][:])
+            state["rz", n] = rz
+
+        def normalise(n):
+            if n % 2 == 0:
+                pn = work.tile([P, 2, 2 * H, N], F32, name="pn", bufs=3)
+                state["pn2", n // 2] = pn
+            pn = state["pn2", n // 2]
+            nc.gpsimd.tensor_tensor(
+                out=pn[:, n % 2, :, :],
+                in0=state["e", n][:].rearrange("p a h k -> p (a h) k"),
+                in1=state["rz", n][:].unsqueeze(2).broadcast_to([P, 2 * H, N]),
+                op=ALU.mult,
+            )
+            state["pn", n] = pn[:, n % 2, :, :].rearrange("p (a h) k -> p a h k", a=2)
+
+        def p2_to_psum(q):
+            p2 = psum.tile([P, 2, 2, N], F32, name="p2_ps", tag="p2", bufs=2)
+            nc.tensor.matmul(
+                p2[:].rearrange("p s h k -> p s (h k)"),
+                lhsT=ident[:],
+                rhs=state["pn2", q][:, :, H : H + 2, :].rearrange("p s h k -> p s (h k)"),
+                start=True,
+                stop=True,
+            )
+            state["p2", 2 * q], state["p2", 2 * q + 1] = p2[:, 0, :, :], p2[:, 1, :, :]
+
+        def wide_product(eng, n, h, lo, hi, p2, pr):
+            ni = hi - lo
+            p1 = state["pn", n][:, 0, h, lo:hi]
+            eng.tensor_tensor(
+                out=pr[:].rearrange("p t (i m) -> p t i m", m=8),
+                in0=p1.unsqueeze(1).unsqueeze(3).broadcast_to([P, 4, ni, 8]),
+                in1=p2.rearrange("p (t m) -> p t m", t=4).unsqueeze(2).broadcast_to([P, 4, ni, 8]),
+                op=ALU.mult,
+            )
+
+        def whole_product(eng, n, h, p2):
+            pr = work.tile([P, 4, 2 * P], F32, name="pr%d" % h, bufs=2)
+            wide_product(eng, n, h, 0, N, p2, pr)
+            state["pr", n, h, 0] = pr[:, :, 0:P]
+            state["pr", n, h, 1] = pr[:, :, P : 2 * P]
+
+        def half_product(eng, n, h, g, p2):
+            pr = work.tile([P, 4, P], F32, name="pr%d_%d" % (h, 16 * g), bufs=2)
+            wide_product(eng, n, h, 16 * g, 16 * (g + 1), p2, pr)
+            state["pr", n, h, g] = pr[:]
+
+        def scalar_product(n, h, g):
+            pr = work.tile([P, 4, P], F32, name="pr%d_%d" % (h, 16 * g), bufs=2)
+            for i in range(16):
+                ii = 16 * g + i
+                nc.scalar.activation(
+                    out=pr[:, :, 8 * i : 8 * (i + 1)],
+                    in_=state["pn", n][:, 1, h, :].rearrange("p (t m) -> p t m", t=4),
+                    func=ACT.Copy,
+                    scale=state["pn", n][:, 0, h, ii : ii + 1],
+                )
+            state["pr", n, h, g] = pr[:]
+
+        def sum_heads(n, g):
+            ub = psum.tile([P, 4, P], F32, name="ub_ps", tag="ub", bufs=3)
+            for t in range(4):
+                for h in range(H):
+                    nc.tensor.matmul(
+                        ub[:, t, :],
+                        lhsT=state["pr", n, h, g][:, t, :],
+                        rhs=ident[:],
+                        start=(h == 0),
+                        stop=(h == H - 1),
+                        is_transpose=True,
+                    )
+            state["ub", n, g] = ub
+
+        def gain(n, g):
+            if g == 0:
+                u = work.tile([P, 2, P, 4], BF16, name="u", align_bytes=64)
+                state["u", n] = u
+            nc.vector.tensor_tensor(
+                out=state["u", n][:, g, :, :],
+                in0=state["ub", n, g][:].rearrange("p t k -> p k t"),
+                in1=gain_sb[:, g, :].unsqueeze(1).broadcast_to([P, P, 4]),
+                op=ALU.mult,
+            )
+
+        def u_quant(n):
+            uc = work.tile([P, 2 * P], U32, name="uc", align_bytes=64)
+            us = work.tile([P, 2 * P], U8, name="us", align_bytes=64)
+            nc.vector.quantize_mx(
+                out=uc[:].bitcast(FP8X4),
+                scales=us[:],
+                in_=state["u", n][:].rearrange("p g k t -> p (g k t)"),
+            )
+            state["uc", n] = (uc, us)
+
+        def memory(n):
+            mem = psum.tile([P, D], F32, name="mem", tag="mem", bufs=1)
+            uc, us = state["uc", n]
+            for g in range(2):
+                cols = slice(P * g, P * (g + 1))
+                nc.tensor.matmul_mx(
+                    out=mem[:],
+                    lhsT=uc[:, cols].bitcast(FP8X4),
+                    lhsT_scale=us[:, cols],
+                    rhs=v_codes[:, g, :].bitcast(FP8X4),
+                    rhs_scale=v_planes[:, g, :],
+                    start=(g == 0),
+                    stop=(g == 1),
+                )
+            state["mem", n] = mem
+
+        def final(n):
+            o = work.tile([P, D], F32, name="o", bufs=4)
+            nc.vector.tensor_tensor(
+                out=o[:], in0=state["mem", n][:], in1=gate[:, n, :], op=ALU.mult
+            )
+            nc.sync.dma_start(out=out_view[:, n, :], in_=o[:])
+
+        def has(n):
+            return 0 <= n < NT
+
+        def shared_on_scalar(n):
+            return n % 2 == 1
+
+        for s in range(-5, NT + 3):
+            if has(s - 2):
+                memory(s - 2)
+            if has(s + 5):
+                scores(s + 5)
+            if has(s + 3):
+                normalise(s + 3)
+            if has(s + 1):
+                whole_product(nc.gpsimd, s + 1, G_WHOLE, state["pn", s + 1][:, 1, G_WHOLE, :])
+            if has(s):
+                sum_heads(s, 0)
+            if s % 2 == 0 and has(s + 2):
+                p2_to_psum(s // 2 + 1)
+            if has(s):
+                sum_heads(s, 1)
+            for k in range(3):
+                if has(s + 1):
+                    scalar_product(s + 1, *S_HALVES[k])
+                if k == 0 and has(s + 4):
+                    exps(s + 4)
+            if has(s + 1) and shared_on_scalar(s + 1):
+                scalar_product(s + 1, *SHARED)
+            if has(s - 1):
+                gain(s - 1, 0)
+            if has(s + 1):
+                whole_product(nc.vector, s + 1, V_WHOLE, state["p2", s + 1][:, 0, :])
+            if has(s - 1):
+                gain(s - 1, 1)
+            if has(s - 2):
+                final(s - 2)
+            if has(s + 1) and not shared_on_scalar(s + 1):
+                half_product(nc.vector, s + 1, *SHARED, state["p2", s + 1][:, 1, :])
+            if has(s - 1):
+                u_quant(s - 1)
+            if has(s + 4):
+                recips(s + 4)
+            if has(s + 5):
+                maxima(s + 5)

@@ -18,13 +18,15 @@ C = H * 2 * N
 SLOTS = N * N
 P = 128
 NT = T // P
+NPAIR = NT // 2
 
 FLOPS = 2 * T * D * C + 2 * T * SLOTS * D + 2 * T * D * D
 
-V_WHOLE = 0
-G_WHOLE = 3
-SHARED = (1, 0)
-S_HALVES = [(1, 1), (2, 0), (2, 1)]
+V_HEAD, G_HEAD = 0, 3
+S_HALVES = [(1, 0), (2, 0), (2, 1)]
+CUT_HALF = (1, 1)
+V_PLANES = 2
+V_KEYS = N + 8 * V_PLANES
 
 X_CHUNKS = [(0, 2), (2, 8), (8, 16), (16, 24), (24, 32)]
 
@@ -41,6 +43,7 @@ def tile_productkeysoftmemoryplus_t_kernel(
         work = ctx.enter_context(tc.tile_pool(name="work", bufs=2))
         psum = ctx.enter_context(tc.psum_pool(name="psum", bufs=1))
         ctx.enter_context(tc.manual_schedule())
+        state = {}
 
         xraw = []
         for a, b in X_CHUNKS:
@@ -56,51 +59,63 @@ def tile_productkeysoftmemoryplus_t_kernel(
             a, b = X_CHUNKS[i]
             nc.sync.dma_start(out=xraw[i][:], in_=x_view[:, a:b, :])
 
-        nc.sync.dma_start(out=scale_sb[:], in_=x_scale.rearrange("o k -> (o k)").partition_broadcast(P))
+        nc.sync.dma_start(
+            out=scale_sb[:], in_=x_scale.rearrange("o k -> (o k)").partition_broadcast(P)
+        )
         load_x(0)
         nc.sync.dma_start(out=wg_raw[:], in_=wg.rearrange("(p j) c -> p j c", j=4))
         load_x(1)
         nc.sync.dma_start(out=wk_raw[:], in_=wk.rearrange("(p j) c -> p j c", j=4))
         load_x(2)
+        load_x(3)
+        load_x(4)
         for g in range(2):
             nc.sync.dma_start(
                 out=v_raw[:, g, :, :],
                 in_=values[512 * g : 512 * (g + 1), :].rearrange("(p j) c -> p j c", j=4),
             )
         nc.sync.dma_start(out=gain_sb[:], in_=slot_gain.rearrange("(g p t) -> p g t", p=P, t=4))
-        load_x(3)
-        load_x(4)
 
         ident = keep.tile([P, P], F32, name="ident")
         make_identity(nc, ident[:])
-        warm = keep.tile([P, 1], F32, name="warm")
-        nc.gpsimd.memset(warm[:], 0.0)
-        warm_out = keep.tile([P, 1], F32, name="warm_out")
-        nc.scalar.activation(out=warm_out[:], in_=warm[:], func=ACT.Silu)
 
         x_codes = keep.tile([P, T], U32, name="x_codes", align_bytes=64)
-        x_planes = keep.tile([P, T], U8, name="x_planes", align_bytes=64)
+        x_scales = keep.tile([P, T], U8, name="x_scales", align_bytes=64)
         wg_codes = keep.tile([P, D], U32, name="wg_codes", align_bytes=64)
-        wg_planes = keep.tile([P, D], U8, name="wg_planes", align_bytes=64)
+        wg_scales = keep.tile([P, D], U8, name="wg_scales", align_bytes=64)
         wk_codes = keep.tile([P, C], U32, name="wk_codes", align_bytes=64)
-        wk_planes = keep.tile([P, C], U8, name="wk_planes", align_bytes=64)
+        wk_scales = keep.tile([P, C], U8, name="wk_scales", align_bytes=64)
         v_codes = keep.tile([P, 2, D], U32, name="v_codes", align_bytes=64)
-        v_planes = keep.tile([P, 2, D], U8, name="v_planes", align_bytes=64)
-        gate = keep.tile([P, NT, D], F32, name="gate")
+        v_scales = keep.tile([P, 2, D], U8, name="v_scales", align_bytes=64)
+        gates = [keep.tile([P, D], F32, name="gate%d" % n) for n in range(NT)]
+
+        def quantise(codes, scales, interleaved):
+            nc.vector.quantize_mx(
+                out=codes.bitcast(FP8X4),
+                scales=scales,
+                in_=interleaved.rearrange("p c j -> p (c j)"),
+            )
 
         wg_il = keep.tile([P, D, 4], BF16, name="wg_il", align_bytes=64)
+        wk_il = keep.tile([P, C, 4], BF16, name="wk_il", align_bytes=64)
+
+        def wg_copy():
+            nc.vector.tensor_copy(out=wg_il[:], in_=wg_raw[:].rearrange("p j c -> p c j"))
+
+        def wg_quant():
+            quantise(wg_codes[:], wg_scales[:], wg_il[:])
 
         def wk_copy():
-            wk_il = keep.tile([P, C, 4], BF16, name="wk_il", align_bytes=64)
-            nc.vector.tensor_copy(out=wk_il[:], in_=wk_raw[:].rearrange("p j c -> p c j"))
-            state["wk_il"] = wk_il
+            src = wk_raw[:].rearrange("p j (h a k) -> p a h k j", a=2, k=N)
+            dst = wk_il[:].rearrange("p (a h k) j -> p a h k j", a=2, k=N)
+            nc.vector.tensor_copy(out=dst[:, 0], in_=src[:, 0])
+            nc.vector.tensor_copy(
+                out=dst[:, 1].rearrange("p h (t m) j -> p h t m j", t=4),
+                in_=src[:, 1].rearrange("p h (m t) j -> p h t m j", t=4),
+            )
 
         def wk_quant():
-            nc.vector.quantize_mx(
-                out=wk_codes[:].bitcast(FP8X4),
-                scales=wk_planes[:],
-                in_=state["wk_il"][:].rearrange("p c j -> p (c j)"),
-            )
+            quantise(wk_codes[:], wk_scales[:], wk_il[:])
 
         def v_copy(i):
             g, b = divmod(i, 2)
@@ -114,17 +129,7 @@ def tile_productkeysoftmemoryplus_t_kernel(
         def v_quant(i):
             g, b = divmod(i, 2)
             cols = slice(256 * b, 256 * (b + 1))
-            nc.vector.quantize_mx(
-                out=v_codes[:, g, cols].bitcast(FP8X4),
-                scales=v_planes[:, g, cols],
-                in_=state["v_il", i][:].rearrange("p c j -> p (c j)"),
-            )
-
-        state = {}
-        prep = {5: [wk_copy], 6: [wk_quant]}
-        for i in range(4):
-            prep.setdefault(7 + 2 * i, []).append(lambda i=i: v_copy(i))
-            prep.setdefault(8 + 2 * i, []).append(lambda i=i: v_quant(i))
+            quantise(v_codes[:, g, cols], v_scales[:, g, cols], state["v_il", i][:])
 
         def x_product(q):
             xb = work.tile([P, 2, D], BF16, name="xb", bufs=3, align_bytes=64)
@@ -141,7 +146,7 @@ def tile_productkeysoftmemoryplus_t_kernel(
 
         def x_transpose(q):
             words = state["xb", q][:].rearrange("p s d -> p (s d)").bitcast(F32)
-            xt = psum.tile([P, 2, 2, P], F32, name="xt", tag="sc", bufs=2)
+            xt = psum.tile([P, 2, 2, P], F32, name="xt", tag="p2", bufs=2)
             for s in range(2):
                 for u in range(2):
                     nc.tensor.transpose(
@@ -161,62 +166,33 @@ def tile_productkeysoftmemoryplus_t_kernel(
 
         def x_quant(q):
             cols = slice(256 * q, 256 * (q + 1))
-            nc.vector.quantize_mx(
-                out=x_codes[:, cols].bitcast(FP8X4),
-                scales=x_planes[:, cols],
-                in_=state["xg", q][:].rearrange("p k t -> p (k t)"),
-            )
+            quantise(x_codes[:, cols], x_scales[:, cols], state["xg", q][:])
 
-        def mx_x(dst, n, codes, planes):
+        def mx_x(dst, n, codes, scales):
             cols = slice(P * n, P * (n + 1))
             nc.tensor.matmul_mx(
                 out=dst,
                 lhsT=x_codes[:, cols].bitcast(FP8X4),
-                lhsT_scale=x_planes[:, cols],
+                lhsT_scale=x_scales[:, cols],
                 rhs=codes[:].bitcast(FP8X4),
-                rhs_scale=planes[:],
+                rhs_scale=scales[:],
                 start=True,
                 stop=True,
             )
 
         def gate_matmul(q):
-            for s in range(2):
+            for n in (2 * q, 2 * q + 1):
                 a_ps = psum.tile([P, D], F32, name="a_ps", tag="ub", bufs=3)
-                mx_x(a_ps[:], 2 * q + s, wg_codes, wg_planes)
-                state["a", 2 * q + s] = a_ps
+                mx_x(a_ps[:], n, wg_codes, wg_scales)
+                state["a", n] = a_ps
 
         def gate_silu(q):
             for n in (2 * q, 2 * q + 1):
-                nc.scalar.activation(out=gate[:, n, :], in_=state["a", n][:], func=ACT.Silu)
-
-        NQ = NT // 2
-        for q in range(NQ + 5):
-            if 0 <= q - 4 < NQ:
-                gate_matmul(q - 4)
-            if 0 <= q - 1 < NQ:
-                x_transpose(q - 1)
-            if 0 <= q - 5 < NQ:
-                gate_silu(q - 5)
-            if 0 <= q - 2 < NQ:
-                x_copy(q - 2)
-            if q < NQ:
-                x_product(q)
-            if q == 1:
-                nc.vector.tensor_copy(out=wg_il[:], in_=wg_raw[:].rearrange("p j c -> p c j"))
-            if q == 2:
-                nc.vector.quantize_mx(
-                    out=wg_codes[:].bitcast(FP8X4),
-                    scales=wg_planes[:],
-                    in_=wg_il[:].rearrange("p c j -> p (c j)"),
-                )
-            for f in prep.get(q, []):
-                f()
-            if 0 <= q - 3 < NQ:
-                x_quant(q - 3)
+                nc.scalar.activation(out=gates[n][:], in_=state["a", n][:], func=ACT.Silu)
 
         def scores(n):
             sc = psum.tile([P, C], F32, name="sc_ps", tag="sc", bufs=2)
-            mx_x(sc[:], n, wk_codes, wk_planes)
+            mx_x(sc[:], n, wk_codes, wk_scales)
             state["sc", n] = sc
 
         def maxima(n):
@@ -231,87 +207,119 @@ def tile_productkeysoftmemoryplus_t_kernel(
             state["nm", n] = nm
 
         def exps(n):
-            e = work.tile([P, 2, H, N], F32, name="e", bufs=4)
-            z = work.tile([P, 2 * H], F32, name="z", bufs=3)
+            q, s = divmod(n, 2)
+            if s == 0:
+                e = work.tile([P, 2, 2, H, N], F32, name="e", bufs=4)
+                z = work.tile([P, 2, H, 2], F32, name="z", bufs=2)
+                state["e", q], state["z", q] = e, z
+            e, z = state["e", q], state["z", q]
             sc, nm = state["sc", n], state["nm", n]
             for half in range(2):
                 for h in range(H):
-                    c = 2 * h + half
-                    src = sc[:, N * c : N * (c + 1)]
-                    dst = e[:, half, h, :]
-                    if half == 1:
-                        src = src.rearrange("p (m t) -> p t m", t=4)
-                        dst = dst.rearrange("p (t m) -> p t m", t=4)
+                    c = H * half + h
                     nc.scalar.activation(
-                        out=dst,
-                        in_=src,
+                        out=e[:, s, half, h, :],
+                        in_=sc[:, N * c : N * (c + 1)],
                         func=ACT.Exp,
                         bias=nm[:, c : c + 1],
-                        accum_out=z[:, H * half + h : H * half + h + 1],
+                        accum_out=z[:, s, h, half : half + 1],
                     )
-            state["e", n], state["z", n] = e, z
 
-        def recips(n):
-            rz = work.tile([P, 2 * H], F32, name="rz", bufs=3)
-            nc.vector.reciprocal(out=rz[:], in_=state["z", n][:])
-            state["rz", n] = rz
-
-        def normalise(n):
-            if n % 2 == 0:
-                pn = work.tile([P, 2, 2 * H, N], F32, name="pn", bufs=3)
-                state["pn2", n // 2] = pn
-            pn = state["pn2", n // 2]
-            nc.gpsimd.tensor_tensor(
-                out=pn[:, n % 2, :, :],
-                in0=state["e", n][:].rearrange("p a h k -> p (a h) k"),
-                in1=state["rz", n][:].unsqueeze(2).broadcast_to([P, 2 * H, N]),
+        def denominators(q):
+            zz = work.tile([P, 2 * H], F32, name="zz", bufs=2)
+            nc.vector.tensor_reduce(
+                out=zz[:],
+                in_=state["z", q][:].rearrange("p s h a -> p (s h) a"),
+                axis=AX.X,
                 op=ALU.mult,
             )
-            state["pn", n] = pn[:, n % 2, :, :].rearrange("p (a h) k -> p a h k", a=2)
+            state["zz", q] = zz
 
-        def p2_to_psum(q):
-            p2 = psum.tile([P, 2, 2, N], F32, name="p2_ps", tag="p2", bufs=2)
+        def reciprocals(q):
+            rz = work.tile([P, 2 * H], F32, name="rz", bufs=2)
+            nc.vector.reciprocal(out=rz[:], in_=state["zz", q][:])
+            state["rz", q] = rz
+
+        def normalise(n):
+            q, s = divmod(n, 2)
+            p1 = work.tile([P, H, N], F32, name="p1", bufs=3)
+            for h in range(H):
+                nc.scalar.activation(
+                    out=p1[:, h, :],
+                    in_=state["e", q][:, s, 0, h, :],
+                    func=ACT.Copy,
+                    scale=state["rz", q][:, H * s + h : H * s + h + 1],
+                )
+            state["p1", n] = p1
+
+        def e2_to_psum(q):
+            e2 = psum.tile([P, 2, V_KEYS], F32, name="e2_ps", tag="p2", bufs=2)
             nc.tensor.matmul(
-                p2[:].rearrange("p s h k -> p s (h k)"),
+                e2[:],
                 lhsT=ident[:],
-                rhs=state["pn2", q][:, :, H : H + 2, :].rearrange("p s h k -> p s (h k)"),
+                rhs=state["e", q][:, :, 1, :, :].rearrange("p s h k -> p s (h k)")[:, :, 0:V_KEYS],
                 start=True,
                 stop=True,
             )
-            state["p2", 2 * q], state["p2", 2 * q + 1] = p2[:, 0, :, :], p2[:, 1, :, :]
+            state["e2_ps", q] = e2
 
-        def wide_product(eng, n, h, lo, hi, p2, pr):
-            ni = hi - lo
-            p1 = state["pn", n][:, 0, h, lo:hi]
+        def e2_of(n, h):
+            return state["e", n // 2][:, n % 2, 1, h, :]
+
+        def product(eng, dst, p1, e2):
+            nt, ni = dst.shape[1], p1.shape[1]
             eng.tensor_tensor(
-                out=pr[:].rearrange("p t (i m) -> p t i m", m=8),
-                in0=p1.unsqueeze(1).unsqueeze(3).broadcast_to([P, 4, ni, 8]),
-                in1=p2.rearrange("p (t m) -> p t m", t=4).unsqueeze(2).broadcast_to([P, 4, ni, 8]),
+                out=dst.rearrange("p t (i m) -> p t i m", m=8),
+                in0=p1.unsqueeze(1).unsqueeze(3).broadcast_to([P, nt, ni, 8]),
+                in1=e2.rearrange("p (t m) -> p t m", m=8).unsqueeze(2).broadcast_to([P, nt, ni, 8]),
                 op=ALU.mult,
             )
 
-        def whole_product(eng, n, h, p2):
-            pr = work.tile([P, 4, 2 * P], F32, name="pr%d" % h, bufs=2)
-            wide_product(eng, n, h, 0, N, p2, pr)
-            state["pr", n, h, 0] = pr[:, :, 0:P]
-            state["pr", n, h, 1] = pr[:, :, P : 2 * P]
+        def head_product(eng, n, h, e2):
+            pr = work.tile([P, 4, 2 * P], F32, name="pr%d" % h, bufs=3)
+            product(eng, pr[:], state["p1", n][:, h, :], e2)
+            for g in range(2):
+                for t in range(4):
+                    state["pr", n, h, g, t] = pr[:, t, P * g : P * (g + 1)]
 
-        def half_product(eng, n, h, g, p2):
-            pr = work.tile([P, 4, P], F32, name="pr%d_%d" % (h, 16 * g), bufs=2)
-            wide_product(eng, n, h, 16 * g, 16 * (g + 1), p2, pr)
-            state["pr", n, h, g] = pr[:]
+        def cut_product(eng, n, dst, t0, e2):
+            h, g = CUT_HALF
+            product(eng, dst, state["p1", n][:, h, 16 * g : 16 * (g + 1)], e2)
+            for t in range(dst.shape[1]):
+                state["pr", n, h, g, t0 + t] = dst[:, t, :]
+
+        def vector_products(n):
+            e2 = state["e2_ps", n // 2][:, n % 2, :]
+            head_product(nc.vector, n, V_HEAD, e2[:, 0:N])
+            pr = work.tile([P, V_PLANES, P], F32, name="pr_cut_v", bufs=3)
+            cut_product(nc.vector, n, pr[:], 0, e2[:, N:V_KEYS])
+
+        def gpsimd_cut(n):
+            planes = 4 - V_PLANES
+            if n >= 3:
+                room = gates[n - 3][:, 0 : planes * P]
+            else:
+                first = keep.tile([P, planes * P], F32, name="pr_cut_g%d" % n)
+                room = first[:]
+            cut_product(
+                nc.gpsimd,
+                n,
+                room.rearrange("p (t c) -> p t c", c=P),
+                V_PLANES,
+                e2_of(n, CUT_HALF[0])[:, 8 * V_PLANES : N],
+            )
 
         def scalar_product(n, h, g):
-            pr = work.tile([P, 4, P], F32, name="pr%d_%d" % (h, 16 * g), bufs=2)
+            pr = work.tile([P, 4, P], F32, name="pr%d_%d" % (h, g), bufs=3)
             for i in range(16):
-                ii = 16 * g + i
                 nc.scalar.activation(
                     out=pr[:, :, 8 * i : 8 * (i + 1)],
-                    in_=state["pn", n][:, 1, h, :].rearrange("p (t m) -> p t m", t=4),
+                    in_=e2_of(n, h).rearrange("p (t m) -> p t m", t=4),
                     func=ACT.Copy,
-                    scale=state["pn", n][:, 0, h, ii : ii + 1],
+                    scale=state["p1", n][:, h, 16 * g + i : 16 * g + i + 1],
                 )
-            state["pr", n, h, g] = pr[:]
+            for t in range(4):
+                state["pr", n, h, g, t] = pr[:, t, :]
 
         def sum_heads(n, g):
             ub = psum.tile([P, 4, P], F32, name="ub_ps", tag="ub", bufs=3)
@@ -319,7 +327,7 @@ def tile_productkeysoftmemoryplus_t_kernel(
                 for h in range(H):
                     nc.tensor.matmul(
                         ub[:, t, :],
-                        lhsT=state["pr", n, h, g][:, t, :],
+                        lhsT=state["pr", n, h, g, t],
                         rhs=ident[:],
                         start=(h == 0),
                         stop=(h == H - 1),
@@ -341,11 +349,7 @@ def tile_productkeysoftmemoryplus_t_kernel(
         def u_quant(n):
             uc = work.tile([P, 2 * P], U32, name="uc", align_bytes=64)
             us = work.tile([P, 2 * P], U8, name="us", align_bytes=64)
-            nc.vector.quantize_mx(
-                out=uc[:].bitcast(FP8X4),
-                scales=us[:],
-                in_=state["u", n][:].rearrange("p g k t -> p (g k t)"),
-            )
+            quantise(uc[:], us[:], state["u", n][:].rearrange("p g k t -> p (g k) t"))
             state["uc", n] = (uc, us)
 
         def memory(n):
@@ -358,7 +362,7 @@ def tile_productkeysoftmemoryplus_t_kernel(
                     lhsT=uc[:, cols].bitcast(FP8X4),
                     lhsT_scale=us[:, cols],
                     rhs=v_codes[:, g, :].bitcast(FP8X4),
-                    rhs_scale=v_planes[:, g, :],
+                    rhs_scale=v_scales[:, g, :],
                     start=(g == 0),
                     stop=(g == 1),
                 )
@@ -367,51 +371,78 @@ def tile_productkeysoftmemoryplus_t_kernel(
         def final(n):
             o = work.tile([P, D], F32, name="o", bufs=4)
             nc.vector.tensor_tensor(
-                out=o[:], in0=state["mem", n][:], in1=gate[:, n, :], op=ALU.mult
+                out=o[:], in0=state["mem", n][:], in1=gates[n][:], op=ALU.mult
             )
             nc.sync.dma_start(out=out_view[:, n, :], in_=o[:])
 
         def has(n):
             return 0 <= n < NT
 
-        def shared_on_scalar(n):
-            return n % 2 == 1
+        def has_pair(q):
+            return 0 <= q < NPAIR
 
-        for s in range(-5, NT + 3):
+        weight_steps = {1: wg_copy, 2: wg_quant, 5: wk_copy, 6: wk_quant}
+        for q in range(NPAIR + 5):
+            if has_pair(q - 4):
+                gate_matmul(q - 4)
+            if has_pair(q - 1):
+                x_transpose(q - 1)
+            if has_pair(q - 5):
+                gate_silu(q - 5)
+            if has_pair(q - 2):
+                x_copy(q - 2)
+            if has_pair(q):
+                x_product(q)
+            if q in weight_steps:
+                weight_steps[q]()
+            if has_pair(q - 3):
+                x_quant(q - 3)
+            if NPAIR <= q < NPAIR + 2:
+                scores(q - NPAIR)
+                maxima(q - NPAIR)
+
+        for s in range(-5, NT + 2):
+            odd = s % 2 == 1
             if has(s - 2):
                 memory(s - 2)
-            if has(s + 5):
-                scores(s + 5)
-            if has(s + 3):
-                normalise(s + 3)
-            if has(s + 1):
-                whole_product(nc.gpsimd, s + 1, G_WHOLE, state["pn", s + 1][:, 1, G_WHOLE, :])
+            if has(s + 6) and s + 6 >= 2:
+                scores(s + 6)
+            if odd and has(s + 3):
+                e2_to_psum((s + 3) // 2)
             if has(s):
                 sum_heads(s, 0)
-            if s % 2 == 0 and has(s + 2):
-                p2_to_psum(s // 2 + 1)
-            if has(s):
                 sum_heads(s, 1)
-            for k in range(3):
-                if has(s + 1):
-                    scalar_product(s + 1, *S_HALVES[k])
-                if k == 0 and has(s + 4):
-                    exps(s + 4)
-            if has(s + 1) and shared_on_scalar(s + 1):
-                scalar_product(s + 1, *SHARED)
-            if has(s - 1):
-                gain(s - 1, 0)
             if has(s + 1):
-                whole_product(nc.vector, s + 1, V_WHOLE, state["p2", s + 1][:, 0, :])
+                head_product(nc.gpsimd, s + 1, G_HEAD, e2_of(s + 1, G_HEAD))
+            if has(s + 1):
+                scalar_product(s + 1, *S_HALVES[0])
+            if has(s + 2):
+                normalise(s + 2)
+            if has(s + 1):
+                scalar_product(s + 1, *S_HALVES[1])
+            if has(s + 5):
+                exps(s + 5)
+            if has(s + 1):
+                scalar_product(s + 1, *S_HALVES[2])
+            if -5 <= s < -1:
+                v_copy(s + 5)
             if has(s - 1):
                 gain(s - 1, 1)
+            if has(s + 1):
+                vector_products(s + 1)
             if has(s - 2):
                 final(s - 2)
-            if has(s + 1) and not shared_on_scalar(s + 1):
-                half_product(nc.vector, s + 1, *SHARED, state["p2", s + 1][:, 1, :])
+            if has(s + 1):
+                gpsimd_cut(s + 1)
             if has(s - 1):
                 u_quant(s - 1)
-            if has(s + 4):
-                recips(s + 4)
-            if has(s + 5):
-                maxima(s + 5)
+            if odd and has(s + 3):
+                denominators((s + 3) // 2)
+            if has(s):
+                gain(s, 0)
+            if has(s + 6) and s + 6 >= 2:
+                maxima(s + 6)
+            if -5 <= s < -1:
+                v_quant(s + 5)
+            if odd and has(s + 3):
+                reciprocals((s + 3) // 2)

@@ -26,9 +26,16 @@ V_HEAD, G_HEAD = 0, 3
 S_HALVES = [(1, 0), (2, 0), (2, 1)]
 CUT_HALF = (1, 1)
 V_PLANES = 2
-V_KEYS = N + 8 * V_PLANES
+NO_MAXIMA = NT - 6
 
 X_CHUNKS = [(0, 2), (2, 8), (8, 16), (16, 24), (24, 32)]
+EARLY = 10
+V_FIRST = 3
+LATE_GATES = 10
+W_ROUND = 3
+V_ROUND = 7
+V_COPIES = ()
+E_BUFS = 6
 
 
 def tile_productkeysoftmemoryplus_t_kernel(
@@ -49,7 +56,7 @@ def tile_productkeysoftmemoryplus_t_kernel(
         for a, b in X_CHUNKS:
             xr = keep.tile([P, b - a, D], U8, name="xraw%d" % a, align_bytes=64)
             xraw.append(xr)
-        scale_sb = keep.tile([P, D], F32, name="scale_sb")
+        scale_col = keep.tile([P, 4], F32, name="scale_col")
         wg_raw = keep.tile([P, 4, D], BF16, name="wg_raw")
         wk_raw = keep.tile([P, 4, C], BF16, name="wk_raw")
         v_raw = keep.tile([P, 2, 4, D], BF16, name="v_raw")
@@ -59,13 +66,11 @@ def tile_productkeysoftmemoryplus_t_kernel(
             a, b = X_CHUNKS[i]
             nc.sync.dma_start(out=xraw[i][:], in_=x_view[:, a:b, :])
 
-        nc.sync.dma_start(
-            out=scale_sb[:], in_=x_scale.rearrange("o k -> (o k)").partition_broadcast(P)
-        )
+        nc.sync.dma_start(out=scale_col[:], in_=x_scale.rearrange("o (p t) -> p (o t)", t=4))
         load_x(0)
-        nc.sync.dma_start(out=wg_raw[:], in_=wg.rearrange("(p j) c -> p j c", j=4))
-        load_x(1)
         nc.sync.dma_start(out=wk_raw[:], in_=wk.rearrange("(p j) c -> p j c", j=4))
+        load_x(1)
+        nc.sync.dma_start(out=wg_raw[:], in_=wg.rearrange("(p j) c -> p j c", j=4))
         load_x(2)
         load_x(3)
         load_x(4)
@@ -78,6 +83,17 @@ def tile_productkeysoftmemoryplus_t_kernel(
 
         ident = keep.tile([P, P], F32, name="ident")
         make_identity(nc, ident[:])
+
+        scale_ps = psum.tile([P, 4, P], F32, name="scale_ps", tag="mem", bufs=1)
+        for t in range(4):
+            nc.tensor.transpose(
+                scale_ps[:, t, :], scale_col[:, t : t + 1].to_broadcast([P, P]), ident[:]
+            )
+        scale_sb = keep.tile([P, D], F32, name="scale_sb")
+        nc.scalar.copy(
+            out=scale_sb[:].rearrange("p (k t) -> p k t", t=4),
+            in_=scale_ps[:].rearrange("p t k -> p k t"),
+        )
 
         x_codes = keep.tile([P, T], U32, name="x_codes", align_bytes=64)
         x_scales = keep.tile([P, T], U8, name="x_scales", align_bytes=64)
@@ -156,12 +172,13 @@ def tile_productkeysoftmemoryplus_t_kernel(
 
         def x_copy(q):
             xg = work.tile([P, 2 * P, 4], BF16, name="xg", bufs=4, align_bytes=64)
-            nc.scalar.copy(
-                out=xg[:].rearrange("p k t -> p (k t)").bitcast(F32).rearrange(
-                    "p (s k u) -> p s k u", s=2, u=2
-                ),
-                in_=state["xt", q][:].rearrange("p s u k -> p s k u"),
-            )
+            words = xg[:].rearrange("p k t -> p (k t)").bitcast(F32)
+            dst = words.rearrange("p (s k u) -> p s k u", s=2, u=2)
+            src = state["xt", q][:].rearrange("p s u k -> p s k u")
+            if q in V_COPIES:
+                nc.vector.tensor_copy(out=dst, in_=src)
+            else:
+                nc.scalar.copy(out=dst, in_=src)
             state["xg", q] = xg
 
         def x_quant(q):
@@ -180,37 +197,38 @@ def tile_productkeysoftmemoryplus_t_kernel(
                 stop=True,
             )
 
-        def gate_matmul(q):
-            for n in (2 * q, 2 * q + 1):
-                a_ps = psum.tile([P, D], F32, name="a_ps", tag="ub", bufs=3)
-                mx_x(a_ps[:], n, wg_codes, wg_scales)
-                state["a", n] = a_ps
+        def gate_matmul(n):
+            a_ps = psum.tile([P, D], F32, name="a_ps", tag="sc", bufs=2)
+            mx_x(a_ps[:], n, wg_codes, wg_scales)
+            state["a", n] = a_ps
 
-        def gate_silu(q):
-            for n in (2 * q, 2 * q + 1):
-                nc.scalar.activation(out=gates[n][:], in_=state["a", n][:], func=ACT.Silu)
+        def gate_silu(n):
+            nc.scalar.activation(out=gates[n][:], in_=state["a", n][:], func=ACT.Silu)
 
-        def scores(n):
-            sc = psum.tile([P, C], F32, name="sc_ps", tag="sc", bufs=2)
-            mx_x(sc[:], n, wk_codes, wk_scales)
-            state["sc", n] = sc
+        def scores(tiles):
+            sc = psum.tile([P, len(tiles), C], F32, name="sc_ps", tag="sc", bufs=2)
+            for k, n in enumerate(tiles):
+                mx_x(sc[:, k, :], n, wk_codes, wk_scales)
+                state["sc", n] = sc[:, k, :]
+            state["sc_bank", tiles[0]] = sc
 
-        def maxima(n):
-            nm = work.tile([P, 2 * H], F32, name="nm", bufs=3)
+        def maxima(tiles):
+            nm = work.tile([P, len(tiles), 2 * H], F32, name="nm", bufs=3)
             nc.vector.tensor_reduce(
-                out=nm[:],
-                in_=state["sc", n][:].rearrange("p (c k) -> p c k", k=N),
+                out=nm[:].rearrange("p s c -> p (s c)"),
+                in_=state["sc_bank", tiles[0]][:].rearrange("p s (c k) -> p (s c) k", k=N),
                 axis=AX.X,
                 op=ALU.max,
                 negate=True,
             )
-            state["nm", n] = nm
+            for k, n in enumerate(tiles):
+                state["nm", n] = nm[:, k, :]
 
         def exps(n):
             q, s = divmod(n, 2)
             if s == 0:
-                e = work.tile([P, 2, 2, H, N], F32, name="e", bufs=4)
-                z = work.tile([P, 2, H, 2], F32, name="z", bufs=2)
+                e = work.tile([P, 2, 2, H, N], F32, name="e", bufs=E_BUFS)
+                z = work.tile([P, 2, H, 2], F32, name="z", bufs=E_BUFS)
                 state["e", q], state["z", q] = e, z
             e, z = state["e", q], state["z", q]
             sc, nm = state["sc", n], state["nm", n]
@@ -226,7 +244,7 @@ def tile_productkeysoftmemoryplus_t_kernel(
                     )
 
         def denominators(q):
-            zz = work.tile([P, 2 * H], F32, name="zz", bufs=2)
+            zz = work.tile([P, 2 * H], F32, name="zz", bufs=3)
             nc.vector.tensor_reduce(
                 out=zz[:],
                 in_=state["z", q][:].rearrange("p s h a -> p (s h) a"),
@@ -236,7 +254,7 @@ def tile_productkeysoftmemoryplus_t_kernel(
             state["zz", q] = zz
 
         def reciprocals(q):
-            rz = work.tile([P, 2 * H], F32, name="rz", bufs=2)
+            rz = work.tile([P, 2 * H], F32, name="rz", bufs=3)
             nc.vector.reciprocal(out=rz[:], in_=state["zz", q][:])
             state["rz", q] = rz
 
@@ -252,16 +270,21 @@ def tile_productkeysoftmemoryplus_t_kernel(
                 )
             state["p1", n] = p1
 
-        def e2_to_psum(q):
-            e2 = psum.tile([P, 2, V_KEYS], F32, name="e2_ps", tag="p2", bufs=2)
-            nc.tensor.matmul(
-                e2[:],
-                lhsT=ident[:],
-                rhs=state["e", q][:, :, 1, :, :].rearrange("p s h k -> p s (h k)")[:, :, 0:V_KEYS],
-                start=True,
-                stop=True,
-            )
-            state["e2_ps", q] = e2
+        def e2_to_psum(tiles, keys, tag, bufs):
+            e2 = psum.tile([P, len(tiles), keys], F32, name="e2_ps", tag=tag, bufs=bufs)
+            for q in sorted(set(n // 2 for n in tiles)):
+                mine = [n for n in tiles if n // 2 == q]
+                rows = slice(mine[0] % 2, mine[-1] % 2 + 1)
+                k = tiles.index(mine[0])
+                nc.tensor.matmul(
+                    e2[:, k : k + len(mine), :],
+                    lhsT=ident[:],
+                    rhs=state["e", q][:, rows, 1, :, :].rearrange("p s h k -> p s (h k)")[:, :, 0:keys],
+                    start=True,
+                    stop=True,
+                )
+            for k, n in enumerate(tiles):
+                state["e2_ps", n] = e2[:, k, :]
 
         def e2_of(n, h):
             return state["e", n // 2][:, n % 2, 1, h, :]
@@ -288,29 +311,48 @@ def tile_productkeysoftmemoryplus_t_kernel(
             for t in range(dst.shape[1]):
                 state["pr", n, h, g, t0 + t] = dst[:, t, :]
 
+        def v_planes(n):
+            return V_PLANES + (n >= NO_MAXIMA)
+
         def vector_products(n):
-            e2 = state["e2_ps", n // 2][:, n % 2, :]
+            e2 = state["e2_ps", n]
             head_product(nc.vector, n, V_HEAD, e2[:, 0:N])
-            pr = work.tile([P, V_PLANES, P], F32, name="pr_cut_v", bufs=3)
-            cut_product(nc.vector, n, pr[:], 0, e2[:, N:V_KEYS])
+            if n == 0:
+                for h, g in S_HALVES[3 - V_FIRST :]:
+                    pr = half_tile(n, h, g)
+                    p1 = state["p1", n][:, h, 16 * g : 16 * (g + 1)]
+                    product(nc.vector, pr[:], p1, e2[:, N * h : N * (h + 1)])
+            planes = v_planes(n)
+            pr = work.tile([P, planes, P], F32, name="pr_cut_v", bufs=3)
+            first = N * CUT_HALF[0]
+            cut_product(nc.vector, n, pr[:], 0, e2[:, first : first + 8 * planes])
 
         def gpsimd_cut(n):
-            planes = 4 - V_PLANES
+            planes = 4 - v_planes(n)
             if n >= 3:
                 room = gates[n - 3][:, 0 : planes * P]
             else:
-                first = keep.tile([P, planes * P], F32, name="pr_cut_g%d" % n)
-                room = first[:]
+                spare = keep.tile([P, planes * P], F32, name="pr_cut_g%d" % n)
+                room = spare[:]
             cut_product(
                 nc.gpsimd,
                 n,
                 room.rearrange("p (t c) -> p t c", c=P),
-                V_PLANES,
-                e2_of(n, CUT_HALF[0])[:, 8 * V_PLANES : N],
+                4 - planes,
+                e2_of(n, CUT_HALF[0])[:, N - 8 * planes : N],
             )
 
-        def scalar_product(n, h, g):
+        def half_tile(n, h, g):
             pr = work.tile([P, 4, P], F32, name="pr%d_%d" % (h, g), bufs=3)
+            for t in range(4):
+                state["pr", n, h, g, t] = pr[:, t, :]
+            return pr
+
+        def scalar_product(n, k):
+            if n == 0 and k >= 3 - V_FIRST:
+                return
+            h, g = S_HALVES[k]
+            pr = half_tile(n, h, g)
             for i in range(16):
                 nc.scalar.activation(
                     out=pr[:, :, 8 * i : 8 * (i + 1)],
@@ -318,8 +360,6 @@ def tile_productkeysoftmemoryplus_t_kernel(
                     func=ACT.Copy,
                     scale=state["p1", n][:, h, 16 * g + i : 16 * g + i + 1],
                 )
-            for t in range(4):
-                state["pr", n, h, g, t] = pr[:, t, :]
 
         def sum_heads(n, g):
             ub = psum.tile([P, 4, P], F32, name="ub_ps", tag="ub", bufs=3)
@@ -381,68 +421,107 @@ def tile_productkeysoftmemoryplus_t_kernel(
         def has_pair(q):
             return 0 <= q < NPAIR
 
-        weight_steps = {1: wg_copy, 2: wg_quant, 5: wk_copy, 6: wk_quant}
-        for q in range(NPAIR + 5):
-            if has_pair(q - 4):
-                gate_matmul(q - 4)
-            if has_pair(q - 1):
-                x_transpose(q - 1)
-            if has_pair(q - 5):
-                gate_silu(q - 5)
-            if has_pair(q - 2):
-                x_copy(q - 2)
-            if has_pair(q):
-                x_product(q)
-            if q in weight_steps:
-                weight_steps[q]()
-            if has_pair(q - 3):
-                x_quant(q - 3)
-            if NPAIR <= q < NPAIR + 2:
-                scores(q - NPAIR)
-                maxima(q - NPAIR)
-
-        for s in range(-5, NT + 2):
+        def step(s):
             odd = s % 2 == 1
+            shared = has(s + 1)
+            late = NPAIR - LATE_GATES // 2 + s + 1
+            late = late if s >= -1 and has_pair(late) else None
             if has(s - 2):
                 memory(s - 2)
-            if has(s + 6) and s + 6 >= 2:
-                scores(s + 6)
-            if odd and has(s + 3):
-                e2_to_psum((s + 3) // 2)
+            if has(s + 6) and s + 6 >= EARLY:
+                scores([s + 6])
+            if late is not None:
+                gate_matmul(2 * late)
+                gate_matmul(2 * late + 1)
+            if odd and has(s + 3) and s > -2:
+                e2_to_psum([s + 3, s + 4], N + 8 * v_planes(s + 4), "p2", 2)
             if has(s):
                 sum_heads(s, 0)
                 sum_heads(s, 1)
             if has(s + 1):
                 head_product(nc.gpsimd, s + 1, G_HEAD, e2_of(s + 1, G_HEAD))
-            if has(s + 1):
-                scalar_product(s + 1, *S_HALVES[0])
+            if shared:
+                scalar_product(s + 1, 0)
             if has(s + 2):
                 normalise(s + 2)
-            if has(s + 1):
-                scalar_product(s + 1, *S_HALVES[1])
-            if has(s + 5):
+            if shared:
+                scalar_product(s + 1, 1)
+            if has(s + 5) and s + 5 >= EARLY:
                 exps(s + 5)
-            if has(s + 1):
-                scalar_product(s + 1, *S_HALVES[2])
-            if -5 <= s < -1:
-                v_copy(s + 5)
+            if late is not None:
+                gate_silu(2 * late)
+                gate_silu(2 * late + 1)
+            if shared:
+                scalar_product(s + 1, 2)
             if has(s - 1):
                 gain(s - 1, 1)
             if has(s + 1):
                 vector_products(s + 1)
             if has(s - 2):
                 final(s - 2)
-            if has(s + 1):
+            if shared:
                 gpsimd_cut(s + 1)
             if has(s - 1):
                 u_quant(s - 1)
+            if s in (-1, 0):
+                x_quant(NPAIR - 1 + s)
             if odd and has(s + 3):
                 denominators((s + 3) // 2)
             if has(s):
                 gain(s, 0)
-            if has(s + 6) and s + 6 >= 2:
-                maxima(s + 6)
-            if -5 <= s < -1:
-                v_quant(s + 5)
+            if has(s + 6) and s + 6 >= EARLY:
+                maxima([s + 6])
             if odd and has(s + 3):
                 reciprocals((s + 3) // 2)
+
+        def pair(q):
+            return [2 * q, 2 * q + 1]
+
+        early_pairs = EARLY // 2
+        first = early_pairs + 2
+        gated = NPAIR - LATE_GATES // 2
+        extra = {0: wk_copy, 1: wk_quant, W_ROUND: wg_copy, W_ROUND + 1: wg_quant}
+        for i in range(4):
+            extra[V_ROUND + 2 * i] = lambda i=i: v_copy(i)
+            extra[V_ROUND + 2 * i + 1] = lambda i=i: v_quant(i)
+        for q in range(first):
+            x_product(q)
+            x_transpose(q)
+            if 0 <= q - 2 < early_pairs:
+                maxima(pair(q - 2))
+                exps(2 * q - 4)
+                exps(2 * q - 3)
+            if q in extra:
+                extra[q]()
+            if q > 0:
+                x_quant(q - 1)
+            x_copy(q)
+            if 0 <= q - 1 < early_pairs:
+                scores(pair(q - 1))
+        denominators(0)
+        e2_to_psum([0, 1], 3 * N, "mem", 1)
+        for q in range(first, max(NPAIR + 2, first + gated + 1)):
+            g = q - first - 1
+            if q == NPAIR:
+                normalise(0)
+            if q - 2 >= first and has_pair(q - 2):
+                x_copy(q - 2)
+            if 0 <= g < gated:
+                gate_silu(2 * g)
+                gate_silu(2 * g + 1)
+            if q - 1 >= first and has_pair(q - 1):
+                x_transpose(q - 1)
+            if g + 1 < gated:
+                gate_matmul(2 * g + 2)
+                gate_matmul(2 * g + 3)
+            if has_pair(q):
+                x_product(q)
+            if q == NPAIR - 1:
+                reciprocals(0)
+            if q in extra:
+                extra[q]()
+            if first - 1 <= q - 2 < NPAIR - 2:
+                x_quant(q - 2)
+
+        for s in range(-1, NT + 2):
+            step(s)

@@ -28,14 +28,11 @@ CUT_HALF = (1, 1)
 V_PLANES = 2
 NO_MAXIMA = NT - 6
 
-X_CHUNKS = [(0, 2), (2, 8), (8, 16), (16, 24), (24, 32)]
-EARLY = 10
-V_FIRST = 3
-LATE_GATES = 10
-W_ROUND = 3
-V_ROUND = 7
-V_COPIES = ()
-E_BUFS = 6
+X_CHUNKS = [(0, 4), (4, 8), (8, 16), (16, 24), (24, 32)]
+GATE_LEAD = 4
+GATES_BY_ROUND = (0, 0, 4, 6, 6, 6, 6)
+E_BUFS = 5
+EARLY = 8
 
 
 def tile_productkeysoftmemoryplus_t_kernel(
@@ -59,41 +56,33 @@ def tile_productkeysoftmemoryplus_t_kernel(
         scale_col = keep.tile([P, 4], F32, name="scale_col")
         wg_raw = keep.tile([P, 4, D], BF16, name="wg_raw")
         wk_raw = keep.tile([P, 4, C], BF16, name="wk_raw")
-        v_raw = keep.tile([P, 2, 4, D], BF16, name="v_raw")
+        v_raw = [keep.tile([P, 4, D], BF16, name="v_raw%d" % g) for g in range(2)]
         gain_sb = keep.tile([P, 2, 4], BF16, name="gain_sb")
 
         def load_x(i):
             a, b = X_CHUNKS[i]
             nc.sync.dma_start(out=xraw[i][:], in_=x_view[:, a:b, :])
 
-        nc.sync.dma_start(out=scale_col[:], in_=x_scale.rearrange("o (p t) -> p (o t)", t=4))
-        load_x(0)
-        nc.sync.dma_start(out=wk_raw[:], in_=wk.rearrange("(p j) c -> p j c", j=4))
-        load_x(1)
-        nc.sync.dma_start(out=wg_raw[:], in_=wg.rearrange("(p j) c -> p j c", j=4))
-        load_x(2)
-        load_x(3)
-        load_x(4)
-        for g in range(2):
+        def load_values(g):
             nc.sync.dma_start(
-                out=v_raw[:, g, :, :],
+                out=v_raw[g][:],
                 in_=values[512 * g : 512 * (g + 1), :].rearrange("(p j) c -> p j c", j=4),
             )
+
+        load_x(0)
+        nc.sync.dma_start(out=wk_raw[:], in_=wk.rearrange("(p j) c -> p j c", j=4))
+        nc.sync.dma_start(out=scale_col[:], in_=x_scale.rearrange("o (p t) -> p (o t)", t=4))
+        load_x(1)
+        nc.sync.dma_start(out=wg_raw[:], in_=wg.rearrange("(p j) c -> p j c", j=4))
+        load_values(0)
+        load_x(2)
+        load_values(1)
+        load_x(3)
+        load_x(4)
         nc.sync.dma_start(out=gain_sb[:], in_=slot_gain.rearrange("(g p t) -> p g t", p=P, t=4))
 
         ident = keep.tile([P, P], F32, name="ident")
         make_identity(nc, ident[:])
-
-        scale_ps = psum.tile([P, 4, P], F32, name="scale_ps", tag="mem", bufs=1)
-        for t in range(4):
-            nc.tensor.transpose(
-                scale_ps[:, t, :], scale_col[:, t : t + 1].to_broadcast([P, P]), ident[:]
-            )
-        scale_sb = keep.tile([P, D], F32, name="scale_sb")
-        nc.scalar.copy(
-            out=scale_sb[:].rearrange("p (k t) -> p k t", t=4),
-            in_=scale_ps[:].rearrange("p t k -> p k t"),
-        )
 
         x_codes = keep.tile([P, T], U32, name="x_codes", align_bytes=64)
         x_scales = keep.tile([P, T], U8, name="x_scales", align_bytes=64)
@@ -112,18 +101,29 @@ def tile_productkeysoftmemoryplus_t_kernel(
                 in_=interleaved.rearrange("p c j -> p (c j)"),
             )
 
-        wg_il = keep.tile([P, D, 4], BF16, name="wg_il", align_bytes=64)
-        wk_il = keep.tile([P, C, 4], BF16, name="wk_il", align_bytes=64)
+        rooms = [
+            keep.tile([P, 4 * D], BF16, name="x_room%d" % r, align_bytes=64) for r in range(4)
+        ]
 
-        def wg_copy():
-            nc.vector.tensor_copy(out=wg_il[:], in_=wg_raw[:].rearrange("p j c -> p c j"))
+        wg_il = keep.tile([P, D, 4], BF16, name="wg_il", align_bytes=64)
+        wk_il = rooms[1][:, 0 : 4 * C].rearrange("p (c j) -> p c j", j=4)
+
+        def interleave(copy, dst, src):
+            copy(
+                out=dst.rearrange("p (c i) j -> p c j i", i=4),
+                in_=src.rearrange("p j (c i) -> p c j i", i=4),
+            )
+
+        def wg_copy(b):
+            cols = slice(256 * b, 256 * (b + 1))
+            interleave(nc.scalar.copy, wg_il[:, cols, :], wg_raw[:, :, cols])
 
         def wg_quant():
             quantise(wg_codes[:], wg_scales[:], wg_il[:])
 
         def wk_copy():
             src = wk_raw[:].rearrange("p j (h a k) -> p a h k j", a=2, k=N)
-            dst = wk_il[:].rearrange("p (a h k) j -> p a h k j", a=2, k=N)
+            dst = wk_il.rearrange("p (a h k) j -> p a h k j", a=2, k=N)
             nc.vector.tensor_copy(out=dst[:, 0], in_=src[:, 0])
             nc.vector.tensor_copy(
                 out=dst[:, 1].rearrange("p h (t m) j -> p h t m j", t=4),
@@ -131,59 +131,64 @@ def tile_productkeysoftmemoryplus_t_kernel(
             )
 
         def wk_quant():
-            quantise(wk_codes[:], wk_scales[:], wk_il[:])
+            quantise(wk_codes[:], wk_scales[:], wk_il)
 
         def v_copy(i):
             g, b = divmod(i, 2)
-            v_il = work.tile([P, 256, 4], BF16, name="v_il", align_bytes=64)
-            nc.vector.tensor_copy(
-                out=v_il[:],
-                in_=v_raw[:, g, :, 256 * b : 256 * (b + 1)].rearrange("p j c -> p c j"),
-            )
-            state["v_il", i] = v_il
+            v_il = work.tile([P, 256, 4], BF16, name="v_il", bufs=4, align_bytes=64)
+            copy = nc.vector.tensor_copy if i == 3 else nc.scalar.copy
+            interleave(copy, v_il[:], v_raw[g][:, :, 256 * b : 256 * (b + 1)])
+            state["v_il", i] = v_il[:]
 
         def v_quant(i):
             g, b = divmod(i, 2)
             cols = slice(256 * b, 256 * (b + 1))
-            quantise(v_codes[:, g, cols], v_scales[:, g, cols], state["v_il", i][:])
+            quantise(v_codes[:, g, cols], v_scales[:, g, cols], state["v_il", i])
 
-        def x_product(q):
-            xb = work.tile([P, 2, D], BF16, name="xb", bufs=3, align_bytes=64)
-            for s in range(2):
-                n = 2 * q + s
-                i = [k for k, (a, b) in enumerate(X_CHUNKS) if a <= n < b][0]
-                nc.vector.tensor_tensor(
-                    out=xb[:, s, :],
-                    in0=xraw[i][:, n - X_CHUNKS[i][0], :].bitcast(FP8),
-                    in1=scale_sb[:],
-                    op=ALU.mult,
-                )
-            state["xb", q] = xb
+
+        def raw_tiles(n0, n1):
+            i = [k for k, (a, b) in enumerate(X_CHUNKS) if a <= n0 < b][0]
+            rows = xraw[i][:, n0 - X_CHUNKS[i][0] : n1 - X_CHUNKS[i][0], :]
+            return rows.rearrange("p s d -> p (s d)").bitcast(FP8)
+
+        def widen_pair(q):
+            half = rooms[q // 2 % 4][:, 2 * D * (q % 2) : 2 * D * (q % 2 + 1)]
+            nc.scalar.copy(out=half, in_=raw_tiles(2 * q, 2 * q + 2))
+
+        def widen_group(j):
+            nc.gpsimd.tensor_copy(out=rooms[j % 4][:], in_=raw_tiles(4 * j, 4 * j + 4))
 
         def x_transpose(q):
-            words = state["xb", q][:].rearrange("p s d -> p (s d)").bitcast(F32)
+            half = rooms[q // 2 % 4][:, 2 * D * (q % 2) : 2 * D * (q % 2 + 1)]
+            words = half.bitcast(F32)
             xt = psum.tile([P, 2, 2, P], F32, name="xt", tag="p2", bufs=2)
             for s in range(2):
                 for u in range(2):
                     nc.tensor.transpose(
-                        xt[:, s, u, :], words[:, 256 * s + u : 256 * (s + 1) : 2], ident[:]
+                        xt[:, u, s, :], words[:, 256 * s + u : 256 * (s + 1) : 2], ident[:]
                     )
             state["xt", q] = xt
 
-        def x_copy(q):
-            xg = work.tile([P, 2 * P, 4], BF16, name="xg", bufs=4, align_bytes=64)
-            words = xg[:].rearrange("p k t -> p (k t)").bitcast(F32)
-            dst = words.rearrange("p (s k u) -> p s k u", s=2, u=2)
-            src = state["xt", q][:].rearrange("p s u k -> p s k u")
-            if q in V_COPIES:
-                nc.vector.tensor_copy(out=dst, in_=src)
-            else:
-                nc.scalar.copy(out=dst, in_=src)
-            state["xg", q] = xg
+        def scaled(q0, q1):
+            room = rooms[(q0 // 2 - 1) % 4]
+            return room[:, 2 * D * (q0 % 2) : 2 * D * (q0 % 2 + q1 - q0)]
 
-        def x_quant(q):
-            cols = slice(256 * q, 256 * (q + 1))
-            quantise(x_codes[:, cols], x_scales[:, cols], state["xg", q][:])
+        def x_scale_out(q):
+            pairs = state["xt", q][:].rearrange("p u s k -> p (u s k)").bitcast(BF16)
+            nc.vector.tensor_tensor(
+                out=scaled(q, q + 1).rearrange("p (k u e) -> p k u e", u=2, e=2),
+                in0=pairs.rearrange("p (u k e) -> p k u e", u=2, e=2),
+                in1=scale_col[:]
+                .rearrange("p (u e) -> p u e", e=2)
+                .unsqueeze(1)
+                .broadcast_to([P, 2 * P, 2, 2]),
+                op=ALU.mult,
+            )
+
+        def x_quant(q0, q1):
+            cols = slice(256 * q0, 256 * q1)
+            values_of = scaled(q0, q1).rearrange("p (c j) -> p c j", j=4)
+            quantise(x_codes[:, cols], x_scales[:, cols], values_of)
 
         def mx_x(dst, n, codes, scales):
             cols = slice(P * n, P * (n + 1))
@@ -197,10 +202,16 @@ def tile_productkeysoftmemoryplus_t_kernel(
                 stop=True,
             )
 
-        def gate_matmul(n):
-            a_ps = psum.tile([P, D], F32, name="a_ps", tag="sc", bufs=2)
+        def gate_matmul(n, tag="sc", bufs=2):
+            a_ps = psum.tile([P, D], F32, name="a_ps", tag=tag, bufs=bufs)
             mx_x(a_ps[:], n, wg_codes, wg_scales)
             state["a", n] = a_ps
+
+        def early_gate_matmul(n):
+            if n % 5 < 3:
+                gate_matmul(n, "ub", 3)
+            else:
+                gate_matmul(n)
 
         def gate_silu(n):
             nc.scalar.activation(out=gates[n][:], in_=state["a", n][:], func=ACT.Silu)
@@ -253,10 +264,12 @@ def tile_productkeysoftmemoryplus_t_kernel(
             )
             state["zz", q] = zz
 
-        def reciprocals(q):
-            rz = work.tile([P, 2 * H], F32, name="rz", bufs=3)
-            nc.vector.reciprocal(out=rz[:], in_=state["zz", q][:])
-            state["rz", q] = rz
+        def reciprocals(q, tiles=(0, 1)):
+            if tiles[0] == 0:
+                rz = work.tile([P, 2 * H], F32, name="rz", bufs=3)
+                state["rz", q] = rz
+            cols = slice(H * tiles[0], H * (tiles[-1] + 1))
+            nc.vector.reciprocal(out=state["rz", q][:, cols], in_=state["zz", q][:, cols])
 
         def normalise(n):
             q, s = divmod(n, 2)
@@ -298,9 +311,13 @@ def tile_productkeysoftmemoryplus_t_kernel(
                 op=ALU.mult,
             )
 
-        def head_product(eng, n, h, e2):
-            pr = work.tile([P, 4, 2 * P], F32, name="pr%d" % h, bufs=3)
-            product(eng, pr[:], state["p1", n][:, h, :], e2)
+        def head_product(eng, n, h, e2, room=None):
+            if room is None:
+                tile = work.tile([P, 4, 2 * P], F32, name="pr%d" % h, bufs=3)
+                pr = tile[:]
+            else:
+                pr = room[:].bitcast(F32).rearrange("p (t c) -> p t c", t=4)
+            product(eng, pr, state["p1", n][:, h, :], e2)
             for g in range(2):
                 for t in range(4):
                     state["pr", n, h, g, t] = pr[:, t, P * g : P * (g + 1)]
@@ -312,16 +329,13 @@ def tile_productkeysoftmemoryplus_t_kernel(
                 state["pr", n, h, g, t0 + t] = dst[:, t, :]
 
         def v_planes(n):
+            if n == 2:
+                return 4
             return V_PLANES + (n >= NO_MAXIMA)
 
         def vector_products(n):
             e2 = state["e2_ps", n]
             head_product(nc.vector, n, V_HEAD, e2[:, 0:N])
-            if n == 0:
-                for h, g in S_HALVES[3 - V_FIRST :]:
-                    pr = half_tile(n, h, g)
-                    p1 = state["p1", n][:, h, 16 * g : 16 * (g + 1)]
-                    product(nc.vector, pr[:], p1, e2[:, N * h : N * (h + 1)])
             planes = v_planes(n)
             pr = work.tile([P, planes, P], F32, name="pr_cut_v", bufs=3)
             first = N * CUT_HALF[0]
@@ -329,11 +343,7 @@ def tile_productkeysoftmemoryplus_t_kernel(
 
         def gpsimd_cut(n):
             planes = 4 - v_planes(n)
-            if n >= 3:
-                room = gates[n - 3][:, 0 : planes * P]
-            else:
-                spare = keep.tile([P, planes * P], F32, name="pr_cut_g%d" % n)
-                room = spare[:]
+            room = gates[n - 3][:, 0 : planes * P]
             cut_product(
                 nc.gpsimd,
                 n,
@@ -342,6 +352,19 @@ def tile_productkeysoftmemoryplus_t_kernel(
                 e2_of(n, CUT_HALF[0])[:, N - 8 * planes : N],
             )
 
+        def half_product(eng, n, h, g, room=None):
+            if eng is nc.vector:
+                e2 = state["e2_ps", n][:, N * h : N * (h + 1)]
+            else:
+                e2 = e2_of(n, h)
+            if room is None:
+                pr = half_tile(n, h, g)[:]
+            else:
+                pr = room[:, 0 : 2 * D].bitcast(F32).rearrange("p (t c) -> p t c", t=4)
+                for t in range(4):
+                    state["pr", n, h, g, t] = pr[:, t, :]
+            product(eng, pr, state["p1", n][:, h, 16 * g : 16 * (g + 1)], e2)
+
         def half_tile(n, h, g):
             pr = work.tile([P, 4, P], F32, name="pr%d_%d" % (h, g), bufs=3)
             for t in range(4):
@@ -349,8 +372,6 @@ def tile_productkeysoftmemoryplus_t_kernel(
             return pr
 
         def scalar_product(n, k):
-            if n == 0 and k >= 3 - V_FIRST:
-                return
             h, g = S_HALVES[k]
             pr = half_tile(n, h, g)
             for i in range(16):
@@ -361,19 +382,20 @@ def tile_productkeysoftmemoryplus_t_kernel(
                     scale=state["p1", n][:, h, 16 * g + i : 16 * g + i + 1],
                 )
 
-        def sum_heads(n, g):
-            ub = psum.tile([P, 4, P], F32, name="ub_ps", tag="ub", bufs=3)
-            for t in range(4):
+        def sum_heads(n, g, planes=range(4)):
+            if planes[0] == 0:
+                ub = psum.tile([P, 4, P], F32, name="ub_ps", tag="ub", bufs=3)
+                state["ub", n, g] = ub
+            for t in planes:
                 for h in range(H):
                     nc.tensor.matmul(
-                        ub[:, t, :],
+                        state["ub", n, g][:, t, :],
                         lhsT=state["pr", n, h, g, t],
                         rhs=ident[:],
                         start=(h == 0),
                         stop=(h == H - 1),
                         is_transpose=True,
                     )
-            state["ub", n, g] = ub
 
         def gain(n, g):
             if g == 0:
@@ -386,19 +408,25 @@ def tile_productkeysoftmemoryplus_t_kernel(
                 op=ALU.mult,
             )
 
-        def u_quant(n):
-            uc = work.tile([P, 2 * P], U32, name="uc", align_bytes=64)
-            us = work.tile([P, 2 * P], U8, name="us", align_bytes=64)
-            quantise(uc[:], us[:], state["u", n][:].rearrange("p g k t -> p (g k) t"))
-            state["uc", n] = (uc, us)
-
-        def memory(n):
-            mem = psum.tile([P, D], F32, name="mem", tag="mem", bufs=1)
+        def u_quant(n, passes=(0, 1)):
+            if passes[0] == 0:
+                uc = work.tile([P, 2 * P], U32, name="uc", align_bytes=64)
+                us = work.tile([P, 2 * P], U8, name="us", align_bytes=64)
+                state["uc", n] = (uc, us)
             uc, us = state["uc", n]
-            for g in range(2):
+            cols = slice(P * passes[0], P * (passes[-1] + 1))
+            u = state["u", n][:, passes[0] : passes[-1] + 1, :, :]
+            quantise(uc[:, cols], us[:, cols], u.rearrange("p g k t -> p (g k) t"))
+
+        def memory(n, passes=(0, 1)):
+            if passes[0] == 0:
+                mem = psum.tile([P, D], F32, name="mem", tag="mem", bufs=1)
+                state["mem", n] = mem
+            uc, us = state["uc", n]
+            for g in passes:
                 cols = slice(P * g, P * (g + 1))
                 nc.tensor.matmul_mx(
-                    out=mem[:],
+                    out=state["mem", n][:],
                     lhsT=uc[:, cols].bitcast(FP8X4),
                     lhsT_scale=us[:, cols],
                     rhs=v_codes[:, g, :].bitcast(FP8X4),
@@ -406,7 +434,6 @@ def tile_productkeysoftmemoryplus_t_kernel(
                     start=(g == 0),
                     stop=(g == 1),
                 )
-            state["mem", n] = mem
 
         def final(n):
             o = work.tile([P, D], F32, name="o", bufs=4)
@@ -424,17 +451,13 @@ def tile_productkeysoftmemoryplus_t_kernel(
         def step(s):
             odd = s % 2 == 1
             shared = has(s + 1)
-            late = NPAIR - LATE_GATES // 2 + s + 1
-            late = late if s >= -1 and has_pair(late) else None
             if has(s - 2):
                 memory(s - 2)
             if has(s + 6) and s + 6 >= EARLY:
                 scores([s + 6])
-            if late is not None:
-                gate_matmul(2 * late)
-                gate_matmul(2 * late + 1)
-            if odd and has(s + 3) and s > -2:
-                e2_to_psum([s + 3, s + 4], N + 8 * v_planes(s + 4), "p2", 2)
+            if odd and has(s + 3):
+                keys = N + 8 * max(v_planes(s + 3), v_planes(s + 4))
+                e2_to_psum([s + 3, s + 4], keys, "p2", 2)
             if has(s):
                 sum_heads(s, 0)
                 sum_heads(s, 1)
@@ -442,15 +465,12 @@ def tile_productkeysoftmemoryplus_t_kernel(
                 head_product(nc.gpsimd, s + 1, G_HEAD, e2_of(s + 1, G_HEAD))
             if shared:
                 scalar_product(s + 1, 0)
-            if has(s + 2):
+            if has(s + 2) and s > 1:
                 normalise(s + 2)
             if shared:
                 scalar_product(s + 1, 1)
             if has(s + 5) and s + 5 >= EARLY:
                 exps(s + 5)
-            if late is not None:
-                gate_silu(2 * late)
-                gate_silu(2 * late + 1)
             if shared:
                 scalar_product(s + 1, 2)
             if has(s - 1):
@@ -459,12 +479,13 @@ def tile_productkeysoftmemoryplus_t_kernel(
                 vector_products(s + 1)
             if has(s - 2):
                 final(s - 2)
-            if shared:
+            if shared and v_planes(s + 1) < 4:
                 gpsimd_cut(s + 1)
+            if s == 1:
+                reciprocals(1, (1,))
+                normalise(3)
             if has(s - 1):
                 u_quant(s - 1)
-            if s in (-1, 0):
-                x_quant(NPAIR - 1 + s)
             if odd and has(s + 3):
                 denominators((s + 3) // 2)
             if has(s):
@@ -477,51 +498,126 @@ def tile_productkeysoftmemoryplus_t_kernel(
         def pair(q):
             return [2 * q, 2 * q + 1]
 
-        early_pairs = EARLY // 2
-        first = early_pairs + 2
-        gated = NPAIR - LATE_GATES // 2
-        extra = {0: wk_copy, 1: wk_quant, W_ROUND: wg_copy, W_ROUND + 1: wg_quant}
-        for i in range(4):
-            extra[V_ROUND + 2 * i] = lambda i=i: v_copy(i)
-            extra[V_ROUND + 2 * i + 1] = lambda i=i: v_quant(i)
-        for q in range(first):
-            x_product(q)
-            x_transpose(q)
-            if 0 <= q - 2 < early_pairs:
-                maxima(pair(q - 2))
-                exps(2 * q - 4)
-                exps(2 * q - 3)
-            if q in extra:
-                extra[q]()
-            if q > 0:
-                x_quant(q - 1)
-            x_copy(q)
-            if 0 <= q - 1 < early_pairs:
-                scores(pair(q - 1))
-        denominators(0)
-        e2_to_psum([0, 1], 3 * N, "mem", 1)
-        for q in range(first, max(NPAIR + 2, first + gated + 1)):
-            g = q - first - 1
-            if q == NPAIR:
-                normalise(0)
-            if q - 2 >= first and has_pair(q - 2):
-                x_copy(q - 2)
-            if 0 <= g < gated:
-                gate_silu(2 * g)
-                gate_silu(2 * g + 1)
-            if q - 1 >= first and has_pair(q - 1):
-                x_transpose(q - 1)
-            if g + 1 < gated:
-                gate_matmul(2 * g + 2)
-                gate_matmul(2 * g + 3)
-            if has_pair(q):
-                x_product(q)
-            if q == NPAIR - 1:
-                reciprocals(0)
-            if q in extra:
-                extra[q]()
-            if first - 1 <= q - 2 < NPAIR - 2:
-                x_quant(q - 2)
+        def softmax_start(q):
+            maxima(pair(q))
+            exps(2 * q)
+            exps(2 * q + 1)
 
-        for s in range(-1, NT + 2):
+        counts = {"matmul": 0, "silu": 0}
+
+        def gates_up_to(quantised, more):
+            for k in range(more + 1):
+                if k > 0 and counts["silu"] < counts["matmul"]:
+                    gate_silu(counts["silu"])
+                    counts["silu"] = counts["silu"] + 1
+                while counts["matmul"] < min(counts["silu"] + GATE_LEAD, quantised):
+                    early_gate_matmul(counts["matmul"])
+                    counts["matmul"] = counts["matmul"] + 1
+
+        widen_pair(0)
+        widen_pair(1)
+        wk_copy()
+        x_transpose(0)
+        x_transpose(1)
+        wk_quant()
+        widen_group(1)
+        widen_group(2)
+        wg_copy(0)
+        wg_copy(1)
+        v_copy(0)
+        v_copy(1)
+        x_scale_out(0)
+        x_scale_out(1)
+        x_transpose(2)
+        x_transpose(3)
+        x_quant(0, 2)
+        widen_group(3)
+        scores(pair(0))
+        scores(pair(1))
+        x_scale_out(2)
+        softmax_start(0)
+        x_transpose(4)
+        last_group = NPAIR // 2 - 1
+        for j in range(1, last_group + 1):
+            more = GATES_BY_ROUND[j - 1]
+            x_scale_out(2 * j + 1)
+            if j == 1:
+                softmax_start(1)
+            if j == 2:
+                softmax_start(2)
+                e2_to_psum([0, 1], 3 * N, "mem", 1)
+                denominators(0)
+            if j == 3:
+                denominators(1)
+                reciprocals(0)
+            if j == 4:
+                reciprocals(1, (0,))
+                normalise(0)
+                normalise(1)
+            if j < last_group:
+                x_transpose(2 * j + 3)
+            if j > 2:
+                gates_up_to(4 * j, more // 2)
+            if j < last_group:
+                x_scale_out(2 * j + 2)
+            if j == 2:
+                softmax_start(3)
+            if j + 1 < last_group:
+                x_transpose(2 * j + 4)
+            if j > 2:
+                gates_up_to(4 * j, more - more // 2)
+            if j == 1:
+                v_copy(2)
+            if j == 2:
+                wg_quant()
+            if j >= 5:
+                half_product(nc.vector, 0, *S_HALVES[j - 5])
+            if 3 <= j < 7:
+                v_quant(j - 3)
+            x_quant(2 * j, 2 * j + 2)
+            if j == 1:
+                scores(pair(2))
+                scores(pair(3))
+            if j == 2:
+                v_copy(3)
+                gates_up_to(4 * j, 0)
+            if j + 3 <= last_group:
+                widen_group(j + 3)
+            elif j == last_group - 1:
+                half_product(nc.gpsimd, 0, 1, 1, rooms[(j + 3) % 4])
+            else:
+                n = (j + 2 - last_group) // 2
+                head_product(nc.gpsimd, n, G_HEAD, e2_of(n, G_HEAD), rooms[(j + 3) % 4])
+
+        head_product(nc.vector, 0, V_HEAD, state["e2_ps", 0][:, 0:N])
+        normalise(2)
+        gates_up_to(NT, NT - counts["silu"])
+        e2_to_psum([2, 3], 2 * N, "p2", 2)
+        sum_heads(0, 0)
+        sum_heads(0, 1)
+        head_product(nc.vector, 1, V_HEAD, state["e2_ps", 1][:, 0:N])
+        half_product(nc.vector, 1, 1, 0)
+        half_product(nc.gpsimd, 1, 1, 1)
+        scalar_product(1, 1)
+        scalar_product(1, 2)
+        gain(0, 0)
+
+        for s in range(1, NT - 1):
             step(s)
+
+        last = NT - 1
+        memory(last - 2)
+        sum_heads(last, 0)
+        gain(last - 1, 1)
+        final(last - 2)
+        u_quant(last - 1)
+        memory(last - 1)
+        sum_heads(last, 1)
+        gain(last, 0)
+        final(last - 1)
+        u_quant(last, (0,))
+        memory(last, (0,))
+        gain(last, 1)
+        u_quant(last, (1,))
+        memory(last, (1,))
+        final(last)

@@ -28,7 +28,7 @@ CUT_HALF = (1, 1)
 V_PLANES = 2
 NO_MAXIMA = NT - 6
 
-X_CHUNKS = [(0, 4), (4, 8), (8, 16), (16, 24), (24, 32)]
+X_CHUNKS = [(0, 2), (2, 4), (4, 8), (8, 16), (16, 24), (24, 32)]
 GATE_LEAD = 4
 GATES_BY_ROUND = (0, 0, 4, 6, 6, 6, 6)
 E_BUFS = 5
@@ -70,15 +70,16 @@ def tile_productkeysoftmemoryplus_t_kernel(
             )
 
         load_x(0)
-        nc.sync.dma_start(out=wk_raw[:], in_=wk.rearrange("(p j) c -> p j c", j=4))
-        nc.sync.dma_start(out=scale_col[:], in_=x_scale.rearrange("o (p t) -> p (o t)", t=4))
         load_x(1)
-        nc.sync.dma_start(out=wg_raw[:], in_=wg.rearrange("(p j) c -> p j c", j=4))
-        load_values(0)
+        nc.sync.dma_start(out=scale_col[:], in_=x_scale.rearrange("o (p t) -> p (o t)", t=4))
+        nc.sync.dma_start(out=wk_raw[:], in_=wk.rearrange("(p j) c -> p j c", j=4))
         load_x(2)
-        load_values(1)
+        nc.sync.dma_start(out=wg_raw[:], in_=wg.rearrange("(p j) c -> p j c", j=4))
         load_x(3)
+        load_values(0)
+        load_values(1)
         load_x(4)
+        load_x(5)
         nc.sync.dma_start(out=gain_sb[:], in_=slot_gain.rearrange("(g p t) -> p g t", p=P, t=4))
 
         ident = keep.tile([P, P], F32, name="ident")
@@ -106,7 +107,8 @@ def tile_productkeysoftmemoryplus_t_kernel(
         ]
 
         wg_il = keep.tile([P, D, 4], BF16, name="wg_il", align_bytes=64)
-        wk_il = rooms[1][:, 0 : 4 * C].rearrange("p (c j) -> p c j", j=4)
+        wk_tile = keep.tile([P, C, 4], BF16, name="wk_il", align_bytes=64)
+        wk_il = wk_tile[:]
 
         def interleave(copy, dst, src):
             copy(
@@ -124,8 +126,8 @@ def tile_productkeysoftmemoryplus_t_kernel(
         def wk_copy():
             src = wk_raw[:].rearrange("p j (h a k) -> p a h k j", a=2, k=N)
             dst = wk_il.rearrange("p (a h k) j -> p a h k j", a=2, k=N)
-            nc.vector.tensor_copy(out=dst[:, 0], in_=src[:, 0])
-            nc.vector.tensor_copy(
+            nc.scalar.copy(out=dst[:, 0], in_=src[:, 0])
+            nc.scalar.copy(
                 out=dst[:, 1].rearrange("p h (t m) j -> p h t m j", t=4),
                 in_=src[:, 1].rearrange("p h (m t) j -> p h t m j", t=4),
             )
@@ -153,7 +155,7 @@ def tile_productkeysoftmemoryplus_t_kernel(
 
         def widen_pair(q):
             half = rooms[q // 2 % 4][:, 2 * D * (q % 2) : 2 * D * (q % 2 + 1)]
-            nc.scalar.copy(out=half, in_=raw_tiles(2 * q, 2 * q + 2))
+            nc.vector.tensor_copy(out=half, in_=raw_tiles(2 * q, 2 * q + 2))
 
         def widen_group(j):
             nc.gpsimd.tensor_copy(out=rooms[j % 4][:], in_=raw_tiles(4 * j, 4 * j + 4))
@@ -463,27 +465,16 @@ def tile_productkeysoftmemoryplus_t_kernel(
                 sum_heads(s, 1)
             if has(s + 1):
                 head_product(nc.gpsimd, s + 1, G_HEAD, e2_of(s + 1, G_HEAD))
-            if shared:
-                scalar_product(s + 1, 0)
-            if has(s + 2) and s > 1:
-                normalise(s + 2)
-            if shared:
-                scalar_product(s + 1, 1)
-            if has(s + 5) and s + 5 >= EARLY:
-                exps(s + 5)
-            if shared:
-                scalar_product(s + 1, 2)
+            if has(s + 1) and s > 1:
+                vector_products(s + 1)
             if has(s - 1):
                 gain(s - 1, 1)
-            if has(s + 1):
-                vector_products(s + 1)
             if has(s - 2):
                 final(s - 2)
             if shared and v_planes(s + 1) < 4:
                 gpsimd_cut(s + 1)
             if s == 1:
                 reciprocals(1, (1,))
-                normalise(3)
             if has(s - 1):
                 u_quant(s - 1)
             if odd and has(s + 3):
@@ -494,6 +485,16 @@ def tile_productkeysoftmemoryplus_t_kernel(
                 maxima([s + 6])
             if odd and has(s + 3):
                 reciprocals((s + 3) // 2)
+            if shared:
+                scalar_product(s + 1, 0)
+            if has(s + 2):
+                normalise(s + 2)
+            if shared:
+                scalar_product(s + 1, 1)
+            if has(s + 5) and s + 5 >= EARLY:
+                exps(s + 5)
+            if shared:
+                scalar_product(s + 1, 2)
 
         def pair(q):
             return [2 * q, 2 * q + 1]
@@ -519,7 +520,6 @@ def tile_productkeysoftmemoryplus_t_kernel(
         wk_copy()
         x_transpose(0)
         x_transpose(1)
-        wk_quant()
         widen_group(1)
         widen_group(2)
         wg_copy(0)
@@ -530,6 +530,7 @@ def tile_productkeysoftmemoryplus_t_kernel(
         x_scale_out(1)
         x_transpose(2)
         x_transpose(3)
+        wk_quant()
         x_quant(0, 2)
         widen_group(3)
         scores(pair(0))
@@ -544,16 +545,14 @@ def tile_productkeysoftmemoryplus_t_kernel(
             if j == 1:
                 softmax_start(1)
             if j == 2:
+                denominators(0)
                 softmax_start(2)
                 e2_to_psum([0, 1], 3 * N, "mem", 1)
-                denominators(0)
+                reciprocals(0)
             if j == 3:
                 denominators(1)
-                reciprocals(0)
             if j == 4:
                 reciprocals(1, (0,))
-                normalise(0)
-                normalise(1)
             if j < last_group:
                 x_transpose(2 * j + 3)
             if j > 2:
@@ -562,6 +561,8 @@ def tile_productkeysoftmemoryplus_t_kernel(
                 x_scale_out(2 * j + 2)
             if j == 2:
                 softmax_start(3)
+                normalise(0)
+                normalise(1)
             if j + 1 < last_group:
                 x_transpose(2 * j + 4)
             if j > 2:
@@ -570,10 +571,15 @@ def tile_productkeysoftmemoryplus_t_kernel(
                 v_copy(2)
             if j == 2:
                 wg_quant()
+            if j == 4:
+                head_product(nc.vector, 0, V_HEAD, state["e2_ps", 0][:, 0:N])
             if j >= 5:
                 half_product(nc.vector, 0, *S_HALVES[j - 5])
             if 3 <= j < 7:
                 v_quant(j - 3)
+            if j == last_group:
+                normalise(2)
+                e2_to_psum([2, 3], 2 * N, "p2", 2)
             x_quant(2 * j, 2 * j + 2)
             if j == 1:
                 scores(pair(2))
@@ -589,17 +595,15 @@ def tile_productkeysoftmemoryplus_t_kernel(
                 n = (j + 2 - last_group) // 2
                 head_product(nc.gpsimd, n, G_HEAD, e2_of(n, G_HEAD), rooms[(j + 3) % 4])
 
-        head_product(nc.vector, 0, V_HEAD, state["e2_ps", 0][:, 0:N])
-        normalise(2)
         gates_up_to(NT, NT - counts["silu"])
-        e2_to_psum([2, 3], 2 * N, "p2", 2)
         sum_heads(0, 0)
         sum_heads(0, 1)
         head_product(nc.vector, 1, V_HEAD, state["e2_ps", 1][:, 0:N])
         half_product(nc.vector, 1, 1, 0)
-        half_product(nc.gpsimd, 1, 1, 1)
         scalar_product(1, 1)
         scalar_product(1, 2)
+        vector_products(2)
+        half_product(nc.vector, 1, 1, 1)
         gain(0, 0)
 
         for s in range(1, NT - 1):

@@ -49,13 +49,17 @@ def tile_productkeysoftmemoryplus_t_kernel(
         ctx.enter_context(tc.manual_schedule())
         state = {}
 
+        rooms = [
+            keep.tile([P, 4 * D], BF16, name="x_room%d" % r, align_bytes=64) for r in range(4)
+        ]
+
         xraw = []
         for a, b in X_CHUNKS:
             xr = keep.tile([P, b - a, D], U8, name="xraw%d" % a, align_bytes=64)
             xraw.append(xr)
         scale_col = keep.tile([P, 4], F32, name="scale_col")
         wg_raw = keep.tile([P, 4, D], BF16, name="wg_raw")
-        wk_raw = keep.tile([P, 4, C], BF16, name="wk_raw")
+        wk_raw = rooms[1][:, 0 : 4 * C].rearrange("p (j c) -> p j c", j=4)
         v_raw = [keep.tile([P, 4, D], BF16, name="v_raw%d" % g) for g in range(2)]
         gain_sb = keep.tile([P, 2, 4], BF16, name="gain_sb")
 
@@ -70,9 +74,9 @@ def tile_productkeysoftmemoryplus_t_kernel(
             )
 
         load_x(0)
+        nc.sync.dma_start(out=wk_raw, in_=wk.rearrange("(p j) c -> p j c", j=4))
         load_x(1)
         nc.sync.dma_start(out=scale_col[:], in_=x_scale.rearrange("o (p t) -> p (o t)", t=4))
-        nc.sync.dma_start(out=wk_raw[:], in_=wk.rearrange("(p j) c -> p j c", j=4))
         load_x(2)
         nc.sync.dma_start(out=wg_raw[:], in_=wg.rearrange("(p j) c -> p j c", j=4))
         load_x(3)
@@ -102,13 +106,8 @@ def tile_productkeysoftmemoryplus_t_kernel(
                 in_=interleaved.rearrange("p c j -> p (c j)"),
             )
 
-        rooms = [
-            keep.tile([P, 4 * D], BF16, name="x_room%d" % r, align_bytes=64) for r in range(4)
-        ]
-
         wg_il = keep.tile([P, D, 4], BF16, name="wg_il", align_bytes=64)
-        wk_tile = keep.tile([P, C, 4], BF16, name="wk_il", align_bytes=64)
-        wk_il = wk_tile[:]
+        wk_il = rooms[2][:, 0 : 4 * C].rearrange("p (c j) -> p c j", j=4)
 
         def interleave(copy, dst, src):
             copy(
@@ -124,10 +123,10 @@ def tile_productkeysoftmemoryplus_t_kernel(
             quantise(wg_codes[:], wg_scales[:], wg_il[:])
 
         def wk_copy():
-            src = wk_raw[:].rearrange("p j (h a k) -> p a h k j", a=2, k=N)
+            src = wk_raw.rearrange("p j (h a k) -> p a h k j", a=2, k=N)
             dst = wk_il.rearrange("p (a h k) j -> p a h k j", a=2, k=N)
-            nc.scalar.copy(out=dst[:, 0], in_=src[:, 0])
-            nc.scalar.copy(
+            nc.vector.tensor_copy(out=dst[:, 0], in_=src[:, 0])
+            nc.vector.tensor_copy(
                 out=dst[:, 1].rearrange("p h (t m) j -> p h t m j", t=4),
                 in_=src[:, 1].rearrange("p h (m t) j -> p h t m j", t=4),
             )
@@ -155,7 +154,7 @@ def tile_productkeysoftmemoryplus_t_kernel(
 
         def widen_pair(q):
             half = rooms[q // 2 % 4][:, 2 * D * (q % 2) : 2 * D * (q % 2 + 1)]
-            nc.vector.tensor_copy(out=half, in_=raw_tiles(2 * q, 2 * q + 2))
+            nc.scalar.copy(out=half, in_=raw_tiles(2 * q, 2 * q + 2))
 
         def widen_group(j):
             nc.gpsimd.tensor_copy(out=rooms[j % 4][:], in_=raw_tiles(4 * j, 4 * j + 4))
@@ -455,13 +454,15 @@ def tile_productkeysoftmemoryplus_t_kernel(
             shared = has(s + 1)
             if has(s - 2):
                 memory(s - 2)
-            if has(s + 6) and s + 6 >= EARLY:
+            if has(s + 6) and s + 6 > EARLY:
                 scores([s + 6])
-            if odd and has(s + 3):
+            if odd and has(s + 3) and s > 1:
                 keys = N + 8 * max(v_planes(s + 3), v_planes(s + 4))
                 e2_to_psum([s + 3, s + 4], keys, "p2", 2)
             if has(s):
                 sum_heads(s, 0)
+                if s == 1:
+                    scores([EARLY])
                 sum_heads(s, 1)
             if has(s + 1):
                 head_product(nc.gpsimd, s + 1, G_HEAD, e2_of(s + 1, G_HEAD))
@@ -521,7 +522,6 @@ def tile_productkeysoftmemoryplus_t_kernel(
         x_transpose(0)
         x_transpose(1)
         widen_group(1)
-        widen_group(2)
         wg_copy(0)
         wg_copy(1)
         v_copy(0)
@@ -532,6 +532,7 @@ def tile_productkeysoftmemoryplus_t_kernel(
         x_transpose(3)
         wk_quant()
         x_quant(0, 2)
+        widen_group(2)
         widen_group(3)
         scores(pair(0))
         scores(pair(1))
@@ -597,6 +598,7 @@ def tile_productkeysoftmemoryplus_t_kernel(
 
         gates_up_to(NT, NT - counts["silu"])
         sum_heads(0, 0)
+        e2_to_psum([4, 5], N + 8 * V_PLANES, "p2", 2)
         sum_heads(0, 1)
         head_product(nc.vector, 1, V_HEAD, state["e2_ps", 1][:, 0:N])
         half_product(nc.vector, 1, 1, 0)

@@ -383,20 +383,19 @@ def tile_productkeysoftmemoryplus_t_kernel(
                     scale=state["p1", n][:, h, 16 * g + i : 16 * g + i + 1],
                 )
 
-        def sum_heads(n, g, planes=range(4)):
-            if planes[0] == 0:
-                ub = psum.tile([P, 4, P], F32, name="ub_ps", tag="ub", bufs=3)
-                state["ub", n, g] = ub
-            for t in planes:
-                for h in range(H):
+        def sum_heads(n, g):
+            ub = psum.tile([P, 4, P], F32, name="ub_ps", tag="ub", bufs=3)
+            for h in range(H):
+                for t in range(4):
                     nc.tensor.matmul(
-                        state["ub", n, g][:, t, :],
+                        ub[:, t, :],
                         lhsT=state["pr", n, h, g, t],
                         rhs=ident[:],
-                        start=(h == 0),
-                        stop=(h == H - 1),
+                        start=(h == 0 and t == 0),
+                        stop=(h == H - 1 and t == 3),
                         is_transpose=True,
                     )
+            state["ub", n, g] = ub
 
         def gain(n, g):
             if g == 0:

@@ -29,10 +29,10 @@ V_PLANES = 2
 NO_MAXIMA = NT - 6
 
 X_CHUNKS = [(0, 2), (2, 4), (4, 8), (8, 16), (16, 24), (24, 32)]
-GATE_LEAD = 4
-GATES_BY_ROUND = (0, 0, 4, 6, 6, 6, 6)
-E_BUFS = 5
 EARLY = 8
+GATE_LEAD = 4
+GATES_A_ROUND = 6
+FIRST_GATES = 4
 
 
 def tile_productkeysoftmemoryplus_t_kernel(
@@ -146,7 +146,6 @@ def tile_productkeysoftmemoryplus_t_kernel(
             cols = slice(256 * b, 256 * (b + 1))
             quantise(v_codes[:, g, cols], v_scales[:, g, cols], state["v_il", i])
 
-
         def raw_tiles(n0, n1):
             i = [k for k, (a, b) in enumerate(X_CHUNKS) if a <= n0 < b][0]
             rows = xraw[i][:, n0 - X_CHUNKS[i][0] : n1 - X_CHUNKS[i][0], :]
@@ -203,16 +202,13 @@ def tile_productkeysoftmemoryplus_t_kernel(
                 stop=True,
             )
 
-        def gate_matmul(n, tag="sc", bufs=2):
-            a_ps = psum.tile([P, D], F32, name="a_ps", tag=tag, bufs=bufs)
+        def gate_matmul(n):
+            if n % 5 < 3:
+                a_ps = psum.tile([P, D], F32, name="a_ps", tag="ub", bufs=3)
+            else:
+                a_ps = psum.tile([P, D], F32, name="a_ps", tag="sc", bufs=2)
             mx_x(a_ps[:], n, wg_codes, wg_scales)
             state["a", n] = a_ps
-
-        def early_gate_matmul(n):
-            if n % 5 < 3:
-                gate_matmul(n, "ub", 3)
-            else:
-                gate_matmul(n)
 
         def gate_silu(n):
             nc.scalar.activation(out=gates[n][:], in_=state["a", n][:], func=ACT.Silu)
@@ -239,8 +235,8 @@ def tile_productkeysoftmemoryplus_t_kernel(
         def exps(n):
             q, s = divmod(n, 2)
             if s == 0:
-                e = work.tile([P, 2, 2, H, N], F32, name="e", bufs=E_BUFS)
-                z = work.tile([P, 2, H, 2], F32, name="z", bufs=E_BUFS)
+                e = work.tile([P, 2, 2, H, N], F32, name="e", bufs=EARLY // 2 + 1)
+                z = work.tile([P, 2, H, 2], F32, name="z", bufs=EARLY // 2 + 1)
                 state["e", q], state["z", q] = e, z
             e, z = state["e", q], state["z", q]
             sc, nm = state["sc", n], state["nm", n]
@@ -284,21 +280,14 @@ def tile_productkeysoftmemoryplus_t_kernel(
                 )
             state["p1", n] = p1
 
-        def e2_to_psum(tiles, keys, tag, bufs):
-            e2 = psum.tile([P, len(tiles), keys], F32, name="e2_ps", tag=tag, bufs=bufs)
-            for q in sorted(set(n // 2 for n in tiles)):
-                mine = [n for n in tiles if n // 2 == q]
-                rows = slice(mine[0] % 2, mine[-1] % 2 + 1)
-                k = tiles.index(mine[0])
-                nc.tensor.matmul(
-                    e2[:, k : k + len(mine), :],
-                    lhsT=ident[:],
-                    rhs=state["e", q][:, rows, 1, :, :].rearrange("p s h k -> p s (h k)")[:, :, 0:keys],
-                    start=True,
-                    stop=True,
-                )
-            for k, n in enumerate(tiles):
-                state["e2_ps", n] = e2[:, k, :]
+        def e2_to_psum(q, keys, tag="p2", bufs=2):
+            e2 = psum.tile([P, 2, keys], F32, name="e2_ps", tag=tag, bufs=bufs)
+            second = state["e", q][:, :, 1, :, :].rearrange("p s h k -> p s (h k)")
+            nc.tensor.matmul(
+                e2[:], lhsT=ident[:], rhs=second[:, :, 0:keys], start=True, stop=True
+            )
+            for s in range(2):
+                state["e2_ps", 2 * q + s] = e2[:, s, :]
 
         def e2_of(n, h):
             return state["e", n // 2][:, n % 2, 1, h, :]
@@ -332,7 +321,7 @@ def tile_productkeysoftmemoryplus_t_kernel(
         def v_planes(n):
             if n == 2:
                 return 4
-            return V_PLANES + (n >= NO_MAXIMA)
+            return V_PLANES - n % 2 + (n >= NO_MAXIMA)
 
         def vector_products(n):
             e2 = state["e2_ps", n]
@@ -445,56 +434,43 @@ def tile_productkeysoftmemoryplus_t_kernel(
         def has(n):
             return 0 <= n < NT
 
-        def has_pair(q):
-            return 0 <= q < NPAIR
-
         def step(s):
             odd = s % 2 == 1
-            shared = has(s + 1)
-            if has(s - 2):
+            if s >= 2:
                 memory(s - 2)
-            if has(s + 6) and s + 6 > EARLY:
+            if EARLY < s + 6 < NT:
                 scores([s + 6])
             if odd and has(s + 3) and s > 1:
                 keys = N + 8 * max(v_planes(s + 3), v_planes(s + 4))
-                e2_to_psum([s + 3, s + 4], keys, "p2", 2)
-            if has(s):
-                sum_heads(s, 0)
-                if s == 1:
-                    scores([EARLY])
-                sum_heads(s, 1)
-            if has(s + 1):
-                head_product(nc.gpsimd, s + 1, G_HEAD, e2_of(s + 1, G_HEAD))
-            if has(s + 1) and s > 1:
-                vector_products(s + 1)
-            if has(s - 1):
-                gain(s - 1, 1)
-            if has(s - 2):
-                final(s - 2)
-            if shared and v_planes(s + 1) < 4:
-                gpsimd_cut(s + 1)
+                e2_to_psum((s + 3) // 2, keys)
+            sum_heads(s, 0)
             if s == 1:
+                scores([EARLY])
+            sum_heads(s, 1)
+            head_product(nc.gpsimd, s + 1, G_HEAD, e2_of(s + 1, G_HEAD))
+            if s > 1:
+                vector_products(s + 1)
+            gain(s - 1, 1)
+            if s >= 2:
+                final(s - 2)
+                gpsimd_cut(s + 1)
+            else:
                 reciprocals(1, (1,))
-            if has(s - 1):
-                u_quant(s - 1)
+            u_quant(s - 1)
             if odd and has(s + 3):
                 denominators((s + 3) // 2)
-            if has(s):
-                gain(s, 0)
-            if has(s + 6) and s + 6 >= EARLY:
+            gain(s, 0)
+            if EARLY <= s + 6 < NT:
                 maxima([s + 6])
             if odd and has(s + 3):
                 reciprocals((s + 3) // 2)
-            if shared:
-                scalar_product(s + 1, 0)
+            scalar_product(s + 1, 0)
             if has(s + 2):
                 normalise(s + 2)
-            if shared:
-                scalar_product(s + 1, 1)
-            if has(s + 5) and s + 5 >= EARLY:
+            scalar_product(s + 1, 1)
+            if EARLY <= s + 5 < NT:
                 exps(s + 5)
-            if shared:
-                scalar_product(s + 1, 2)
+            scalar_product(s + 1, 2)
 
         def pair(q):
             return [2 * q, 2 * q + 1]
@@ -512,7 +488,7 @@ def tile_productkeysoftmemoryplus_t_kernel(
                     gate_silu(counts["silu"])
                     counts["silu"] = counts["silu"] + 1
                 while counts["matmul"] < min(counts["silu"] + GATE_LEAD, quantised):
-                    early_gate_matmul(counts["matmul"])
+                    gate_matmul(counts["matmul"])
                     counts["matmul"] = counts["matmul"] + 1
 
         widen_pair(0)
@@ -540,14 +516,14 @@ def tile_productkeysoftmemoryplus_t_kernel(
         x_transpose(4)
         last_group = NPAIR // 2 - 1
         for j in range(1, last_group + 1):
-            more = GATES_BY_ROUND[j - 1]
+            more = FIRST_GATES if j == 3 else GATES_A_ROUND
             x_scale_out(2 * j + 1)
             if j == 1:
                 softmax_start(1)
             if j == 2:
                 denominators(0)
                 softmax_start(2)
-                e2_to_psum([0, 1], 3 * N, "mem", 1)
+                e2_to_psum(0, 3 * N, "mem", 1)
                 reciprocals(0)
             if j == 3:
                 denominators(1)
@@ -579,7 +555,7 @@ def tile_productkeysoftmemoryplus_t_kernel(
                 v_quant(j - 3)
             if j == last_group:
                 normalise(2)
-                e2_to_psum([2, 3], 2 * N, "p2", 2)
+                e2_to_psum(1, 2 * N)
             x_quant(2 * j, 2 * j + 2)
             if j == 1:
                 scores(pair(2))
@@ -597,7 +573,7 @@ def tile_productkeysoftmemoryplus_t_kernel(
 
         gates_up_to(NT, NT - counts["silu"])
         sum_heads(0, 0)
-        e2_to_psum([4, 5], N + 8 * V_PLANES, "p2", 2)
+        e2_to_psum(2, N + 8 * V_PLANES)
         sum_heads(0, 1)
         head_product(nc.vector, 1, V_HEAD, state["e2_ps", 1][:, 0:N])
         half_product(nc.vector, 1, 1, 0)

@@ -19,20 +19,15 @@ SLOTS = N * N
 P = 128
 NT = T // P
 NPAIR = NT // 2
+NGROUP = NT // 4
 
 FLOPS = 2 * T * D * C + 2 * T * SLOTS * D + 2 * T * D * D
 
-V_HEAD, G_HEAD = 0, 3
-S_HALVES = [(1, 0), (2, 0), (2, 1)]
-CUT_HALF = (1, 1)
-V_PLANES = 2
-NO_MAXIMA = NT - 6
+BASE, RATIO, HEAD_C, HEAD_D = 0, 1, 2, 3
+FLOOR = -80.0
+EARLY_ROWS = 10
 
 X_CHUNKS = [(0, 2), (2, 4), (4, 8), (8, 16), (16, 24), (24, 32)]
-EARLY = 8
-GATE_LEAD = 4
-GATES_A_ROUND = 6
-FIRST_GATES = 4
 
 
 def tile_productkeysoftmemoryplus_t_kernel(
@@ -49,8 +44,12 @@ def tile_productkeysoftmemoryplus_t_kernel(
         ctx.enter_context(tc.manual_schedule())
         state = {}
 
-        rooms = [
-            keep.tile([P, 4 * D], BF16, name="x_room%d" % r, align_bytes=64) for r in range(4)
+        def bank(b, shape, name):
+            tile = psum.tile([P] + shape, F32, name=name, tag="bank%d" % b, bufs=1)
+            return tile
+
+        x_rooms = [
+            keep.tile([P, 4 * D], BF16, name="x_room%d" % r, align_bytes=64) for r in range(3)
         ]
 
         xraw = []
@@ -59,7 +58,7 @@ def tile_productkeysoftmemoryplus_t_kernel(
             xraw.append(xr)
         scale_col = keep.tile([P, 4], F32, name="scale_col")
         wg_raw = keep.tile([P, 4, D], BF16, name="wg_raw")
-        wk_raw = rooms[1][:, 0 : 4 * C].rearrange("p (j c) -> p j c", j=4)
+        wk_raw = keep.tile([P, 4, C], BF16, name="wk_raw")
         v_raw = [keep.tile([P, 4, D], BF16, name="v_raw%d" % g) for g in range(2)]
         gain_sb = keep.tile([P, 2, 4], BF16, name="gain_sb")
 
@@ -74,7 +73,7 @@ def tile_productkeysoftmemoryplus_t_kernel(
             )
 
         load_x(0)
-        nc.sync.dma_start(out=wk_raw, in_=wk.rearrange("(p j) c -> p j c", j=4))
+        nc.sync.dma_start(out=wk_raw[:], in_=wk.rearrange("(p j) c -> p j c", j=4))
         load_x(1)
         nc.sync.dma_start(out=scale_col[:], in_=x_scale.rearrange("o (p t) -> p (o t)", t=4))
         load_x(2)
@@ -97,71 +96,46 @@ def tile_productkeysoftmemoryplus_t_kernel(
         wk_scales = keep.tile([P, C], U8, name="wk_scales", align_bytes=64)
         v_codes = keep.tile([P, 2, D], U32, name="v_codes", align_bytes=64)
         v_scales = keep.tile([P, 2, D], U8, name="v_scales", align_bytes=64)
-        gates = [keep.tile([P, D], F32, name="gate%d" % n) for n in range(NT)]
 
         def quantise(codes, scales, interleaved):
-            nc.vector.quantize_mx(
-                out=codes.bitcast(FP8X4),
-                scales=scales,
-                in_=interleaved.rearrange("p c j -> p (c j)"),
-            )
+            nc.vector.quantize_mx(out=codes.bitcast(FP8X4), scales=scales, in_=interleaved)
 
-        wg_il = keep.tile([P, D, 4], BF16, name="wg_il", align_bytes=64)
-        wk_il = rooms[2][:, 0 : 4 * C].rearrange("p (c j) -> p c j", j=4)
+        wg_il = keep.tile([P, 4 * D], BF16, name="wg_il", align_bytes=64)
+        v_il = [keep.tile([P, 4 * D], BF16, name="v_il%d" % g, align_bytes=64) for g in range(2)]
+        wk_il = wg_il[:, 0 : 4 * C]
 
-        def interleave(copy, dst, src):
+        def interleave(copy, dst, src, c0, c1):
             copy(
-                out=dst.rearrange("p (c i) j -> p c j i", i=4),
-                in_=src.rearrange("p j (c i) -> p c j i", i=4),
+                out=dst[:, 4 * c0 : 4 * c1].rearrange("p (c i j) -> p c j i", i=4, j=4),
+                in_=src[:, :, c0:c1].rearrange("p j (c i) -> p c j i", i=4),
             )
-
-        def wg_copy(b):
-            cols = slice(256 * b, 256 * (b + 1))
-            interleave(nc.scalar.copy, wg_il[:, cols, :], wg_raw[:, :, cols])
-
-        def wg_quant():
-            quantise(wg_codes[:], wg_scales[:], wg_il[:])
 
         def wk_copy():
-            src = wk_raw.rearrange("p j (h a k) -> p a h k j", a=2, k=N)
-            dst = wk_il.rearrange("p (a h k) j -> p a h k j", a=2, k=N)
+            src = wk_raw[:].rearrange("p j (h a k) -> p a h k j", a=2, k=N)
+            dst = wk_il.rearrange("p (a h k j) -> p a h k j", a=2, k=N, j=4)
             nc.vector.tensor_copy(out=dst[:, 0], in_=src[:, 0])
             nc.vector.tensor_copy(
                 out=dst[:, 1].rearrange("p h (t m) j -> p h t m j", t=4),
                 in_=src[:, 1].rearrange("p h (m t) j -> p h t m j", t=4),
             )
 
-        def wk_quant():
-            quantise(wk_codes[:], wk_scales[:], wk_il)
-
-        def v_copy(i):
-            g, b = divmod(i, 2)
-            v_il = work.tile([P, 256, 4], BF16, name="v_il", bufs=4, align_bytes=64)
-            copy = nc.vector.tensor_copy if i == 3 else nc.scalar.copy
-            interleave(copy, v_il[:], v_raw[g][:, :, 256 * b : 256 * (b + 1)])
-            state["v_il", i] = v_il[:]
-
-        def v_quant(i):
-            g, b = divmod(i, 2)
-            cols = slice(256 * b, 256 * (b + 1))
-            quantise(v_codes[:, g, cols], v_scales[:, g, cols], state["v_il", i])
-
         def raw_tiles(n0, n1):
             i = [k for k, (a, b) in enumerate(X_CHUNKS) if a <= n0 < b][0]
             rows = xraw[i][:, n0 - X_CHUNKS[i][0] : n1 - X_CHUNKS[i][0], :]
             return rows.rearrange("p s d -> p (s d)").bitcast(FP8)
 
+        def widened(q):
+            return x_rooms[q // 2 % 3][:, 2 * D * (q % 2) : 2 * D * (q % 2 + 1)]
+
         def widen_pair(q):
-            half = rooms[q // 2 % 4][:, 2 * D * (q % 2) : 2 * D * (q % 2 + 1)]
-            nc.scalar.copy(out=half, in_=raw_tiles(2 * q, 2 * q + 2))
+            nc.scalar.copy(out=widened(q), in_=raw_tiles(2 * q, 2 * q + 2))
 
         def widen_group(j):
-            nc.gpsimd.tensor_copy(out=rooms[j % 4][:], in_=raw_tiles(4 * j, 4 * j + 4))
+            nc.gpsimd.tensor_copy(out=x_rooms[j % 3][:], in_=raw_tiles(4 * j, 4 * j + 4))
 
         def x_transpose(q):
-            half = rooms[q // 2 % 4][:, 2 * D * (q % 2) : 2 * D * (q % 2 + 1)]
-            words = half.bitcast(F32)
-            xt = psum.tile([P, 2, 2, P], F32, name="xt", tag="p2", bufs=2)
+            words = widened(q).bitcast(F32)
+            xt = bank(q % 2, [2, 2, P], "xt")
             for s in range(2):
                 for u in range(2):
                     nc.tensor.transpose(
@@ -169,14 +143,12 @@ def tile_productkeysoftmemoryplus_t_kernel(
                     )
             state["xt", q] = xt
 
-        def scaled(q0, q1):
-            room = rooms[(q0 // 2 - 1) % 4]
-            return room[:, 2 * D * (q0 % 2) : 2 * D * (q0 % 2 + q1 - q0)]
-
         def x_scale_out(q):
+            room = x_rooms[(q // 2 - 1) % 3]
+            scaled = room[:, 2 * D * (q % 2) : 2 * D * (q % 2 + 1)]
             pairs = state["xt", q][:].rearrange("p u s k -> p (u s k)").bitcast(BF16)
             nc.vector.tensor_tensor(
-                out=scaled(q, q + 1).rearrange("p (k u e) -> p k u e", u=2, e=2),
+                out=scaled.rearrange("p (k u e) -> p k u e", u=2, e=2),
                 in0=pairs.rearrange("p (u k e) -> p k u e", u=2, e=2),
                 in1=scale_col[:]
                 .rearrange("p (u e) -> p u e", e=2)
@@ -187,8 +159,9 @@ def tile_productkeysoftmemoryplus_t_kernel(
 
         def x_quant(q0, q1):
             cols = slice(256 * q0, 256 * q1)
-            values_of = scaled(q0, q1).rearrange("p (c j) -> p c j", j=4)
-            quantise(x_codes[:, cols], x_scales[:, cols], values_of)
+            room = x_rooms[(q0 // 2 - 1) % 3]
+            scaled = room[:, 2 * D * (q0 % 2) : 2 * D * (q0 % 2 + q1 - q0)]
+            quantise(x_codes[:, cols], x_scales[:, cols], scaled)
 
         def mx_x(dst, n, codes, scales):
             cols = slice(P * n, P * (n + 1))
@@ -202,220 +175,263 @@ def tile_productkeysoftmemoryplus_t_kernel(
                 stop=True,
             )
 
-        def gate_matmul(n):
-            if n % 5 < 3:
-                a_ps = psum.tile([P, D], F32, name="a_ps", tag="ub", bufs=3)
-            else:
-                a_ps = psum.tile([P, D], F32, name="a_ps", tag="sc", bufs=2)
-            mx_x(a_ps[:], n, wg_codes, wg_scales)
-            state["a", n] = a_ps
+        def scores(q):
+            sc = bank(2 + (q + 4) % 5, [2, C], "sc_ps")
+            for s in range(2):
+                mx_x(sc[:, s, :], 2 * q + s, wk_codes, wk_scales)
+            state["sc", q] = sc
 
-        def gate_silu(n):
-            nc.scalar.activation(out=gates[n][:], in_=state["a", n][:], func=ACT.Silu)
-
-        def scores(tiles):
-            sc = psum.tile([P, len(tiles), C], F32, name="sc_ps", tag="sc", bufs=2)
-            for k, n in enumerate(tiles):
-                mx_x(sc[:, k, :], n, wk_codes, wk_scales)
-                state["sc", n] = sc[:, k, :]
-            state["sc_bank", tiles[0]] = sc
-
-        def maxima(tiles):
-            nm = work.tile([P, len(tiles), 2 * H], F32, name="nm", bufs=3)
+        def maxima(q):
+            nm = work.tile([P, 2, 2 * H], F32, name="nm", bufs=5)
             nc.vector.tensor_reduce(
                 out=nm[:].rearrange("p s c -> p (s c)"),
-                in_=state["sc_bank", tiles[0]][:].rearrange("p s (c k) -> p (s c) k", k=N),
+                in_=state["sc", q][:].rearrange("p s (c k) -> p (s c) k", k=N),
                 axis=AX.X,
                 op=ALU.max,
                 negate=True,
             )
-            for k, n in enumerate(tiles):
-                state["nm", n] = nm[:, k, :]
+            state["nm", q] = nm
+
+        p1 = [keep.tile([P, 4, H, N], F32, name="p1_%d" % j) for j in range(NGROUP)]
+        base = [keep.tile([P, 4, N], F32, name="base%d" % j) for j in range(NGROUP)]
+        ratio = [keep.tile([P, 4, N], F32, name="ratio%d" % j) for j in range(NGROUP)]
+        e2_cd = [keep.tile([P, 4, 2, N], F32, name="e2_cd%d" % j) for j in range(NGROUP)]
+
+        rooms = [keep.tile([P, 2 * SLOTS], F32, name="room%d" % r) for r in range(3)]
+
+        first_b = keep.tile([P, 2, N], F32, name="first_b")
+
+        def group_tiles(j):
+            state["low", j] = work.tile([P, 4, N], F32, name="low", bufs=3)
+            state["gap", j] = work.tile([P, 4, N], F32, name="gap", bufs=3)
+            if j == 2:
+                z = rooms[2][:, 0 : 8 * H].rearrange("p (s h a) -> p s h a", h=H, a=2)
+            else:
+                tile = work.tile([P, 4, H, 2], F32, name="z", bufs=NGROUP)
+                z = tile[:]
+            state["z", j] = z
+
+        def floor_base(n):
+            j, s = divmod(n, 4)
+            if s == 0:
+                group_tiles(j)
+            c = H + BASE
+            nc.vector.tensor_scalar(
+                out=state["low", j][:, s, :],
+                in0=state["sc", n // 2][:, n % 2, N * c : N * (c + 1)],
+                scalar1=state["nm", n // 2][:, n % 2, c : c + 1],
+                scalar2=FLOOR,
+                op0=ALU.add,
+                op1=ALU.max,
+            )
+
+        def gap_to_base(n):
+            j, s = divmod(n, 4)
+            c = H + RATIO
+            nc.vector.scalar_tensor_tensor(
+                out=state["gap", j][:, s, :],
+                in0=state["sc", n // 2][:, n % 2, N * c : N * (c + 1)],
+                scalar=state["nm", n // 2][:, n % 2, c : c + 1],
+                in1=state["low", j][:, s, :],
+                op0=ALU.add,
+                op1=ALU.subtract,
+            )
+
+        def e2_of(n, h):
+            j, s = divmod(n, 4)
+            if h == BASE:
+                return base[j][:, s, :]
+            if h == RATIO:
+                return first_b[:, s, :] if n < 2 else ratio[j][:, s, :]
+            return e2_cd[j][:, s, h - HEAD_C, :]
 
         def exps(n):
-            q, s = divmod(n, 2)
-            if s == 0:
-                e = work.tile([P, 2, 2, H, N], F32, name="e", bufs=EARLY // 2 + 1)
-                z = work.tile([P, 2, H, 2], F32, name="z", bufs=EARLY // 2 + 1)
-                state["e", q], state["z", q] = e, z
-            e, z = state["e", q], state["z", q]
-            sc, nm = state["sc", n], state["nm", n]
-            for half in range(2):
-                for h in range(H):
-                    c = H * half + h
+            j, s = divmod(n, 4)
+            sc, nm, z = state["sc", n // 2], state["nm", n // 2], state["z", j]
+            for c in range(2 * H):
+                half, h = divmod(c, H)
+                total = z[:, s, h, half : half + 1]
+                if c == H + BASE:
                     nc.scalar.activation(
-                        out=e[:, s, half, h, :],
-                        in_=sc[:, N * c : N * (c + 1)],
+                        out=e2_of(n, h), in_=state["low", j][:, s, :], func=ACT.Exp, accum_out=total
+                    )
+                else:
+                    nc.scalar.activation(
+                        out=e2_of(n, h) if half else p1[j][:, s, h, :],
+                        in_=sc[:, n % 2, N * c : N * (c + 1)],
                         func=ACT.Exp,
-                        bias=nm[:, c : c + 1],
-                        accum_out=z[:, s, h, half : half + 1],
+                        bias=nm[:, n % 2, c : c + 1],
+                        accum_out=total,
                     )
 
-        def denominators(q):
-            zz = work.tile([P, 2 * H], F32, name="zz", bufs=3)
+        def ratios(j):
+            nc.scalar.activation(out=ratio[j][:], in_=state["gap", j][:], func=ACT.Exp)
+
+        def denominators(j):
+            zz = work.tile([P, 4 * H], F32, name="zz", bufs=2)
             nc.vector.tensor_reduce(
                 out=zz[:],
-                in_=state["z", q][:].rearrange("p s h a -> p (s h) a"),
+                in_=state["z", j].rearrange("p s h a -> p (s h) a"),
                 axis=AX.X,
                 op=ALU.mult,
             )
-            state["zz", q] = zz
+            state["zz", j] = zz
 
-        def reciprocals(q, tiles=(0, 1)):
-            if tiles[0] == 0:
-                rz = work.tile([P, 2 * H], F32, name="rz", bufs=3)
-                state["rz", q] = rz
-            cols = slice(H * tiles[0], H * (tiles[-1] + 1))
-            nc.vector.reciprocal(out=state["rz", q][:, cols], in_=state["zz", q][:, cols])
+        def reciprocals(j):
+            rz = work.tile([P, 4 * H], F32, name="rz", bufs=NGROUP)
+            nc.vector.reciprocal(out=rz[:], in_=state["zz", j][:])
+            state["rz", j] = rz
 
-        def normalise(n):
-            q, s = divmod(n, 2)
-            p1 = work.tile([P, H, N], F32, name="p1", bufs=3)
-            for h in range(H):
+        def normalise(j):
+            for k in range(4 * H):
+                s, h = divmod(k, H)
                 nc.scalar.activation(
-                    out=p1[:, h, :],
-                    in_=state["e", q][:, s, 0, h, :],
+                    out=p1[j][:, s, h, :],
+                    in_=p1[j][:, s, h, :],
                     func=ACT.Copy,
-                    scale=state["rz", q][:, H * s + h : H * s + h + 1],
+                    scale=state["rz", j][:, k : k + 1],
                 )
-            state["p1", n] = p1
 
-        def e2_to_psum(q, keys, tag="p2", bufs=2):
-            e2 = psum.tile([P, 2, keys], F32, name="e2_ps", tag=tag, bufs=bufs)
-            second = state["e", q][:, :, 1, :, :].rearrange("p s h k -> p s (h k)")
+        sums_of_two = [keep.tile([P, 2 * SLOTS], F32, name="two%d" % r) for r in range(2)]
+
+        def p1_of(n, h):
+            return p1[n // 4][:, n % 4, h, :]
+
+        def terms(n, g, t):
+            return state.setdefault(("terms", n, g, t), [])
+
+        def e2_to_psum(q):
+            e2 = bank(7, [2, 2, N], "e2_ps")
+            second = e2_cd[q // 2][:, 2 * (q % 2) : 2 * (q % 2) + 2, :, :]
             nc.tensor.matmul(
-                e2[:], lhsT=ident[:], rhs=second[:, :, 0:keys], start=True, stop=True
+                e2[:].rearrange("p s h k -> p (s h k)"),
+                lhsT=ident[:],
+                rhs=second.rearrange("p s h k -> p (s h k)"),
+                start=True,
+                stop=True,
             )
-            for s in range(2):
-                state["e2_ps", 2 * q + s] = e2[:, s, :]
+            state["e2_ps", q] = e2
 
-        def e2_of(n, h):
-            return state["e", n // 2][:, n % 2, 1, h, :]
-
-        def product(eng, dst, p1, e2):
-            nt, ni = dst.shape[1], p1.shape[1]
-            eng.tensor_tensor(
-                out=dst.rearrange("p t (i m) -> p t i m", m=8),
-                in0=p1.unsqueeze(1).unsqueeze(3).broadcast_to([P, nt, ni, 8]),
-                in1=e2.rearrange("p (t m) -> p t m", m=8).unsqueeze(2).broadcast_to([P, nt, ni, 8]),
-                op=ALU.mult,
-            )
-
-        def head_product(eng, n, h, e2, room=None):
-            if room is None:
-                tile = work.tile([P, 4, 2 * P], F32, name="pr%d" % h, bufs=3)
-                pr = tile[:]
-            else:
-                pr = room[:].bitcast(F32).rearrange("p (t c) -> p t c", t=4)
-            product(eng, pr, state["p1", n][:, h, :], e2)
-            for g in range(2):
-                for t in range(4):
-                    state["pr", n, h, g, t] = pr[:, t, P * g : P * (g + 1)]
-
-        def cut_product(eng, n, dst, t0, e2):
-            h, g = CUT_HALF
-            product(eng, dst, state["p1", n][:, h, 16 * g : 16 * (g + 1)], e2)
-            for t in range(dst.shape[1]):
-                state["pr", n, h, g, t0 + t] = dst[:, t, :]
-
-        def v_planes(n):
-            if n == 2:
-                return 4
-            return V_PLANES - n % 2 + (n >= NO_MAXIMA)
-
-        def vector_products(n):
-            e2 = state["e2_ps", n]
-            head_product(nc.vector, n, V_HEAD, e2[:, 0:N])
-            planes = v_planes(n)
-            pr = work.tile([P, planes, P], F32, name="pr_cut_v", bufs=3)
-            first = N * CUT_HALF[0]
-            cut_product(nc.vector, n, pr[:], 0, e2[:, first : first + 8 * planes])
-
-        def gpsimd_cut(n):
-            planes = 4 - v_planes(n)
-            room = gates[n - 3][:, 0 : planes * P]
-            cut_product(
-                nc.gpsimd,
-                n,
-                room.rearrange("p (t c) -> p t c", c=P),
-                4 - planes,
-                e2_of(n, CUT_HALF[0])[:, N - 8 * planes : N],
-            )
-
-        def half_product(eng, n, h, g, room=None):
+        def product(eng, dst, n, h, t0, t1, g0, g1):
             if eng is nc.vector:
-                e2 = state["e2_ps", n][:, N * h : N * (h + 1)]
+                e2 = state["e2_ps", n // 2][:, n % 2, h - HEAD_C, :]
             else:
                 e2 = e2_of(n, h)
-            if room is None:
-                pr = half_tile(n, h, g)[:]
-            else:
-                pr = room[:, 0 : 2 * D].bitcast(F32).rearrange("p (t c) -> p t c", t=4)
-                for t in range(4):
-                    state["pr", n, h, g, t] = pr[:, t, :]
-            product(eng, pr, state["p1", n][:, h, 16 * g : 16 * (g + 1)], e2)
+            nt, ni = t1 - t0, 16 * (g1 - g0)
+            planes = dst.rearrange("p (t c) -> p t c", t=nt)
+            eng.tensor_tensor(
+                out=planes.rearrange("p t (i m) -> p t i m", m=8),
+                in0=p1_of(n, h)[:, 16 * g0 : 16 * g1]
+                .unsqueeze(1)
+                .unsqueeze(3)
+                .broadcast_to([P, nt, ni, 8]),
+                in1=e2[:, 8 * t0 : 8 * t1]
+                .rearrange("p (t m) -> p t m", m=8)
+                .unsqueeze(2)
+                .broadcast_to([P, nt, ni, 8]),
+                op=ALU.mult,
+            )
+            for t in range(t0, t1):
+                for g in range(g0, g1):
+                    terms(n, g, t).append(planes[:, t - t0, P * (g - g0) : P * (g - g0 + 1)])
 
-        def half_tile(n, h, g):
-            pr = work.tile([P, 4, P], F32, name="pr%d_%d" % (h, g), bufs=3)
-            for t in range(4):
-                state["pr", n, h, g, t] = pr[:, t, :]
-            return pr
+        def new_product(eng, name, bufs, n, h, t0, t1, g0, g1):
+            pr = work.tile([P, P * (t1 - t0) * (g1 - g0)], F32, name=name, bufs=bufs)
+            product(eng, pr[:], n, h, t0, t1, g0, g1)
 
-        def scalar_product(n, k):
-            h, g = S_HALVES[k]
-            pr = half_tile(n, h, g)
+        def scalar_half(n, h, g):
+            pr = work.tile([P, 4, P], F32, name="pr_s", bufs=5)
             for i in range(16):
                 nc.scalar.activation(
                     out=pr[:, :, 8 * i : 8 * (i + 1)],
                     in_=e2_of(n, h).rearrange("p (t m) -> p t m", t=4),
                     func=ACT.Copy,
-                    scale=state["p1", n][:, h, 16 * g + i : 16 * g + i + 1],
+                    scale=p1_of(n, h)[:, 16 * g + i : 16 * g + i + 1],
+                )
+            for t in range(4):
+                terms(n, g, t).append(pr[:, t, :])
+
+        def two_heads(n, i0=0, i1=N):
+            two = sums_of_two[n // 2 % 2][:, SLOTS * (n % 2) : SLOTS * (n % 2 + 1)]
+            planes = two.rearrange("p (t c) -> p t c", t=4)
+            for i in range(i0, i1):
+                nc.scalar.activation(
+                    out=planes[:, :, 8 * i : 8 * (i + 1)],
+                    in_=ratio[n // 4][:, n % 4, :].rearrange("p (t m) -> p t m", t=4),
+                    func=ACT.Identity,
+                    scale=p1_of(n, RATIO)[:, i : i + 1],
+                    bias=p1_of(n, BASE)[:, i : i + 1],
                 )
 
-        def sum_heads(n, g):
-            ub = psum.tile([P, 4, P], F32, name="ub_ps", tag="ub", bufs=3)
-            for h in range(H):
-                for t in range(4):
-                    nc.tensor.matmul(
-                        ub[:, t, :],
-                        lhsT=state["pr", n, h, g, t],
-                        rhs=ident[:],
-                        start=(h == 0 and t == 0),
-                        stop=(h == H - 1 and t == 3),
-                        is_transpose=True,
-                    )
-            state["ub", n, g] = ub
+        def times_base(n0, n1):
+            q, rows = n0 // 2, 4 * (n1 - n0)
+            cols = slice(SLOTS * (n0 % 2), SLOTS * (n0 % 2 + n1 - n0))
+            room = rooms[q % 3][:, cols]
+            factor = base[n0 // 4][:, n0 % 4 : n0 % 4 + n1 - n0, :]
+            nc.gpsimd.tensor_tensor(
+                out=room.rearrange("p (r i m) -> p r i m", r=rows, m=8),
+                in0=sums_of_two[q % 2][:, cols].rearrange("p (r i m) -> p r i m", r=rows, m=8),
+                in1=factor.rearrange("p s (t m) -> p (s t) m", m=8)
+                .unsqueeze(2)
+                .broadcast_to([P, rows, N, 8]),
+                op=ALU.mult,
+            )
+            for r in range(rows):
+                for g in range(2):
+                    first = 2 * P * r + P * g
+                    state["last", n0 + r // 4, g, r % 4] = room[:, first : first + P]
 
-        def gain(n, g):
-            if g == 0:
-                u = work.tile([P, 2, P, 4], BF16, name="u", align_bytes=64)
-                state["u", n] = u
+        def turn(k):
+            n, g = divmod(k, 2)
+            ub = bank(k % 3, [4, P], "ub_ps")
+            todo = []
+            for t in range(4):
+                if ("last", n, g, t) in state:
+                    terms(n, g, t).append(state["last", n, g, t])
+            for r in range(len(terms(n, g, 0))):
+                for t in range(4):
+                    todo.append((t, terms(n, g, t)[r]))
+            for i, (t, term) in enumerate(todo):
+                nc.tensor.matmul(
+                    ub[:, t, :],
+                    lhsT=term,
+                    rhs=ident[:],
+                    start=(i == 0),
+                    stop=(i == len(todo) - 1),
+                    is_transpose=True,
+                )
+            state["ub", k] = ub
+
+        def gain(k):
+            if k % 4 == 0:
+                u = work.tile([P, 4, P, 4], BF16, name="u", align_bytes=64)
+                state["u", k // 4] = u
             nc.vector.tensor_tensor(
-                out=state["u", n][:, g, :, :],
-                in0=state["ub", n, g][:].rearrange("p t k -> p k t"),
-                in1=gain_sb[:, g, :].unsqueeze(1).broadcast_to([P, P, 4]),
+                out=state["u", k // 4][:, k % 4, :, :],
+                in0=state["ub", k][:].rearrange("p t k -> p k t"),
+                in1=gain_sb[:, k % 2, :].unsqueeze(1).broadcast_to([P, P, 4]),
                 op=ALU.mult,
             )
 
-        def u_quant(n, passes=(0, 1)):
-            if passes[0] == 0:
-                uc = work.tile([P, 2 * P], U32, name="uc", align_bytes=64)
-                us = work.tile([P, 2 * P], U8, name="us", align_bytes=64)
-                state["uc", n] = (uc, us)
-            uc, us = state["uc", n]
-            cols = slice(P * passes[0], P * (passes[-1] + 1))
-            u = state["u", n][:, passes[0] : passes[-1] + 1, :, :]
-            quantise(uc[:, cols], us[:, cols], u.rearrange("p g k t -> p (g k) t"))
+        def u_quant(q, k0=0, k1=4):
+            if k0 == 0:
+                uc = work.tile([P, 4 * P], U32, name="uc", align_bytes=64)
+                us = work.tile([P, 4 * P], U8, name="us", align_bytes=64)
+                state["uc", q] = (uc, us)
+            uc, us = state["uc", q]
+            cols = slice(P * k0, P * k1)
+            u = state["u", q][:, k0:k1, :, :].rearrange("p g k t -> p (g k t)")
+            quantise(uc[:, cols], us[:, cols], u)
 
         def memory(n, passes=(0, 1)):
             if passes[0] == 0:
-                mem = psum.tile([P, D], F32, name="mem", tag="mem", bufs=1)
-                state["mem", n] = mem
-            uc, us = state["uc", n]
+                state["mem", n] = bank(3 + n % 2, [D], "mem")
+            mem = state["mem", n]
+            uc, us = state["uc", n // 2]
             for g in passes:
-                cols = slice(P * g, P * (g + 1))
+                cols = slice(P * (2 * (n % 2) + g), P * (2 * (n % 2) + g + 1))
                 nc.tensor.matmul_mx(
-                    out=state["mem", n][:],
+                    out=mem[:],
                     lhsT=uc[:, cols].bitcast(FP8X4),
                     lhsT_scale=us[:, cols],
                     rhs=v_codes[:, g, :].bitcast(FP8X4),
@@ -424,181 +440,250 @@ def tile_productkeysoftmemoryplus_t_kernel(
                     stop=(g == 1),
                 )
 
+        def gate_matmul(n):
+            a_ps = bank(5 + n % 2, [D], "a_ps")
+            mx_x(a_ps[:], n, wg_codes, wg_scales)
+            state["a", n] = a_ps
+
+        def gate_of(n):
+            return rooms[n // 2 % 3][:, D * (n % 2) : D * (n % 2 + 1)]
+
+        def gate_silu(n):
+            nc.scalar.activation(out=gate_of(n), in_=state["a", n][:], func=ACT.Silu)
+
         def final(n):
-            o = work.tile([P, D], F32, name="o", bufs=4)
-            nc.vector.tensor_tensor(
-                out=o[:], in0=state["mem", n][:], in1=gates[n][:], op=ALU.mult
-            )
+            o = work.tile([P, D], F32, name="o", bufs=3)
+            nc.vector.tensor_tensor(out=o[:], in0=state["mem", n][:], in1=gate_of(n), op=ALU.mult)
             nc.sync.dma_start(out=out_view[:, n, :], in_=o[:])
 
-        def has(n):
-            return 0 <= n < NT
 
-        def step(s):
-            odd = s % 2 == 1
-            if s >= 2:
-                memory(s - 2)
-            if EARLY < s + 6 < NT:
-                scores([s + 6])
-            if odd and has(s + 3) and s > 1:
-                keys = N + 8 * max(v_planes(s + 3), v_planes(s + 4))
-                e2_to_psum((s + 3) // 2, keys)
-            sum_heads(s, 0)
-            if s == 1:
-                scores([EARLY])
-            sum_heads(s, 1)
-            head_product(nc.gpsimd, s + 1, G_HEAD, e2_of(s + 1, G_HEAD))
-            if s > 1:
-                vector_products(s + 1)
-            gain(s - 1, 1)
-            if s >= 2:
-                final(s - 2)
-                gpsimd_cut(s + 1)
+        last = NT - 1
+
+        def scalar_halves(n):
+            if n < 5:
+                return []
+            if n >= last - 1:
+                return [(HEAD_D, 0), (HEAD_D, 1)]
+            return [(HEAD_D, 0)] if n % 4 != 3 else []
+
+        def gpsimd_planes(n):
+            if n % 2 == 0:
+                return 0
+            return 3 if (n % 4 == 3 or n < 8) and n != last else 2
+
+        def vector_products(n):
+            if gpsimd_planes(n) < 4:
+                new_product(nc.vector, "pr_c", 3, n, HEAD_C, 0, 4 - gpsimd_planes(n), 0, 2)
+            if len(scalar_halves(n)) < 2:
+                new_product(nc.vector, "pr_d", 3, n, HEAD_D, 0, 4, len(scalar_halves(n)), 2)
+
+        def gpsimd_product(n):
+            new_product(nc.gpsimd, "pr_g", 2, n, HEAD_C, 4 - gpsimd_planes(n), 4, 0, 2)
+
+        def cycle(c):
+            if c > 0:
+                e2_to_psum(c + 1)
+            if c > 1:
+                gate_matmul(2 * c - 2)
+                gate_matmul(2 * c - 1)
+            if c > 0:
+                memory(2 * c - 2)
+                memory(2 * c - 1)
+            gain(4 * c)
+            gain(4 * c + 1)
+            if c > 0:
+                times_base(2 * c + 2, 2 * c + 4)
+                gpsimd_product(2 * c + 3)
+            if c % 2 == 1 and (c + 3) // 2 < NGROUP:
+                reciprocals((c + 3) // 2)
+            for h, g in scalar_halves(2 * c + 2):
+                scalar_half(2 * c + 2, h, g)
+            if c > 1:
+                gate_silu(2 * c - 2)
+                gate_silu(2 * c - 1)
+            if c + 2 < NPAIR:
+                two_heads(2 * c + 4, 9 * EARLY_ROWS - 2 * N if c == 0 else 0)
+                two_heads(2 * c + 5)
+            for h, g in scalar_halves(2 * c + 3):
+                scalar_half(2 * c + 3, h, g)
+            if c % 2 == 1 and (c + 3) // 2 < NGROUP:
+                normalise((c + 3) // 2)
+            if c > 0:
+                vector_products(2 * c + 2)
+                vector_products(2 * c + 3)
             else:
-                reciprocals(1, (1,))
-            u_quant(s - 1)
-            if odd and has(s + 3):
-                denominators((s + 3) // 2)
-            gain(s, 0)
-            if EARLY <= s + 6 < NT:
-                maxima([s + 6])
-            if odd and has(s + 3):
-                reciprocals((s + 3) // 2)
-            scalar_product(s + 1, 0)
-            if has(s + 2):
-                normalise(s + 2)
-            scalar_product(s + 1, 1)
-            if EARLY <= s + 5 < NT:
-                exps(s + 5)
-            scalar_product(s + 1, 2)
+                new_product(nc.vector, "pr_c", 3, 2, HEAD_C, 0, 2, 0, 2)
+                new_product(nc.vector, "pr_d", 3, 2, HEAD_D, 0, 4, 0, 2)
+                new_product(nc.vector, "pr_d", 3, 3, HEAD_D, 0, 4, 0, 2)
+            turn(4 * c + 2)
+            turn(4 * c + 3)
+            if c == 0:
+                gate_matmul(0)
+                gate_matmul(1)
+                gate_silu(0)
+                gate_silu(1)
+            if c > 0:
+                final(2 * c - 2)
+            gain(4 * c + 2)
+            gain(4 * c + 3)
+            if c % 2 == 0 and (c + 4) // 2 < NGROUP:
+                denominators((c + 4) // 2)
+            if c > 0:
+                final(2 * c - 1)
+            u_quant(c)
+            turn(4 * c + 4)
+            turn(4 * c + 5)
 
-        def pair(q):
-            return [2 * q, 2 * q + 1]
+        def floors(q):
+            floor_base(2 * q)
+            floor_base(2 * q + 1)
 
-        def softmax_start(q):
-            maxima(pair(q))
+        def softmax_pair(q):
+            gap_to_base(2 * q)
+            gap_to_base(2 * q + 1)
             exps(2 * q)
             exps(2 * q + 1)
 
-        counts = {"matmul": 0, "silu": 0}
+        def early_half(k):
+            h, t0 = k // 2, 2 * (k % 2)
+            new_product(nc.gpsimd, "pr_early", 4, 0, h, t0, t0 + 2, 0, 2)
 
-        def gates_up_to(quantised, more):
-            for k in range(more + 1):
-                if k > 0 and counts["silu"] < counts["matmul"]:
-                    gate_silu(counts["silu"])
-                    counts["silu"] = counts["silu"] + 1
-                while counts["matmul"] < min(counts["silu"] + GATE_LEAD, quantised):
-                    gate_matmul(counts["matmul"])
-                    counts["matmul"] = counts["matmul"] + 1
+        def early_rows(k):
+            first = EARLY_ROWS * k
+            for i in range(first, first + EARLY_ROWS):
+                two_heads(2 + i // N, i % N, i % N + 1)
 
         widen_pair(0)
         widen_pair(1)
         wk_copy()
         x_transpose(0)
         x_transpose(1)
-        widen_group(1)
-        wg_copy(0)
-        wg_copy(1)
-        v_copy(0)
-        v_copy(1)
+        widen_pair(2)
+        widen_pair(3)
         x_scale_out(0)
+        quantise(wk_codes[:], wk_scales[:], wk_il)
+        x_quant(0, 1)
+        interleave(nc.gpsimd.tensor_copy, wg_il, wg_raw, 0, 256)
+        scores(0)
         x_scale_out(1)
         x_transpose(2)
         x_transpose(3)
-        wk_quant()
-        x_quant(0, 2)
+        maxima(0)
+        x_quant(1, 2)
+        scores(1)
         widen_group(2)
-        widen_group(3)
-        scores(pair(0))
-        scores(pair(1))
-        x_scale_out(2)
-        softmax_start(0)
-        x_transpose(4)
-        last_group = NPAIR // 2 - 1
-        for j in range(1, last_group + 1):
-            more = FIRST_GATES if j == 3 else GATES_A_ROUND
-            x_scale_out(2 * j + 1)
-            if j == 1:
-                softmax_start(1)
-            if j == 2:
-                denominators(0)
-                softmax_start(2)
-                e2_to_psum(0, 3 * N, "mem", 1)
-                reciprocals(0)
-            if j == 3:
-                denominators(1)
-            if j == 4:
-                reciprocals(1, (0,))
-            if j < last_group:
-                x_transpose(2 * j + 3)
-            if j > 2:
-                gates_up_to(4 * j, more // 2)
-            if j < last_group:
-                x_scale_out(2 * j + 2)
-            if j == 2:
-                softmax_start(3)
-                normalise(0)
-                normalise(1)
-            if j + 1 < last_group:
-                x_transpose(2 * j + 4)
-            if j > 2:
-                gates_up_to(4 * j, more - more // 2)
-            if j == 1:
-                v_copy(2)
-            if j == 2:
-                wg_quant()
-            if j == 4:
-                head_product(nc.vector, 0, V_HEAD, state["e2_ps", 0][:, 0:N])
-            if j >= 5:
-                half_product(nc.vector, 0, *S_HALVES[j - 5])
-            if 3 <= j < 7:
-                v_quant(j - 3)
-            if j == last_group:
-                normalise(2)
-                e2_to_psum(1, 2 * N)
-            x_quant(2 * j, 2 * j + 2)
-            if j == 1:
-                scores(pair(2))
-                scores(pair(3))
-            if j == 2:
-                v_copy(3)
-                gates_up_to(4 * j, 0)
-            if j + 3 <= last_group:
-                widen_group(j + 3)
-            elif j == last_group - 1:
-                half_product(nc.gpsimd, 0, 1, 1, rooms[(j + 3) % 4])
+        interleave(nc.scalar.copy, wg_il, wg_raw, 256, 512)
+        floors(0)
+        for j in range(1, NGROUP):
+            if j < NGROUP:
+                x_scale_out(2 * j)
             else:
-                n = (j + 2 - last_group) // 2
-                head_product(nc.gpsimd, n, G_HEAD, e2_of(n, G_HEAD), rooms[(j + 3) % 4])
-
-        gates_up_to(NT, NT - counts["silu"])
-        sum_heads(0, 0)
-        e2_to_psum(2, N + 8 * V_PLANES)
-        sum_heads(0, 1)
-        head_product(nc.vector, 1, V_HEAD, state["e2_ps", 1][:, 0:N])
-        half_product(nc.vector, 1, 1, 0)
-        scalar_product(1, 1)
-        scalar_product(1, 2)
-        vector_products(2)
-        half_product(nc.vector, 1, 1, 1)
-        gain(0, 0)
-
-        for s in range(1, NT - 1):
-            step(s)
-
-        last = NT - 1
+                new_product(nc.vector, "pr_c", 3, 0, HEAD_C, 0, 4, 0, 2)
+            softmax_pair(max(0, 2 * j - 3))
+            if j == 1:
+                interleave(nc.scalar.copy, v_il[0], v_raw[0], 0, 256)
+            if j == 2:
+                ratios(0)
+                interleave(nc.scalar.copy, v_il[0], v_raw[0], 256, 512)
+            if j > 2:
+                ratios(j - 2)
+            if 3 <= j < NGROUP:
+                early_rows(2 * j - 6)
+            if j + 1 < NGROUP:
+                x_transpose(2 * j + 2)
+            maxima(max(1, 2 * j - 2))
+            if j < NGROUP:
+                x_scale_out(2 * j + 1)
+            else:
+                new_product(nc.vector, "pr_d", 3, 0, HEAD_D, 0, 4, 0, 2)
+                turn(0)
+                turn(1)
+            if j + 1 < NGROUP:
+                x_transpose(2 * j + 3)
+            floors(max(1, 2 * j - 2))
+            if j in (2, 3):
+                denominators(j - 2)
+            if j > 1:
+                maxima(2 * j - 1)
+                if j in (2, 3):
+                    reciprocals(j - 2)
+                softmax_pair(2 * j - 2)
+            if j == 2:
+                normalise(0)
+            if j == 3:
+                interleave(nc.scalar.copy, v_il[1], v_raw[1], 0, 256)
+            if j == 4:
+                normalise(1)
+            if 4 <= j < NGROUP:
+                early_rows(2 * j - 7)
+            if j == 2:
+                quantise(wg_codes[:], wg_scales[:], wg_il[:])
+            if j in (3, 4):
+                quantise(v_codes[:, j - 3, :], v_scales[:, j - 3, :], v_il[j - 3][:])
+            if j == NGROUP - 1:
+                e2_to_psum(0)
+            if j == NGROUP:
+                new_product(nc.vector, "pr_c", 3, 1, HEAD_C, 0, 4, 0, 2)
+            if j < NGROUP:
+                x_quant(2 * j, 2 * j + 2)
+                scores(2 * j)
+                scores(2 * j + 1)
+            if j + 2 < NGROUP:
+                widen_group(j + 2)
+            if j == 1:
+                interleave(nc.gpsimd.tensor_copy, v_il[1], v_raw[1], 256, 512)
+            if j in (NGROUP - 2, NGROUP - 1):
+                h = j + 2 - NGROUP
+                product(nc.gpsimd, x_rooms[(j - 1) % 3][:].bitcast(F32), 1, h, 0, 4, 0, 2)
+            if 2 <= j <= 5:
+                early_half(j - 2)
+            if j > 1:
+                floors(2 * j - 1)
+        new_product(nc.vector, "pr_c", 3, 0, HEAD_C, 0, 4, 0, 2)
+        softmax_pair(NPAIR - 3)
+        ratios(NGROUP - 2)
+        maxima(NPAIR - 2)
+        maxima(NPAIR - 1)
+        floors(NPAIR - 2)
+        floors(NPAIR - 1)
+        softmax_pair(NPAIR - 2)
+        softmax_pair(NPAIR - 1)
+        ratios(NGROUP - 1)
+        new_product(nc.vector, "pr_d", 3, 0, HEAD_D, 0, 4, 0, 2)
+        turn(0)
+        turn(1)
+        new_product(nc.vector, "pr_c", 3, 1, HEAD_C, 0, 4, 0, 2)
+        times_base(2, 4)
+        new_product(nc.gpsimd, "pr_g", 2, 2, HEAD_C, 2, 4, 0, 2)
+        new_product(nc.gpsimd, "pr_g", 2, 3, HEAD_C, 0, 4, 0, 2)
+        new_product(nc.vector, "pr_d", 3, 1, HEAD_D, 0, 4, 0, 2)
+        e2_to_psum(1)
+        for c in range(NPAIR - 1):
+            cycle(c)
+        c = NPAIR - 1
+        gate_matmul(last - 3)
+        gate_matmul(last - 2)
+        memory(last - 3)
         memory(last - 2)
-        sum_heads(last, 0)
-        gain(last - 1, 1)
-        final(last - 2)
-        u_quant(last - 1)
+        gain(4 * c)
+        gain(4 * c + 1)
+        gate_silu(last - 3)
+        gate_silu(last - 2)
+        turn(4 * c + 2)
+        turn(4 * c + 3)
+        final(last - 3)
+        u_quant(c, 0, 2)
+        gate_matmul(last - 1)
+        gate_matmul(last)
+        gate_silu(last - 1)
+        gate_silu(last)
         memory(last - 1)
-        sum_heads(last, 1)
-        gain(last, 0)
-        final(last - 1)
-        u_quant(last, (0,))
+        gain(4 * c + 2)
+        final(last - 2)
+        gain(4 * c + 3)
+        u_quant(c, 2, 3)
         memory(last, (0,))
-        gain(last, 1)
-        u_quant(last, (1,))
+        final(last - 1)
+        u_quant(c, 3, 4)
         memory(last, (1,))
         final(last)

@@ -26,6 +26,7 @@ FLOPS = 2 * T * D * C + 2 * T * SLOTS * D + 2 * T * D * D
 BASE, RATIO, HEAD_C, HEAD_D = 0, 1, 2, 3
 FLOOR = -80.0
 EARLY_ROWS = 10
+MEM_BANKS = {NT - 2: 7, NT - 1: 1}
 
 X_CHUNKS = [(0, 2), (2, 4), (4, 8), (8, 16), (16, 24), (24, 32)]
 
@@ -130,6 +131,10 @@ def tile_productkeysoftmemoryplus_t_kernel(
         def widen_pair(q):
             nc.scalar.copy(out=widened(q), in_=raw_tiles(2 * q, 2 * q + 2))
 
+        def widen_first_pair():
+            nc.vector.tensor_copy(out=widened(0)[:, 0:D], in_=raw_tiles(0, 1))
+            nc.scalar.copy(out=widened(0)[:, D:], in_=raw_tiles(1, 2))
+
         def widen_group(j):
             nc.gpsimd.tensor_copy(out=x_rooms[j % 3][:], in_=raw_tiles(4 * j, 4 * j + 4))
 
@@ -197,19 +202,16 @@ def tile_productkeysoftmemoryplus_t_kernel(
         ratio = [keep.tile([P, 4, N], F32, name="ratio%d" % j) for j in range(NGROUP)]
         e2_cd = [keep.tile([P, 4, 2, N], F32, name="e2_cd%d" % j) for j in range(NGROUP)]
 
-        rooms = [keep.tile([P, 2 * SLOTS], F32, name="room%d" % r) for r in range(3)]
+        rooms = [
+            keep.tile([P, 2 * SLOTS], F32, name="room%d" % r, align_bytes=64) for r in range(3)
+        ]
 
         first_b = keep.tile([P, 2, N], F32, name="first_b")
 
         def group_tiles(j):
             state["low", j] = work.tile([P, 4, N], F32, name="low", bufs=3)
             state["gap", j] = work.tile([P, 4, N], F32, name="gap", bufs=3)
-            if j == 2:
-                z = rooms[2][:, 0 : 8 * H].rearrange("p (s h a) -> p s h a", h=H, a=2)
-            else:
-                tile = work.tile([P, 4, H, 2], F32, name="z", bufs=NGROUP)
-                z = tile[:]
-            state["z", j] = z
+            state["z", j] = work.tile([P, 4, H, 2], F32, name="z", bufs=NGROUP)
 
         def floor_base(n):
             j, s = divmod(n, 4)
@@ -271,7 +273,7 @@ def tile_productkeysoftmemoryplus_t_kernel(
             zz = work.tile([P, 4 * H], F32, name="zz", bufs=2)
             nc.vector.tensor_reduce(
                 out=zz[:],
-                in_=state["z", j].rearrange("p s h a -> p (s h) a"),
+                in_=state["z", j][:].rearrange("p s h a -> p (s h) a"),
                 axis=AX.X,
                 op=ALU.mult,
             )
@@ -403,33 +405,36 @@ def tile_productkeysoftmemoryplus_t_kernel(
             state["ub", k] = ub
 
         def gain(k):
+            n, g = divmod(k, 2)
             if k % 4 == 0:
-                u = work.tile([P, 4, P, 4], BF16, name="u", align_bytes=64)
-                state["u", k // 4] = u
+                state["u", n] = rooms[(n // 2 + 2) % 3][:, SLOTS : SLOTS + D].bitcast(BF16)
+            if k % 4 == 2:
+                u = work.tile([P, SLOTS], BF16, name="u", align_bytes=64)
+                state["u", n] = u[:]
             nc.vector.tensor_tensor(
-                out=state["u", k // 4][:, k % 4, :, :],
+                out=state["u", n][:, D * g : D * (g + 1)].rearrange("p (k t) -> p k t", t=4),
                 in0=state["ub", k][:].rearrange("p t k -> p k t"),
-                in1=gain_sb[:, k % 2, :].unsqueeze(1).broadcast_to([P, P, 4]),
+                in1=gain_sb[:, g, :].unsqueeze(1).broadcast_to([P, P, 4]),
                 op=ALU.mult,
             )
 
-        def u_quant(q, k0=0, k1=4):
-            if k0 == 0:
-                uc = work.tile([P, 4 * P], U32, name="uc", align_bytes=64)
-                us = work.tile([P, 4 * P], U8, name="us", align_bytes=64)
-                state["uc", q] = (uc, us)
-            uc, us = state["uc", q]
-            cols = slice(P * k0, P * k1)
-            u = state["u", q][:, k0:k1, :, :].rearrange("p g k t -> p (g k t)")
+        def u_quant(n, passes=(0, 1)):
+            if passes[0] == 0:
+                uc = work.tile([P, 2 * P], U32, name="uc", bufs=4, align_bytes=64)
+                us = work.tile([P, 2 * P], U8, name="us", bufs=4, align_bytes=64)
+                state["uc", n] = (uc, us)
+            uc, us = state["uc", n]
+            cols = slice(P * passes[0], P * (passes[-1] + 1))
+            u = state["u", n][:, D * passes[0] : D * (passes[-1] + 1)]
             quantise(uc[:, cols], us[:, cols], u)
 
         def memory(n, passes=(0, 1)):
             if passes[0] == 0:
-                state["mem", n] = bank(3 + n % 2, [D], "mem")
+                state["mem", n] = bank(MEM_BANKS.get(n, 3 + n % 2), [D], "mem")
             mem = state["mem", n]
-            uc, us = state["uc", n // 2]
+            uc, us = state["uc", n]
             for g in passes:
-                cols = slice(P * (2 * (n % 2) + g), P * (2 * (n % 2) + g + 1))
+                cols = slice(P * g, P * (g + 1))
                 nc.tensor.matmul_mx(
                     out=mem[:],
                     lhsT=uc[:, cols].bitcast(FP8X4),
@@ -446,13 +451,14 @@ def tile_productkeysoftmemoryplus_t_kernel(
             state["a", n] = a_ps
 
         def gate_of(n):
-            return rooms[n // 2 % 3][:, D * (n % 2) : D * (n % 2 + 1)]
+            room = rooms[n // 2 % 3] if n < NT - 2 else sums_of_two[0]
+            return room[:, D * (n % 2) : D * (n % 2 + 1)]
 
         def gate_silu(n):
             nc.scalar.activation(out=gate_of(n), in_=state["a", n][:], func=ACT.Silu)
 
         def final(n):
-            o = work.tile([P, D], F32, name="o", bufs=3)
+            o = work.tile([P, D], F32, name="o", bufs=5)
             nc.vector.tensor_tensor(out=o[:], in0=state["mem", n][:], in1=gate_of(n), op=ALU.mult)
             nc.sync.dma_start(out=out_view[:, n, :], in_=o[:])
 
@@ -463,22 +469,20 @@ def tile_productkeysoftmemoryplus_t_kernel(
             if n < 5:
                 return []
             if n >= last - 1:
-                return [(HEAD_D, 0), (HEAD_D, 1)]
+                return [(HEAD_D, 0), (HEAD_C, 0), (HEAD_D, 1)]
             return [(HEAD_D, 0)] if n % 4 != 3 else []
 
         def gpsimd_planes(n):
-            if n % 2 == 0:
+            if n % 2 == 0 or n == last:
                 return 0
-            return 3 if (n % 4 == 3 or n < 8) and n != last else 2
+            return 3 if (n % 4 == 3 or n < 8) else 2
 
         def vector_products(n):
-            if gpsimd_planes(n) < 4:
-                new_product(nc.vector, "pr_c", 3, n, HEAD_C, 0, 4 - gpsimd_planes(n), 0, 2)
-            if len(scalar_halves(n)) < 2:
-                new_product(nc.vector, "pr_d", 3, n, HEAD_D, 0, 4, len(scalar_halves(n)), 2)
-
-        def gpsimd_product(n):
-            new_product(nc.gpsimd, "pr_g", 2, n, HEAD_C, 4 - gpsimd_planes(n), 4, 0, 2)
+            if n >= last - 1:
+                new_product(nc.vector, "pr_c", 3, n, HEAD_C, 0, 4, 1, 2)
+                return
+            new_product(nc.vector, "pr_c", 3, n, HEAD_C, 0, 4 - gpsimd_planes(n), 0, 2)
+            new_product(nc.vector, "pr_d", 3, n, HEAD_D, 0, 4, len(scalar_halves(n)), 2)
 
         def cycle(c):
             if c > 0:
@@ -491,18 +495,26 @@ def tile_productkeysoftmemoryplus_t_kernel(
                 memory(2 * c - 1)
             gain(4 * c)
             gain(4 * c + 1)
-            if c > 0:
+            if 0 < c < NPAIR - 2:
                 times_base(2 * c + 2, 2 * c + 4)
-                gpsimd_product(2 * c + 3)
+                n = 2 * c + 3
+                new_product(nc.gpsimd, "pr_g", 2, n, HEAD_C, 4 - gpsimd_planes(n), 4, 0, 2)
+            if c == NPAIR - 2:
+                times_base(last - 1, last)
+                times_base(last, NT)
             if c % 2 == 1 and (c + 3) // 2 < NGROUP:
                 reciprocals((c + 3) // 2)
-            for h, g in scalar_halves(2 * c + 2):
+            for h, g in scalar_halves(2 * c + 2)[:2]:
                 scalar_half(2 * c + 2, h, g)
             if c > 1:
                 gate_silu(2 * c - 2)
                 gate_silu(2 * c - 1)
-            if c + 2 < NPAIR:
-                two_heads(2 * c + 4, 9 * EARLY_ROWS - 2 * N if c == 0 else 0)
+            for h, g in scalar_halves(2 * c + 2)[2:]:
+                scalar_half(2 * c + 2, h, g)
+            if c == 0:
+                rows_up_to(4 * N)
+            elif c + 2 < NPAIR:
+                two_heads(2 * c + 4)
                 two_heads(2 * c + 5)
             for h, g in scalar_halves(2 * c + 3):
                 scalar_half(2 * c + 3, h, g)
@@ -530,7 +542,8 @@ def tile_productkeysoftmemoryplus_t_kernel(
                 denominators((c + 4) // 2)
             if c > 0:
                 final(2 * c - 1)
-            u_quant(c)
+            u_quant(2 * c)
+            u_quant(2 * c + 1)
             turn(4 * c + 4)
             turn(4 * c + 5)
 
@@ -548,12 +561,15 @@ def tile_productkeysoftmemoryplus_t_kernel(
             h, t0 = k // 2, 2 * (k % 2)
             new_product(nc.gpsimd, "pr_early", 4, 0, h, t0, t0 + 2, 0, 2)
 
-        def early_rows(k):
-            first = EARLY_ROWS * k
-            for i in range(first, first + EARLY_ROWS):
-                two_heads(2 + i // N, i % N, i % N + 1)
+        rows_done = [0]
 
-        widen_pair(0)
+        def rows_up_to(total):
+            for i in range(rows_done[0], total):
+                two_heads(2 + i // N, i % N, i % N + 1)
+            rows_done.append(total)
+            rows_done.remove(rows_done[0])
+
+        widen_first_pair()
         widen_pair(1)
         wk_copy()
         x_transpose(0)
@@ -574,71 +590,66 @@ def tile_productkeysoftmemoryplus_t_kernel(
         widen_group(2)
         interleave(nc.scalar.copy, wg_il, wg_raw, 256, 512)
         floors(0)
-        for j in range(1, NGROUP):
-            if j < NGROUP:
-                x_scale_out(2 * j)
-            else:
-                new_product(nc.vector, "pr_c", 3, 0, HEAD_C, 0, 4, 0, 2)
-            softmax_pair(max(0, 2 * j - 3))
-            if j == 1:
-                interleave(nc.scalar.copy, v_il[0], v_raw[0], 0, 256)
-            if j == 2:
-                ratios(0)
-                interleave(nc.scalar.copy, v_il[0], v_raw[0], 256, 512)
+        softmax_pair(0)
+        interleave(nc.scalar.copy, v_il[0], v_raw[0], 0, 256)
+        maxima(1)
+        x_scale_out(2)
+        x_transpose(4)
+        floors(1)
+        x_scale_out(3)
+        x_transpose(5)
+        softmax_pair(1)
+        ratios(0)
+        interleave(nc.scalar.copy, v_il[0], v_raw[0], 256, 512)
+        x_quant(2, 4)
+        scores(2)
+        scores(3)
+        widen_group(3)
+        interleave(nc.gpsimd.tensor_copy, v_il[1], v_raw[1], 384, 512)
+        for j in range(2, NGROUP):
+            x_scale_out(2 * j)
             if j > 2:
+                softmax_pair(2 * j - 3)
                 ratios(j - 2)
-            if 3 <= j < NGROUP:
-                early_rows(2 * j - 6)
+                rows_up_to(EARLY_ROWS * (2 * j - 4))
             if j + 1 < NGROUP:
                 x_transpose(2 * j + 2)
-            maxima(max(1, 2 * j - 2))
-            if j < NGROUP:
-                x_scale_out(2 * j + 1)
-            else:
-                new_product(nc.vector, "pr_d", 3, 0, HEAD_D, 0, 4, 0, 2)
-                turn(0)
-                turn(1)
+            maxima(2 * j - 2)
+            if j == 2:
+                denominators(0)
+            x_scale_out(2 * j + 1)
             if j + 1 < NGROUP:
                 x_transpose(2 * j + 3)
-            floors(max(1, 2 * j - 2))
-            if j in (2, 3):
-                denominators(j - 2)
-            if j > 1:
-                maxima(2 * j - 1)
-                if j in (2, 3):
-                    reciprocals(j - 2)
-                softmax_pair(2 * j - 2)
+            floors(2 * j - 2)
             if j == 2:
+                reciprocals(0)
+                interleave(nc.scalar.copy, v_il[1], v_raw[1], 0, 384)
                 normalise(0)
+            maxima(2 * j - 1)
             if j == 3:
-                interleave(nc.scalar.copy, v_il[1], v_raw[1], 0, 256)
+                denominators(1)
+            softmax_pair(2 * j - 2)
             if j == 4:
                 normalise(1)
-            if 4 <= j < NGROUP:
-                early_rows(2 * j - 7)
-            if j == 2:
-                quantise(wg_codes[:], wg_scales[:], wg_il[:])
-            if j in (3, 4):
-                quantise(v_codes[:, j - 3, :], v_scales[:, j - 3, :], v_il[j - 3][:])
+            rows_up_to(EARLY_ROWS * (2 * j - 3))
             if j == NGROUP - 1:
                 e2_to_psum(0)
-            if j == NGROUP:
-                new_product(nc.vector, "pr_c", 3, 1, HEAD_C, 0, 4, 0, 2)
-            if j < NGROUP:
-                x_quant(2 * j, 2 * j + 2)
-                scores(2 * j)
-                scores(2 * j + 1)
+            x_quant(2 * j, 2 * j + 2)
+            scores(2 * j)
+            scores(2 * j + 1)
+            if j == 3:
+                quantise(wg_codes[:], wg_scales[:], wg_il[:])
+            if j in (4, 5):
+                quantise(v_codes[:, j - 4, :], v_scales[:, j - 4, :], v_il[j - 4][:])
             if j + 2 < NGROUP:
                 widen_group(j + 2)
-            if j == 1:
-                interleave(nc.gpsimd.tensor_copy, v_il[1], v_raw[1], 256, 512)
-            if j in (NGROUP - 2, NGROUP - 1):
+                early_half(j - 2)
+            else:
                 h = j + 2 - NGROUP
                 product(nc.gpsimd, x_rooms[(j - 1) % 3][:].bitcast(F32), 1, h, 0, 4, 0, 2)
-            if 2 <= j <= 5:
-                early_half(j - 2)
-            if j > 1:
-                floors(2 * j - 1)
+            floors(2 * j - 1)
+            if j == 3:
+                reciprocals(1)
         new_product(nc.vector, "pr_c", 3, 0, HEAD_C, 0, 4, 0, 2)
         softmax_pair(NPAIR - 3)
         ratios(NGROUP - 2)
@@ -660,30 +671,27 @@ def tile_productkeysoftmemoryplus_t_kernel(
         e2_to_psum(1)
         for c in range(NPAIR - 1):
             cycle(c)
-        c = NPAIR - 1
+        turn(2 * last)
+        gain(2 * last - 2)
+        turn(2 * last + 1)
+        gain(2 * last - 1)
         gate_matmul(last - 3)
         gate_matmul(last - 2)
         memory(last - 3)
         memory(last - 2)
-        gain(4 * c)
-        gain(4 * c + 1)
         gate_silu(last - 3)
         gate_silu(last - 2)
-        turn(4 * c + 2)
-        turn(4 * c + 3)
+        gain(2 * last)
+        u_quant(last - 1)
+        gain(2 * last + 1)
+        u_quant(last)
         final(last - 3)
-        u_quant(c, 0, 2)
         gate_matmul(last - 1)
         gate_matmul(last)
+        memory(last - 1)
+        memory(last)
         gate_silu(last - 1)
         gate_silu(last)
-        memory(last - 1)
-        gain(4 * c + 2)
         final(last - 2)
-        gain(4 * c + 3)
-        u_quant(c, 2, 3)
-        memory(last, (0,))
         final(last - 1)
-        u_quant(c, 3, 4)
-        memory(last, (1,))
         final(last)

@@ -446,7 +446,7 @@ def tile_productkeysoftmemoryplus_t_kernel(
                 )
 
         def gate_matmul(n):
-            a_ps = bank(5 + n % 2, [D], "a_ps")
+            a_ps = bank((5 if n > 1 else 3) + n % 2, [D], "a_ps")
             mx_x(a_ps[:], n, wg_codes, wg_scales)
             state["a", n] = a_ps
 
@@ -487,9 +487,6 @@ def tile_productkeysoftmemoryplus_t_kernel(
         def cycle(c):
             if c > 0:
                 e2_to_psum(c + 1)
-            if c > 1:
-                gate_matmul(2 * c - 2)
-                gate_matmul(2 * c - 1)
             if c > 0:
                 memory(2 * c - 2)
                 memory(2 * c - 1)
@@ -506,9 +503,6 @@ def tile_productkeysoftmemoryplus_t_kernel(
                 reciprocals((c + 3) // 2)
             for h, g in scalar_halves(2 * c + 2)[:2]:
                 scalar_half(2 * c + 2, h, g)
-            if c > 1:
-                gate_silu(2 * c - 2)
-                gate_silu(2 * c - 1)
             for h, g in scalar_halves(2 * c + 2)[2:]:
                 scalar_half(2 * c + 2, h, g)
             if c == 0:
@@ -522,25 +516,26 @@ def tile_productkeysoftmemoryplus_t_kernel(
                 normalise((c + 3) // 2)
             if c > 0:
                 vector_products(2 * c + 2)
-                vector_products(2 * c + 3)
             else:
                 new_product(nc.vector, "pr_c", 3, 2, HEAD_C, 0, 2, 0, 2)
                 new_product(nc.vector, "pr_d", 3, 2, HEAD_D, 0, 4, 0, 2)
-                new_product(nc.vector, "pr_d", 3, 3, HEAD_D, 0, 4, 0, 2)
             turn(4 * c + 2)
             turn(4 * c + 3)
-            if c == 0:
-                gate_matmul(0)
-                gate_matmul(1)
-                gate_silu(0)
-                gate_silu(1)
             if c > 0:
-                final(2 * c - 2)
+                gate_matmul(2 * c)
+                gate_matmul(2 * c + 1)
+            gate_silu(2 * c)
+            gate_silu(2 * c + 1)
             gain(4 * c + 2)
+            if c > 0:
+                vector_products(2 * c + 3)
+            else:
+                new_product(nc.vector, "pr_d", 3, 3, HEAD_D, 0, 4, 0, 2)
             gain(4 * c + 3)
             if c % 2 == 0 and (c + 4) // 2 < NGROUP:
                 denominators((c + 4) // 2)
             if c > 0:
+                final(2 * c - 2)
                 final(2 * c - 1)
             u_quant(2 * c)
             u_quant(2 * c + 1)
@@ -577,35 +572,35 @@ def tile_productkeysoftmemoryplus_t_kernel(
         widen_pair(2)
         widen_pair(3)
         x_scale_out(0)
+        x_transpose(2)
         quantise(wk_codes[:], wk_scales[:], wk_il)
         x_quant(0, 1)
         interleave(nc.gpsimd.tensor_copy, wg_il, wg_raw, 0, 256)
         scores(0)
         x_scale_out(1)
-        x_transpose(2)
         x_transpose(3)
-        maxima(0)
         x_quant(1, 2)
+        maxima(0)
         scores(1)
         widen_group(2)
         interleave(nc.scalar.copy, wg_il, wg_raw, 256, 512)
-        floors(0)
-        softmax_pair(0)
         interleave(nc.scalar.copy, v_il[0], v_raw[0], 0, 256)
-        maxima(1)
+        floors(0)
         x_scale_out(2)
         x_transpose(4)
-        floors(1)
+        softmax_pair(0)
+        maxima(1)
         x_scale_out(3)
         x_transpose(5)
-        softmax_pair(1)
-        ratios(0)
-        interleave(nc.scalar.copy, v_il[0], v_raw[0], 256, 512)
+        floors(1)
         x_quant(2, 4)
         scores(2)
         scores(3)
         widen_group(3)
         interleave(nc.gpsimd.tensor_copy, v_il[1], v_raw[1], 384, 512)
+        interleave(nc.scalar.copy, v_il[0], v_raw[0], 256, 512)
+        softmax_pair(1)
+        ratios(0)
         for j in range(2, NGROUP):
             x_scale_out(2 * j)
             if j > 2:
@@ -615,19 +610,21 @@ def tile_productkeysoftmemoryplus_t_kernel(
             if j + 1 < NGROUP:
                 x_transpose(2 * j + 2)
             maxima(2 * j - 2)
+            if j == 4:
+                denominators(1)
+            x_scale_out(2 * j + 1)
             if j == 2:
                 denominators(0)
-            x_scale_out(2 * j + 1)
             if j + 1 < NGROUP:
                 x_transpose(2 * j + 3)
             floors(2 * j - 2)
+            if j == 4:
+                reciprocals(1)
+            maxima(2 * j - 1)
             if j == 2:
                 reciprocals(0)
                 interleave(nc.scalar.copy, v_il[1], v_raw[1], 0, 384)
                 normalise(0)
-            maxima(2 * j - 1)
-            if j == 3:
-                denominators(1)
             softmax_pair(2 * j - 2)
             if j == 4:
                 normalise(1)
@@ -648,11 +645,12 @@ def tile_productkeysoftmemoryplus_t_kernel(
                 h = j + 2 - NGROUP
                 product(nc.gpsimd, x_rooms[(j - 1) % 3][:].bitcast(F32), 1, h, 0, 4, 0, 2)
             floors(2 * j - 1)
-            if j == 3:
-                reciprocals(1)
         new_product(nc.vector, "pr_c", 3, 0, HEAD_C, 0, 4, 0, 2)
         softmax_pair(NPAIR - 3)
         ratios(NGROUP - 2)
+        new_product(nc.vector, "pr_d", 3, 0, HEAD_D, 0, 4, 0, 2)
+        turn(0)
+        turn(1)
         maxima(NPAIR - 2)
         maxima(NPAIR - 1)
         floors(NPAIR - 2)
@@ -660,9 +658,8 @@ def tile_productkeysoftmemoryplus_t_kernel(
         softmax_pair(NPAIR - 2)
         softmax_pair(NPAIR - 1)
         ratios(NGROUP - 1)
-        new_product(nc.vector, "pr_d", 3, 0, HEAD_D, 0, 4, 0, 2)
-        turn(0)
-        turn(1)
+        gate_matmul(1)
+        gate_matmul(0)
         new_product(nc.vector, "pr_c", 3, 1, HEAD_C, 0, 4, 0, 2)
         times_base(2, 4)
         new_product(nc.gpsimd, "pr_g", 2, 2, HEAD_C, 2, 4, 0, 2)
@@ -675,12 +672,8 @@ def tile_productkeysoftmemoryplus_t_kernel(
         gain(2 * last - 2)
         turn(2 * last + 1)
         gain(2 * last - 1)
-        gate_matmul(last - 3)
-        gate_matmul(last - 2)
         memory(last - 3)
         memory(last - 2)
-        gate_silu(last - 3)
-        gate_silu(last - 2)
         gain(2 * last)
         u_quant(last - 1)
         gain(2 * last + 1)

@@ -404,37 +404,39 @@ def tile_productkeysoftmemoryplus_t_kernel(
                 )
             state["ub", k] = ub
 
-        def gain(k):
-            n, g = divmod(k, 2)
+        def u_of(k):
+            q = k // 4
             if k % 4 == 0:
-                state["u", n] = rooms[(n // 2 + 2) % 3][:, SLOTS : SLOTS + D].bitcast(BF16)
-            if k % 4 == 2:
-                u = work.tile([P, SLOTS], BF16, name="u", align_bytes=64)
-                state["u", n] = u[:]
+                return rooms[(q + 2) % 3][:, SLOTS : SLOTS + D // 2].bitcast(BF16)
+            if ("u", q) not in state:
+                state["u", q] = work.tile([P, 3 * D], BF16, name="u", align_bytes=64)
+            return state["u", q][:, D * (k % 4 - 1) : D * (k % 4)]
+
+        def gain(k):
             nc.vector.tensor_tensor(
-                out=state["u", n][:, D * g : D * (g + 1)].rearrange("p (k t) -> p k t", t=4),
+                out=u_of(k).rearrange("p (k t) -> p k t", t=4),
                 in0=state["ub", k][:].rearrange("p t k -> p k t"),
-                in1=gain_sb[:, g, :].unsqueeze(1).broadcast_to([P, P, 4]),
+                in1=gain_sb[:, k % 2, :].unsqueeze(1).broadcast_to([P, P, 4]),
                 op=ALU.mult,
             )
 
-        def u_quant(n, passes=(0, 1)):
-            if passes[0] == 0:
-                uc = work.tile([P, 2 * P], U32, name="uc", bufs=4, align_bytes=64)
-                us = work.tile([P, 2 * P], U8, name="us", bufs=4, align_bytes=64)
-                state["uc", n] = (uc, us)
-            uc, us = state["uc", n]
-            cols = slice(P * passes[0], P * (passes[-1] + 1))
-            u = state["u", n][:, D * passes[0] : D * (passes[-1] + 1)]
+        def u_quant(q, k0, k1):
+            if k0 == 0:
+                uc = work.tile([P, 4 * P], U32, name="uc", align_bytes=64)
+                us = work.tile([P, 4 * P], U8, name="us", align_bytes=64)
+                state["uc", q] = (uc, us)
+            uc, us = state["uc", q]
+            cols = slice(P * k0, P * k1)
+            u = u_of(4 * q) if k0 == 0 else state["u", q][:, D * (k0 - 1) : D * (k1 - 1)]
             quantise(uc[:, cols], us[:, cols], u)
 
         def memory(n, passes=(0, 1)):
             if passes[0] == 0:
                 state["mem", n] = bank(MEM_BANKS.get(n, 3 + n % 2), [D], "mem")
             mem = state["mem", n]
-            uc, us = state["uc", n]
+            uc, us = state["uc", n // 2]
             for g in passes:
-                cols = slice(P * g, P * (g + 1))
+                cols = slice(P * (2 * (n % 2) + g), P * (2 * (n % 2) + g + 1))
                 nc.tensor.matmul_mx(
                     out=mem[:],
                     lhsT=uc[:, cols].bitcast(FP8X4),
@@ -457,10 +459,19 @@ def tile_productkeysoftmemoryplus_t_kernel(
         def gate_silu(n):
             nc.scalar.activation(out=gate_of(n), in_=state["a", n][:], func=ACT.Silu)
 
-        def final(n):
-            o = work.tile([P, D], F32, name="o", bufs=5)
-            nc.vector.tensor_tensor(out=o[:], in0=state["mem", n][:], in1=gate_of(n), op=ALU.mult)
-            nc.sync.dma_start(out=out_view[:, n, :], in_=o[:])
+        def final(n, o):
+            nc.vector.tensor_tensor(out=o, in0=state["mem", n][:], in1=gate_of(n), op=ALU.mult)
+
+        def final_pair(q):
+            o = work.tile([P, 2, D], F32, name="o_pair")
+            final(2 * q + 1, o[:, 1, :])
+            final(2 * q, o[:, 0, :])
+            nc.sync.dma_start(out=out_view[:, 2 * q : 2 * q + 2, :], in_=o[:])
+
+        def final_tile(n):
+            o = sums_of_two[1][:, D * (n % 4) : D * (n % 4 + 1)]
+            final(n, o)
+            nc.sync.dma_start(out=out_view[:, n, :], in_=o)
 
 
         last = NT - 1
@@ -475,7 +486,7 @@ def tile_productkeysoftmemoryplus_t_kernel(
         def gpsimd_planes(n):
             if n % 2 == 0 or n == last:
                 return 0
-            return 3 if (n % 4 == 3 or n < 8) else 2
+            return 3
 
         def vector_products(n):
             if n >= last - 1:
@@ -490,8 +501,8 @@ def tile_productkeysoftmemoryplus_t_kernel(
             if c > 0:
                 memory(2 * c - 2)
                 memory(2 * c - 1)
-            gain(4 * c)
             gain(4 * c + 1)
+            gain(4 * c)
             if 0 < c < NPAIR - 2:
                 times_base(2 * c + 2, 2 * c + 4)
                 n = 2 * c + 3
@@ -535,10 +546,9 @@ def tile_productkeysoftmemoryplus_t_kernel(
             if c % 2 == 0 and (c + 4) // 2 < NGROUP:
                 denominators((c + 4) // 2)
             if c > 0:
-                final(2 * c - 2)
-                final(2 * c - 1)
-            u_quant(2 * c)
-            u_quant(2 * c + 1)
+                final_pair(c - 1)
+            u_quant(c, 0, 1)
+            u_quant(c, 1, 4)
             turn(4 * c + 4)
             turn(4 * c + 5)
 
@@ -674,17 +684,18 @@ def tile_productkeysoftmemoryplus_t_kernel(
         gain(2 * last - 1)
         memory(last - 3)
         memory(last - 2)
+        u_quant(NPAIR - 1, 0, 1)
         gain(2 * last)
-        u_quant(last - 1)
+        u_quant(NPAIR - 1, 1, 2)
         gain(2 * last + 1)
-        u_quant(last)
-        final(last - 3)
         gate_matmul(last - 1)
         gate_matmul(last)
         memory(last - 1)
-        memory(last)
         gate_silu(last - 1)
         gate_silu(last)
-        final(last - 2)
-        final(last - 1)
-        final(last)
+        final_tile(last - 3)
+        u_quant(NPAIR - 1, 2, 4)
+        memory(last)
+        final_tile(last - 2)
+        final_tile(last - 1)
+        final_tile(last)

@@ -26,7 +26,8 @@ FLOPS = 2 * T * D * C + 2 * T * SLOTS * D + 2 * T * D * D
 BASE, RATIO, HEAD_C, HEAD_D = 0, 1, 2, 3
 FLOOR = -80.0
 EARLY_ROWS = 10
-MEM_BANKS = {NT - 2: 7, NT - 1: 1}
+G_PLANES = 3
+MEM_BANKS = {NT - 2: 7, NT - 1: 3}
 
 X_CHUNKS = [(0, 2), (2, 4), (4, 8), (8, 16), (16, 24), (24, 32)]
 
@@ -302,9 +303,10 @@ def tile_productkeysoftmemoryplus_t_kernel(
         def terms(n, g, t):
             return state.setdefault(("terms", n, g, t), [])
 
-        def e2_to_psum(q):
-            e2 = bank(7, [2, 2, N], "e2_ps")
-            second = e2_cd[q // 2][:, 2 * (q % 2) : 2 * (q % 2) + 2, :, :]
+        def e2_to_psum(q0, q1):
+            e2 = bank(7, [2 * (q1 - q0), 2, N], "e2_ps")
+            first = 2 * (q0 % 2)
+            second = e2_cd[q0 // 2][:, first : first + 2 * (q1 - q0), :, :]
             nc.tensor.matmul(
                 e2[:].rearrange("p s h k -> p (s h k)"),
                 lhsT=ident[:],
@@ -312,11 +314,12 @@ def tile_productkeysoftmemoryplus_t_kernel(
                 start=True,
                 stop=True,
             )
-            state["e2_ps", q] = e2
+            for s in range(2 * (q1 - q0)):
+                state["e2_ps", 2 * q0 + s] = e2[:, s, :, :]
 
         def product(eng, dst, n, h, t0, t1, g0, g1):
             if eng is nc.vector:
-                e2 = state["e2_ps", n // 2][:, n % 2, h - HEAD_C, :]
+                e2 = state["e2_ps", n][:, h - HEAD_C, :]
             else:
                 e2 = e2_of(n, h)
             nt, ni = t1 - t0, 16 * (g1 - g0)
@@ -383,17 +386,22 @@ def tile_productkeysoftmemoryplus_t_kernel(
                     first = 2 * P * r + P * g
                     state["last", n0 + r // 4, g, r % 4] = room[:, first : first + P]
 
-        def turn(k):
+        def turn(k, before_last=None):
             n, g = divmod(k, 2)
-            ub = bank(k % 3, [4, P], "ub_ps")
+            ub = bank(2 + k % 3, [4, P], "ub_ps")
             todo = []
             for t in range(4):
                 if ("last", n, g, t) in state:
-                    terms(n, g, t).append(state["last", n, g, t])
+                    place = 0 if n == 2 else len(terms(n, g, t))
+                    state["terms", n, g, t] = (
+                        terms(n, g, t)[:place] + [state["last", n, g, t]] + terms(n, g, t)[place:]
+                    )
             for r in range(len(terms(n, g, 0))):
                 for t in range(4):
                     todo.append((t, terms(n, g, t)[r]))
             for i, (t, term) in enumerate(todo):
+                if i == len(todo) - 4 and before_last is not None:
+                    before_last()
                 nc.tensor.matmul(
                     ub[:, t, :],
                     lhsT=term,
@@ -432,7 +440,7 @@ def tile_productkeysoftmemoryplus_t_kernel(
 
         def memory(n, passes=(0, 1)):
             if passes[0] == 0:
-                state["mem", n] = bank(MEM_BANKS.get(n, 3 + n % 2), [D], "mem")
+                state["mem", n] = bank(MEM_BANKS.get(n, n % 2), [D], "mem")
             mem = state["mem", n]
             uc, us = state["uc", n // 2]
             for g in passes:
@@ -448,7 +456,7 @@ def tile_productkeysoftmemoryplus_t_kernel(
                 )
 
         def gate_matmul(n):
-            a_ps = bank((5 if n > 1 else 3) + n % 2, [D], "a_ps")
+            a_ps = bank((5 if n > 1 else 0) + n % 2, [D], "a_ps")
             mx_x(a_ps[:], n, wg_codes, wg_scales)
             state["a", n] = a_ps
 
@@ -477,76 +485,57 @@ def tile_productkeysoftmemoryplus_t_kernel(
         last = NT - 1
 
         def scalar_halves(n):
-            if n < 5:
+            if n == 4:
                 return []
             if n >= last - 1:
                 return [(HEAD_D, 0), (HEAD_C, 0), (HEAD_D, 1)]
             return [(HEAD_D, 0)] if n % 4 != 3 else []
 
-        def gpsimd_planes(n):
-            if n % 2 == 0 or n == last:
-                return 0
-            return 3
-
         def vector_products(n):
             if n >= last - 1:
                 new_product(nc.vector, "pr_c", 3, n, HEAD_C, 0, 4, 1, 2)
                 return
-            new_product(nc.vector, "pr_c", 3, n, HEAD_C, 0, 4 - gpsimd_planes(n), 0, 2)
+            new_product(nc.vector, "pr_c", 3, n, HEAD_C, 0, 4 - G_PLANES * (n % 2), 0, 2)
             new_product(nc.vector, "pr_d", 3, n, HEAD_D, 0, 4, len(scalar_halves(n)), 2)
 
         def cycle(c):
-            if c > 0:
-                e2_to_psum(c + 1)
-            if c > 0:
-                memory(2 * c - 2)
-                memory(2 * c - 1)
+            e2_to_psum(c + 1, c + 2)
+            memory(2 * c - 2)
+            memory(2 * c - 1)
             gain(4 * c + 1)
             gain(4 * c)
-            if 0 < c < NPAIR - 2:
+            if c < NPAIR - 2:
                 times_base(2 * c + 2, 2 * c + 4)
                 n = 2 * c + 3
-                new_product(nc.gpsimd, "pr_g", 2, n, HEAD_C, 4 - gpsimd_planes(n), 4, 0, 2)
-            if c == NPAIR - 2:
+                new_product(nc.gpsimd, "pr_g", 2, n, HEAD_C, 4 - G_PLANES, 4, 0, 2)
+            else:
                 times_base(last - 1, last)
                 times_base(last, NT)
             if c % 2 == 1 and (c + 3) // 2 < NGROUP:
                 reciprocals((c + 3) // 2)
-            for h, g in scalar_halves(2 * c + 2)[:2]:
+            for h, g in scalar_halves(2 * c + 2):
                 scalar_half(2 * c + 2, h, g)
-            for h, g in scalar_halves(2 * c + 2)[2:]:
-                scalar_half(2 * c + 2, h, g)
-            if c == 0:
-                rows_up_to(4 * N)
-            elif c + 2 < NPAIR:
+            if c + 2 < NPAIR:
                 two_heads(2 * c + 4)
                 two_heads(2 * c + 5)
             for h, g in scalar_halves(2 * c + 3):
                 scalar_half(2 * c + 3, h, g)
             if c % 2 == 1 and (c + 3) // 2 < NGROUP:
                 normalise((c + 3) // 2)
-            if c > 0:
-                vector_products(2 * c + 2)
-            else:
-                new_product(nc.vector, "pr_c", 3, 2, HEAD_C, 0, 2, 0, 2)
-                new_product(nc.vector, "pr_d", 3, 2, HEAD_D, 0, 4, 0, 2)
+            vector_products(2 * c + 2)
             turn(4 * c + 2)
             turn(4 * c + 3)
-            if c > 0:
+            if c > 1:
                 gate_matmul(2 * c)
-                gate_matmul(2 * c + 1)
+            gate_matmul(2 * c + 1)
             gate_silu(2 * c)
             gate_silu(2 * c + 1)
             gain(4 * c + 2)
-            if c > 0:
-                vector_products(2 * c + 3)
-            else:
-                new_product(nc.vector, "pr_d", 3, 3, HEAD_D, 0, 4, 0, 2)
+            vector_products(2 * c + 3)
             gain(4 * c + 3)
             if c % 2 == 0 and (c + 4) // 2 < NGROUP:
                 denominators((c + 4) // 2)
-            if c > 0:
-                final_pair(c - 1)
+            final_pair(c - 1)
             u_quant(c, 0, 1)
             u_quant(c, 1, 4)
             turn(4 * c + 4)
@@ -640,10 +629,11 @@ def tile_productkeysoftmemoryplus_t_kernel(
                 normalise(1)
             rows_up_to(EARLY_ROWS * (2 * j - 3))
             if j == NGROUP - 1:
-                e2_to_psum(0)
+                e2_to_psum(0, 2)
             x_quant(2 * j, 2 * j + 2)
-            scores(2 * j)
-            scores(2 * j + 1)
+            if j + 1 < NGROUP:
+                scores(2 * j)
+                scores(2 * j + 1)
             if j == 3:
                 quantise(wg_codes[:], wg_scales[:], wg_il[:])
             if j in (4, 5):
@@ -655,12 +645,20 @@ def tile_productkeysoftmemoryplus_t_kernel(
                 h = j + 2 - NGROUP
                 product(nc.gpsimd, x_rooms[(j - 1) % 3][:].bitcast(F32), 1, h, 0, 4, 0, 2)
             floors(2 * j - 1)
+        def last_scores_first_gates():
+            scores(NPAIR - 2)
+            scores(NPAIR - 1)
+            gate_matmul(0)
+            gate_matmul(1)
+
         new_product(nc.vector, "pr_c", 3, 0, HEAD_C, 0, 4, 0, 2)
         softmax_pair(NPAIR - 3)
         ratios(NGROUP - 2)
+        rows_up_to(4 * N)
         new_product(nc.vector, "pr_d", 3, 0, HEAD_D, 0, 4, 0, 2)
-        turn(0)
+        turn(0, last_scores_first_gates)
         turn(1)
+        new_product(nc.vector, "pr_c", 3, 1, HEAD_C, 0, 4, 0, 2)
         maxima(NPAIR - 2)
         maxima(NPAIR - 1)
         floors(NPAIR - 2)
@@ -668,15 +666,27 @@ def tile_productkeysoftmemoryplus_t_kernel(
         softmax_pair(NPAIR - 2)
         softmax_pair(NPAIR - 1)
         ratios(NGROUP - 1)
-        gate_matmul(1)
-        gate_matmul(0)
-        new_product(nc.vector, "pr_c", 3, 1, HEAD_C, 0, 4, 0, 2)
-        times_base(2, 4)
-        new_product(nc.gpsimd, "pr_g", 2, 2, HEAD_C, 2, 4, 0, 2)
-        new_product(nc.gpsimd, "pr_g", 2, 3, HEAD_C, 0, 4, 0, 2)
+        gate_silu(0)
+        gate_silu(1)
         new_product(nc.vector, "pr_d", 3, 1, HEAD_D, 0, 4, 0, 2)
-        e2_to_psum(1)
-        for c in range(NPAIR - 1):
+        turn(2)
+        gain(0)
+        turn(3)
+        gain(1)
+        times_base(2, 4)
+        new_product(nc.vector, "pr_d", 3, 2, HEAD_D, 0, 4, 0, 2)
+        new_product(nc.gpsimd, "pr_g", 2, 2, HEAD_C, 2, 4, 0, 2)
+        new_product(nc.vector, "pr_c", 3, 2, HEAD_C, 0, 2, 0, 2)
+        new_product(nc.gpsimd, "pr_g", 2, 3, HEAD_C, 0, 4, 0, 2)
+        gain(2)
+        new_product(nc.vector, "pr_d", 3, 3, HEAD_D, 0, 4, 0, 2)
+        gain(3)
+        denominators(2)
+        u_quant(0, 0, 1)
+        u_quant(0, 1, 4)
+        turn(4, lambda: gate_matmul(2))
+        turn(5)
+        for c in range(1, NPAIR - 1):
             cycle(c)
         turn(2 * last)
         gain(2 * last - 2)

@@ -27,6 +27,7 @@ BASE, RATIO, HEAD_C, HEAD_D = 0, 1, 2, 3
 FLOOR = -80.0
 EARLY_ROWS = 10
 G_PLANES = 3
+G_COLUMNS = 192
 MEM_BANKS = {NT - 2: 7, NT - 1: 3}
 
 X_CHUNKS = [(0, 2), (2, 4), (4, 8), (8, 16), (16, 24), (24, 32)]
@@ -104,7 +105,8 @@ def tile_productkeysoftmemoryplus_t_kernel(
 
         wg_il = keep.tile([P, 4 * D], BF16, name="wg_il", align_bytes=64)
         v_il = [keep.tile([P, 4 * D], BF16, name="v_il%d" % g, align_bytes=64) for g in range(2)]
-        wk_il = wg_il[:, 0 : 4 * C]
+        wk_tile = keep.tile([P, 4 * C], BF16, name="wk_il", align_bytes=64)
+        wk_il = wk_tile[:]
 
         def interleave(copy, dst, src, c0, c1):
             copy(
@@ -371,7 +373,9 @@ def tile_productkeysoftmemoryplus_t_kernel(
         def times_base(n0, n1):
             q, rows = n0 // 2, 4 * (n1 - n0)
             cols = slice(SLOTS * (n0 % 2), SLOTS * (n0 % 2 + n1 - n0))
-            room = rooms[q % 3][:, cols]
+            room = rooms[q % 3][:]
+            if n1 - n0 == 1:
+                room = room[:, SLOTS * (1 - n0 % 2) : SLOTS * (2 - n0 % 2)]
             factor = base[n0 // 4][:, n0 % 4 : n0 % 4 + n1 - n0, :]
             nc.gpsimd.tensor_tensor(
                 out=room.rearrange("p (r i m) -> p r i m", r=rows, m=8),
@@ -461,7 +465,10 @@ def tile_productkeysoftmemoryplus_t_kernel(
             state["a", n] = a_ps
 
         def gate_of(n):
-            room = rooms[n // 2 % 3] if n < NT - 2 else sums_of_two[0]
+            if n < NT - 4:
+                room = rooms[n // 2 % 3][:]
+            else:
+                room = x_rooms[n // 2 % 2][:].bitcast(F32)
             return room[:, D * (n % 2) : D * (n % 2 + 1)]
 
         def gate_silu(n):
@@ -502,6 +509,9 @@ def tile_productkeysoftmemoryplus_t_kernel(
             e2_to_psum(c + 1, c + 2)
             memory(2 * c - 2)
             memory(2 * c - 1)
+            if c == NPAIR - 3:
+                gate_matmul(2 * c + 2)
+                gate_matmul(2 * c + 3)
             gain(4 * c + 1)
             gain(4 * c)
             if c < NPAIR - 2:
@@ -517,6 +527,9 @@ def tile_productkeysoftmemoryplus_t_kernel(
                 scalar_half(2 * c + 2, h, g)
             if c + 2 < NPAIR:
                 two_heads(2 * c + 4)
+                if c == NPAIR - 3:
+                    gate_silu(2 * c + 2)
+                    gate_silu(2 * c + 3)
                 two_heads(2 * c + 5)
             for h, g in scalar_halves(2 * c + 3):
                 scalar_half(2 * c + 3, h, g)
@@ -525,17 +538,21 @@ def tile_productkeysoftmemoryplus_t_kernel(
             vector_products(2 * c + 2)
             turn(4 * c + 2)
             turn(4 * c + 3)
-            if c > 1:
-                gate_matmul(2 * c)
-            gate_matmul(2 * c + 1)
-            gate_silu(2 * c)
-            gate_silu(2 * c + 1)
+            if c < NPAIR - 2:
+                if c > 1:
+                    gate_matmul(2 * c)
+                gate_matmul(2 * c + 1)
+                gate_silu(2 * c)
+                gate_silu(2 * c + 1)
+            else:
+                final_pair(c - 1)
             gain(4 * c + 2)
             vector_products(2 * c + 3)
             gain(4 * c + 3)
             if c % 2 == 0 and (c + 4) // 2 < NGROUP:
                 denominators((c + 4) // 2)
-            final_pair(c - 1)
+            if c < NPAIR - 2:
+                final_pair(c - 1)
             u_quant(c, 0, 1)
             u_quant(c, 1, 4)
             turn(4 * c + 4)
@@ -570,11 +587,10 @@ def tile_productkeysoftmemoryplus_t_kernel(
         x_transpose(1)
         widen_pair(2)
         widen_pair(3)
+        quantise(wk_codes[:], wk_scales[:], wk_il)
         x_scale_out(0)
         x_transpose(2)
-        quantise(wk_codes[:], wk_scales[:], wk_il)
         x_quant(0, 1)
-        interleave(nc.gpsimd.tensor_copy, wg_il, wg_raw, 0, 256)
         scores(0)
         x_scale_out(1)
         x_transpose(3)
@@ -582,13 +598,14 @@ def tile_productkeysoftmemoryplus_t_kernel(
         maxima(0)
         scores(1)
         widen_group(2)
-        interleave(nc.scalar.copy, wg_il, wg_raw, 256, 512)
-        interleave(nc.scalar.copy, v_il[0], v_raw[0], 0, 256)
-        floors(0)
+        interleave(nc.gpsimd.tensor_copy, v_il[0], v_raw[0], 0, G_COLUMNS)
+        interleave(nc.scalar.copy, wg_il, wg_raw, 0, D)
+        interleave(nc.scalar.copy, v_il[0], v_raw[0], G_COLUMNS, D)
         x_scale_out(2)
         x_transpose(4)
-        softmax_pair(0)
+        floors(0)
         maxima(1)
+        softmax_pair(0)
         x_scale_out(3)
         x_transpose(5)
         floors(1)
@@ -596,8 +613,8 @@ def tile_productkeysoftmemoryplus_t_kernel(
         scores(2)
         scores(3)
         widen_group(3)
-        interleave(nc.gpsimd.tensor_copy, v_il[1], v_raw[1], 384, 512)
-        interleave(nc.scalar.copy, v_il[0], v_raw[0], 256, 512)
+        interleave(nc.gpsimd.tensor_copy, v_il[1], v_raw[1], 0, G_COLUMNS)
+        interleave(nc.scalar.copy, v_il[1], v_raw[1], G_COLUMNS, 384)
         softmax_pair(1)
         ratios(0)
         for j in range(2, NGROUP):
@@ -622,13 +639,13 @@ def tile_productkeysoftmemoryplus_t_kernel(
             maxima(2 * j - 1)
             if j == 2:
                 reciprocals(0)
-                interleave(nc.scalar.copy, v_il[1], v_raw[1], 0, 384)
+                interleave(nc.scalar.copy, v_il[1], v_raw[1], 384, D)
                 normalise(0)
             softmax_pair(2 * j - 2)
             if j == 4:
                 normalise(1)
             rows_up_to(EARLY_ROWS * (2 * j - 3))
-            if j == NGROUP - 1:
+            if j == NGROUP - 3:
                 e2_to_psum(0, 2)
             x_quant(2 * j, 2 * j + 2)
             if j + 1 < NGROUP:

@@ -28,6 +28,7 @@ FLOOR = -80.0
 EARLY_ROWS = 10
 G_PLANES = 3
 G_COLUMNS = 192
+S_ROWS = 8
 MEM_BANKS = {NT - 2: 7, NT - 1: 3}
 
 X_CHUNKS = [(0, 2), (2, 4), (4, 8), (8, 16), (16, 24), (24, 32)]
@@ -319,44 +320,56 @@ def tile_productkeysoftmemoryplus_t_kernel(
             for s in range(2 * (q1 - q0)):
                 state["e2_ps", 2 * q0 + s] = e2[:, s, :, :]
 
-        def product(eng, dst, n, h, t0, t1, g0, g1):
+        def product(eng, dst, n, h, t0, t1, i0, i1):
             if eng is nc.vector:
                 e2 = state["e2_ps", n][:, h - HEAD_C, :]
             else:
                 e2 = e2_of(n, h)
-            nt, ni = t1 - t0, 16 * (g1 - g0)
-            planes = dst.rearrange("p (t c) -> p t c", t=nt)
+            nt, ni = t1 - t0, i1 - i0
             eng.tensor_tensor(
-                out=planes.rearrange("p t (i m) -> p t i m", m=8),
-                in0=p1_of(n, h)[:, 16 * g0 : 16 * g1]
-                .unsqueeze(1)
-                .unsqueeze(3)
-                .broadcast_to([P, nt, ni, 8]),
+                out=dst.rearrange("p t (i m) -> p t i m", m=8),
+                in0=p1_of(n, h)[:, i0:i1].unsqueeze(1).unsqueeze(3).broadcast_to([P, nt, ni, 8]),
                 in1=e2[:, 8 * t0 : 8 * t1]
                 .rearrange("p (t m) -> p t m", m=8)
                 .unsqueeze(2)
                 .broadcast_to([P, nt, ni, 8]),
                 op=ALU.mult,
             )
+
+        def add_terms(planes, n, t0, t1, g0, g1):
             for t in range(t0, t1):
                 for g in range(g0, g1):
                     terms(n, g, t).append(planes[:, t - t0, P * (g - g0) : P * (g - g0 + 1)])
 
+        def product_into(eng, room, n, h, t0, t1, g0, g1):
+            planes = room.rearrange("p (t c) -> p t c", t=t1 - t0)
+            product(eng, planes, n, h, t0, t1, 16 * g0, 16 * g1)
+            add_terms(planes, n, t0, t1, g0, g1)
+
         def new_product(eng, name, bufs, n, h, t0, t1, g0, g1):
             pr = work.tile([P, P * (t1 - t0) * (g1 - g0)], F32, name=name, bufs=bufs)
-            product(eng, pr[:], n, h, t0, t1, g0, g1)
+            product_into(eng, pr[:], n, h, t0, t1, g0, g1)
+
+        def scalar_rows(planes, n, h, i0, i1, first):
+            for i in range(i0, i1):
+                nc.scalar.activation(
+                    out=planes[:, :, 8 * (i - first) : 8 * (i - first + 1)],
+                    in_=e2_of(n, h).rearrange("p (t m) -> p t m", t=4),
+                    func=ACT.Copy,
+                    scale=p1_of(n, h)[:, i : i + 1],
+                )
 
         def scalar_half(n, h, g):
             pr = work.tile([P, 4, P], F32, name="pr_s", bufs=5)
-            for i in range(16):
-                nc.scalar.activation(
-                    out=pr[:, :, 8 * i : 8 * (i + 1)],
-                    in_=e2_of(n, h).rearrange("p (t m) -> p t m", t=4),
-                    func=ACT.Copy,
-                    scale=p1_of(n, h)[:, 16 * g + i : 16 * g + i + 1],
-                )
-            for t in range(4):
-                terms(n, g, t).append(pr[:, t, :])
+            scalar_rows(pr[:], n, h, 16 * g, 16 * (g + 1), 16 * g)
+            add_terms(pr[:], n, 0, 4, g, g + 1)
+
+        def shared_head(n):
+            pr = work.tile([P, SLOTS], F32, name="pr_d", bufs=3)
+            planes = pr[:].rearrange("p (t c) -> p t c", t=4)
+            product(nc.vector, planes[:, :, 8 * S_ROWS :], n, HEAD_D, 0, 4, S_ROWS, N)
+            add_terms(planes, n, 0, 4, 0, 2)
+            state["shared", n] = planes
 
         def two_heads(n, i0=0, i1=N):
             two = sums_of_two[n // 2 % 2][:, SLOTS * (n % 2) : SLOTS * (n % 2 + 1)]
@@ -390,7 +403,7 @@ def tile_productkeysoftmemoryplus_t_kernel(
                     first = 2 * P * r + P * g
                     state["last", n0 + r // 4, g, r % 4] = room[:, first : first + P]
 
-        def turn(k, before_last=None):
+        def turn(k, gate=None, after=0):
             n, g = divmod(k, 2)
             ub = bank(2 + k % 3, [4, P], "ub_ps")
             todo = []
@@ -404,8 +417,8 @@ def tile_productkeysoftmemoryplus_t_kernel(
                 for t in range(4):
                     todo.append((t, terms(n, g, t)[r]))
             for i, (t, term) in enumerate(todo):
-                if i == len(todo) - 4 and before_last is not None:
-                    before_last()
+                if i == after and gate is not None:
+                    gate()
                 nc.tensor.matmul(
                     ub[:, t, :],
                     lhsT=term,
@@ -465,10 +478,10 @@ def tile_productkeysoftmemoryplus_t_kernel(
             state["a", n] = a_ps
 
         def gate_of(n):
-            if n < NT - 4:
+            if n < NT - 2:
                 room = rooms[n // 2 % 3][:]
             else:
-                room = x_rooms[n // 2 % 2][:].bitcast(F32)
+                room = x_rooms[1][:].bitcast(F32)
             return room[:, D * (n % 2) : D * (n % 2 + 1)]
 
         def gate_silu(n):
@@ -496,22 +509,29 @@ def tile_productkeysoftmemoryplus_t_kernel(
                 return []
             if n >= last - 1:
                 return [(HEAD_D, 0), (HEAD_C, 0), (HEAD_D, 1)]
-            return [(HEAD_D, 0)] if n % 4 != 3 else []
+            return [(HEAD_D, 0)] if n % 2 == 0 else []
 
         def vector_products(n):
             if n >= last - 1:
                 new_product(nc.vector, "pr_c", 3, n, HEAD_C, 0, 4, 1, 2)
                 return
             new_product(nc.vector, "pr_c", 3, n, HEAD_C, 0, 4 - G_PLANES * (n % 2), 0, 2)
-            new_product(nc.vector, "pr_d", 3, n, HEAD_D, 0, 4, len(scalar_halves(n)), 2)
+            if n % 2 == 1:
+                shared_head(n)
+            else:
+                new_product(nc.vector, "pr_d", 3, n, HEAD_D, 0, 4, len(scalar_halves(n)), 2)
 
         def cycle(c):
             e2_to_psum(c + 1, c + 2)
             memory(2 * c - 2)
             memory(2 * c - 1)
-            if c == NPAIR - 3:
-                gate_matmul(2 * c + 2)
-                gate_matmul(2 * c + 3)
+            for h, g in scalar_halves(2 * c + 2)[:1]:
+                scalar_half(2 * c + 2, h, g)
+            gate_silu(2 * c)
+            gate_silu(2 * c + 1)
+            if c == NPAIR - 2:
+                gate_matmul(last - 1)
+                gate_matmul(last)
             gain(4 * c + 1)
             gain(4 * c)
             if c < NPAIR - 2:
@@ -523,13 +543,10 @@ def tile_productkeysoftmemoryplus_t_kernel(
                 times_base(last, NT)
             if c % 2 == 1 and (c + 3) // 2 < NGROUP:
                 reciprocals((c + 3) // 2)
-            for h, g in scalar_halves(2 * c + 2):
+            for h, g in scalar_halves(2 * c + 2)[1:]:
                 scalar_half(2 * c + 2, h, g)
             if c + 2 < NPAIR:
                 two_heads(2 * c + 4)
-                if c == NPAIR - 3:
-                    gate_silu(2 * c + 2)
-                    gate_silu(2 * c + 3)
                 two_heads(2 * c + 5)
             for h, g in scalar_halves(2 * c + 3):
                 scalar_half(2 * c + 3, h, g)
@@ -537,17 +554,16 @@ def tile_productkeysoftmemoryplus_t_kernel(
                 normalise((c + 3) // 2)
             vector_products(2 * c + 2)
             turn(4 * c + 2)
-            turn(4 * c + 3)
             if c < NPAIR - 2:
-                if c > 1:
-                    gate_matmul(2 * c)
-                gate_matmul(2 * c + 1)
-                gate_silu(2 * c)
-                gate_silu(2 * c + 1)
+                turn(4 * c + 3, lambda: gate_matmul(2 * c + 2), 4)
             else:
+                turn(4 * c + 3)
+            if c == NPAIR - 2:
                 final_pair(c - 1)
             gain(4 * c + 2)
             vector_products(2 * c + 3)
+            if c < NPAIR - 2:
+                scalar_rows(state["shared", 2 * c + 3], 2 * c + 3, HEAD_D, 0, S_ROWS, 0)
             gain(4 * c + 3)
             if c % 2 == 0 and (c + 4) // 2 < NGROUP:
                 denominators((c + 4) // 2)
@@ -555,7 +571,10 @@ def tile_productkeysoftmemoryplus_t_kernel(
                 final_pair(c - 1)
             u_quant(c, 0, 1)
             u_quant(c, 1, 4)
-            turn(4 * c + 4)
+            if c < NPAIR - 2:
+                turn(4 * c + 4, lambda: gate_matmul(2 * c + 3), 8)
+            else:
+                turn(4 * c + 4)
             turn(4 * c + 5)
 
         def floors(q):
@@ -660,7 +679,7 @@ def tile_productkeysoftmemoryplus_t_kernel(
                 early_half(j - 2)
             else:
                 h = j + 2 - NGROUP
-                product(nc.gpsimd, x_rooms[(j - 1) % 3][:].bitcast(F32), 1, h, 0, 4, 0, 2)
+                product_into(nc.gpsimd, x_rooms[(j - 1) % 3][:].bitcast(F32), 1, h, 0, 4, 0, 2)
             floors(2 * j - 1)
         def last_scores_first_gates():
             scores(NPAIR - 2)
@@ -673,7 +692,7 @@ def tile_productkeysoftmemoryplus_t_kernel(
         ratios(NGROUP - 2)
         rows_up_to(4 * N)
         new_product(nc.vector, "pr_d", 3, 0, HEAD_D, 0, 4, 0, 2)
-        turn(0, last_scores_first_gates)
+        turn(0, last_scores_first_gates, 12)
         turn(1)
         new_product(nc.vector, "pr_c", 3, 1, HEAD_C, 0, 4, 0, 2)
         maxima(NPAIR - 2)
@@ -688,7 +707,7 @@ def tile_productkeysoftmemoryplus_t_kernel(
         new_product(nc.vector, "pr_d", 3, 1, HEAD_D, 0, 4, 0, 2)
         turn(2)
         gain(0)
-        turn(3)
+        turn(3, lambda: gate_matmul(2), 8)
         gain(1)
         times_base(2, 4)
         new_product(nc.vector, "pr_d", 3, 2, HEAD_D, 0, 4, 0, 2)
@@ -701,10 +720,12 @@ def tile_productkeysoftmemoryplus_t_kernel(
         denominators(2)
         u_quant(0, 0, 1)
         u_quant(0, 1, 4)
-        turn(4, lambda: gate_matmul(2))
+        turn(4, lambda: gate_matmul(3), 8)
         turn(5)
         for c in range(1, NPAIR - 1):
             cycle(c)
+        gate_silu(last - 1)
+        gate_silu(last)
         turn(2 * last)
         gain(2 * last - 2)
         turn(2 * last + 1)
@@ -715,11 +736,7 @@ def tile_productkeysoftmemoryplus_t_kernel(
         gain(2 * last)
         u_quant(NPAIR - 1, 1, 2)
         gain(2 * last + 1)
-        gate_matmul(last - 1)
-        gate_matmul(last)
         memory(last - 1)
-        gate_silu(last - 1)
-        gate_silu(last)
         final_tile(last - 3)
         u_quant(NPAIR - 1, 2, 4)
         memory(last)

@@ -681,11 +681,14 @@ def tile_productkeysoftmemoryplus_t_kernel(
                 h = j + 2 - NGROUP
                 product_into(nc.gpsimd, x_rooms[(j - 1) % 3][:].bitcast(F32), 1, h, 0, 4, 0, 2)
             floors(2 * j - 1)
+        def second_gates():
+            gate_matmul(2)
+            gate_matmul(3)
+
         def last_scores_first_gates():
             scores(NPAIR - 2)
             scores(NPAIR - 1)
             gate_matmul(0)
-            gate_matmul(1)
 
         new_product(nc.vector, "pr_c", 3, 0, HEAD_C, 0, 4, 0, 2)
         softmax_pair(NPAIR - 3)
@@ -702,12 +705,12 @@ def tile_productkeysoftmemoryplus_t_kernel(
         softmax_pair(NPAIR - 2)
         softmax_pair(NPAIR - 1)
         ratios(NGROUP - 1)
+        new_product(nc.vector, "pr_d", 3, 1, HEAD_D, 0, 4, 0, 2)
+        turn(2, lambda: gate_matmul(1), 0)
         gate_silu(0)
         gate_silu(1)
-        new_product(nc.vector, "pr_d", 3, 1, HEAD_D, 0, 4, 0, 2)
-        turn(2)
         gain(0)
-        turn(3, lambda: gate_matmul(2), 8)
+        turn(3)
         gain(1)
         times_base(2, 4)
         new_product(nc.vector, "pr_d", 3, 2, HEAD_D, 0, 4, 0, 2)
@@ -720,7 +723,7 @@ def tile_productkeysoftmemoryplus_t_kernel(
         denominators(2)
         u_quant(0, 0, 1)
         u_quant(0, 1, 4)
-        turn(4, lambda: gate_matmul(3), 8)
+        turn(4, second_gates, 0)
         turn(5)
         for c in range(1, NPAIR - 1):
             cycle(c)

@@ -521,17 +521,21 @@ def tile_productkeysoftmemoryplus_t_kernel(
             else:
                 new_product(nc.vector, "pr_d", 3, n, HEAD_D, 0, 4, len(scalar_halves(n)), 2)
 
+        def gates(q):
+            gate_matmul(2 * q)
+            gate_matmul(2 * q + 1)
+
         def cycle(c):
             e2_to_psum(c + 1, c + 2)
             memory(2 * c - 2)
-            memory(2 * c - 1)
+            if c == NPAIR - 2:
+                memory(2 * c - 1)
             for h, g in scalar_halves(2 * c + 2)[:1]:
                 scalar_half(2 * c + 2, h, g)
             gate_silu(2 * c)
             gate_silu(2 * c + 1)
             if c == NPAIR - 2:
-                gate_matmul(last - 1)
-                gate_matmul(last)
+                gates(c + 1)
             gain(4 * c + 1)
             gain(4 * c)
             if c < NPAIR - 2:
@@ -555,7 +559,7 @@ def tile_productkeysoftmemoryplus_t_kernel(
             vector_products(2 * c + 2)
             turn(4 * c + 2)
             if c < NPAIR - 2:
-                turn(4 * c + 3, lambda: gate_matmul(2 * c + 2), 4)
+                turn(4 * c + 3, lambda: memory(2 * c - 1), 4)
             else:
                 turn(4 * c + 3)
             if c == NPAIR - 2:
@@ -572,7 +576,7 @@ def tile_productkeysoftmemoryplus_t_kernel(
             u_quant(c, 0, 1)
             u_quant(c, 1, 4)
             if c < NPAIR - 2:
-                turn(4 * c + 4, lambda: gate_matmul(2 * c + 3), 8)
+                turn(4 * c + 4, lambda: gates(c + 1), 8)
             else:
                 turn(4 * c + 4)
             turn(4 * c + 5)
@@ -681,10 +685,6 @@ def tile_productkeysoftmemoryplus_t_kernel(
                 h = j + 2 - NGROUP
                 product_into(nc.gpsimd, x_rooms[(j - 1) % 3][:].bitcast(F32), 1, h, 0, 4, 0, 2)
             floors(2 * j - 1)
-        def second_gates():
-            gate_matmul(2)
-            gate_matmul(3)
-
         def last_scores_first_gates():
             scores(NPAIR - 2)
             scores(NPAIR - 1)
@@ -723,7 +723,7 @@ def tile_productkeysoftmemoryplus_t_kernel(
         denominators(2)
         u_quant(0, 0, 1)
         u_quant(0, 1, 4)
-        turn(4, second_gates, 0)
+        turn(4, lambda: gates(1), 0)
         turn(5)
         for c in range(1, NPAIR - 1):
             cycle(c)

@@ -26,9 +26,8 @@ FLOPS = 2 * T * D * C + 2 * T * SLOTS * D + 2 * T * D * D
 BASE, RATIO, HEAD_C, HEAD_D = 0, 1, 2, 3
 FLOOR = -80.0
 EARLY_ROWS = 10
-G_PLANES = 3
 G_COLUMNS = 192
-S_ROWS = 8
+S_ROWS = 9
 MEM_BANKS = {NT - 2: 7, NT - 1: 3}
 
 X_CHUNKS = [(0, 2), (2, 4), (4, 8), (8, 16), (16, 24), (24, 32)]
@@ -306,19 +305,19 @@ def tile_productkeysoftmemoryplus_t_kernel(
         def terms(n, g, t):
             return state.setdefault(("terms", n, g, t), [])
 
-        def e2_to_psum(q0, q1):
-            e2 = bank(7, [2 * (q1 - q0), 2, N], "e2_ps")
-            first = 2 * (q0 % 2)
-            second = e2_cd[q0 // 2][:, first : first + 2 * (q1 - q0), :, :]
+        def e2_to_psum(q, keys):
+            e2 = bank(7, [4, 2, N], "e2_ps")
+            first = 2 * (q % 2)
+            second = e2_cd[q // 2][:, first:, :, :].rearrange("p s h k -> p (s h k)")
             nc.tensor.matmul(
-                e2[:].rearrange("p s h k -> p (s h k)"),
+                e2[:].rearrange("p s h k -> p (s h k)")[:, 0:keys],
                 lhsT=ident[:],
-                rhs=second.rearrange("p s h k -> p (s h k)"),
+                rhs=second[:, 0:keys],
                 start=True,
                 stop=True,
             )
-            for s in range(2 * (q1 - q0)):
-                state["e2_ps", 2 * q0 + s] = e2[:, s, :, :]
+            for s in range(4 - first):
+                state["e2_ps", 2 * q + s] = e2[:, s, :, :]
 
         def product(eng, dst, n, h, t0, t1, i0, i1):
             if eng is nc.vector:
@@ -365,11 +364,10 @@ def tile_productkeysoftmemoryplus_t_kernel(
             add_terms(pr[:], n, 0, 4, g, g + 1)
 
         def shared_head(n):
-            pr = work.tile([P, SLOTS], F32, name="pr_d", bufs=3)
+            pr = work.tile([P, SLOTS], F32, name="pr_g", bufs=2)
             planes = pr[:].rearrange("p (t c) -> p t c", t=4)
-            product(nc.vector, planes[:, :, 8 * S_ROWS :], n, HEAD_D, 0, 4, S_ROWS, N)
             add_terms(planes, n, 0, 4, 0, 2)
-            state["shared", n] = planes
+            return planes
 
         def two_heads(n, i0=0, i1=N):
             two = sums_of_two[n // 2 % 2][:, SLOTS * (n % 2) : SLOTS * (n % 2 + 1)]
@@ -515,10 +513,8 @@ def tile_productkeysoftmemoryplus_t_kernel(
             if n >= last - 1:
                 new_product(nc.vector, "pr_c", 3, n, HEAD_C, 0, 4, 1, 2)
                 return
-            new_product(nc.vector, "pr_c", 3, n, HEAD_C, 0, 4 - G_PLANES * (n % 2), 0, 2)
-            if n % 2 == 1:
-                shared_head(n)
-            else:
+            new_product(nc.vector, "pr_c", 3, n, HEAD_C, 0, 4, 0, 2)
+            if n % 2 == 0:
                 new_product(nc.vector, "pr_d", 3, n, HEAD_D, 0, 4, len(scalar_halves(n)), 2)
 
         def gates(q):
@@ -526,7 +522,7 @@ def tile_productkeysoftmemoryplus_t_kernel(
             gate_matmul(2 * q + 1)
 
         def cycle(c):
-            e2_to_psum(c + 1, c + 2)
+            e2_to_psum(c + 1, 3 * N)
             memory(2 * c - 2)
             if c == NPAIR - 2:
                 memory(2 * c - 1)
@@ -536,12 +532,13 @@ def tile_productkeysoftmemoryplus_t_kernel(
             gate_silu(2 * c + 1)
             if c == NPAIR - 2:
                 gates(c + 1)
-            gain(4 * c + 1)
             gain(4 * c)
+            gain(4 * c + 1)
             if c < NPAIR - 2:
                 times_base(2 * c + 2, 2 * c + 4)
                 n = 2 * c + 3
-                new_product(nc.gpsimd, "pr_g", 2, n, HEAD_C, 4 - G_PLANES, 4, 0, 2)
+                shared = shared_head(n)
+                product(nc.gpsimd, shared[:, :, 8 * S_ROWS :], n, HEAD_D, 0, 4, S_ROWS, N)
             else:
                 times_base(last - 1, last)
                 times_base(last, NT)
@@ -567,7 +564,7 @@ def tile_productkeysoftmemoryplus_t_kernel(
             gain(4 * c + 2)
             vector_products(2 * c + 3)
             if c < NPAIR - 2:
-                scalar_rows(state["shared", 2 * c + 3], 2 * c + 3, HEAD_D, 0, S_ROWS, 0)
+                scalar_rows(shared, 2 * c + 3, HEAD_D, 0, S_ROWS, 0)
             gain(4 * c + 3)
             if c % 2 == 0 and (c + 4) // 2 < NGROUP:
                 denominators((c + 4) // 2)
@@ -669,7 +666,7 @@ def tile_productkeysoftmemoryplus_t_kernel(
                 normalise(1)
             rows_up_to(EARLY_ROWS * (2 * j - 3))
             if j == NGROUP - 3:
-                e2_to_psum(0, 2)
+                e2_to_psum(0, 8 * N)
             x_quant(2 * j, 2 * j + 2)
             if j + 1 < NGROUP:
                 scores(2 * j)
@@ -684,13 +681,15 @@ def tile_productkeysoftmemoryplus_t_kernel(
             else:
                 h = j + 2 - NGROUP
                 product_into(nc.gpsimd, x_rooms[(j - 1) % 3][:].bitcast(F32), 1, h, 0, 4, 0, 2)
+            if j == NGROUP - 2:
+                new_product(nc.gpsimd, "pr_g", 2, 0, HEAD_C, 2, 4, 0, 2)
             floors(2 * j - 1)
         def last_scores_first_gates():
             scores(NPAIR - 2)
             scores(NPAIR - 1)
             gate_matmul(0)
 
-        new_product(nc.vector, "pr_c", 3, 0, HEAD_C, 0, 4, 0, 2)
+        new_product(nc.vector, "pr_c", 3, 0, HEAD_C, 0, 2, 0, 2)
         softmax_pair(NPAIR - 3)
         ratios(NGROUP - 2)
         rows_up_to(4 * N)

@@ -28,7 +28,7 @@ FLOOR = -80.0
 EARLY_ROWS = 10
 G_COLUMNS = 192
 S_ROWS = 9
-MEM_BANKS = {NT - 2: 7, NT - 1: 3}
+LAST_MEM_BANKS = {NT - 2: 7, NT - 1: 3}
 
 X_CHUNKS = [(0, 2), (2, 4), (4, 8), (8, 16), (16, 24), (24, 32)]
 
@@ -105,8 +105,7 @@ def tile_productkeysoftmemoryplus_t_kernel(
 
         wg_il = keep.tile([P, 4 * D], BF16, name="wg_il", align_bytes=64)
         v_il = [keep.tile([P, 4 * D], BF16, name="v_il%d" % g, align_bytes=64) for g in range(2)]
-        wk_tile = keep.tile([P, 4 * C], BF16, name="wk_il", align_bytes=64)
-        wk_il = wk_tile[:]
+        wk_il = keep.tile([P, 4 * C], BF16, name="wk_il", align_bytes=64)
 
         def interleave(copy, dst, src, c0, c1):
             copy(
@@ -116,7 +115,7 @@ def tile_productkeysoftmemoryplus_t_kernel(
 
         def wk_copy():
             src = wk_raw[:].rearrange("p j (h a k) -> p a h k j", a=2, k=N)
-            dst = wk_il.rearrange("p (a h k j) -> p a h k j", a=2, k=N, j=4)
+            dst = wk_il[:].rearrange("p (a h k j) -> p a h k j", a=2, k=N, j=4)
             nc.vector.tensor_copy(out=dst[:, 0], in_=src[:, 0])
             nc.vector.tensor_copy(
                 out=dst[:, 1].rearrange("p h (t m) j -> p h t m j", t=4),
@@ -151,12 +150,14 @@ def tile_productkeysoftmemoryplus_t_kernel(
                     )
             state["xt", q] = xt
 
+        def scaled(q0, q1):
+            room = x_rooms[(q0 // 2 - 1) % 3]
+            return room[:, 2 * D * (q0 % 2) : 2 * D * (q0 % 2 + q1 - q0)]
+
         def x_scale_out(q):
-            room = x_rooms[(q // 2 - 1) % 3]
-            scaled = room[:, 2 * D * (q % 2) : 2 * D * (q % 2 + 1)]
             pairs = state["xt", q][:].rearrange("p u s k -> p (u s k)").bitcast(BF16)
             nc.vector.tensor_tensor(
-                out=scaled.rearrange("p (k u e) -> p k u e", u=2, e=2),
+                out=scaled(q, q + 1).rearrange("p (k u e) -> p k u e", u=2, e=2),
                 in0=pairs.rearrange("p (u k e) -> p k u e", u=2, e=2),
                 in1=scale_col[:]
                 .rearrange("p (u e) -> p u e", e=2)
@@ -167,9 +168,7 @@ def tile_productkeysoftmemoryplus_t_kernel(
 
         def x_quant(q0, q1):
             cols = slice(256 * q0, 256 * q1)
-            room = x_rooms[(q0 // 2 - 1) % 3]
-            scaled = room[:, 2 * D * (q0 % 2) : 2 * D * (q0 % 2 + q1 - q0)]
-            quantise(x_codes[:, cols], x_scales[:, cols], scaled)
+            quantise(x_codes[:, cols], x_scales[:, cols], scaled(q0, q1))
 
         def mx_x(dst, n, codes, scales):
             cols = slice(P * n, P * (n + 1))
@@ -204,11 +203,6 @@ def tile_productkeysoftmemoryplus_t_kernel(
         base = [keep.tile([P, 4, N], F32, name="base%d" % j) for j in range(NGROUP)]
         ratio = [keep.tile([P, 4, N], F32, name="ratio%d" % j) for j in range(NGROUP)]
         e2_cd = [keep.tile([P, 4, 2, N], F32, name="e2_cd%d" % j) for j in range(NGROUP)]
-
-        rooms = [
-            keep.tile([P, 2 * SLOTS], F32, name="room%d" % r, align_bytes=64) for r in range(3)
-        ]
-
         first_b = keep.tile([P, 2, N], F32, name="first_b")
 
         def group_tiles(j):
@@ -270,7 +264,10 @@ def tile_productkeysoftmemoryplus_t_kernel(
                     )
 
         def ratios(j):
-            nc.scalar.activation(out=ratio[j][:], in_=state["gap", j][:], func=ACT.Exp)
+            first = 2 if j == 0 else 0
+            nc.scalar.activation(
+                out=ratio[j][:, first:, :], in_=state["gap", j][:, first:, :], func=ACT.Exp
+            )
 
         def denominators(j):
             zz = work.tile([P, 4 * H], F32, name="zz", bufs=2)
@@ -287,8 +284,8 @@ def tile_productkeysoftmemoryplus_t_kernel(
             nc.vector.reciprocal(out=rz[:], in_=state["zz", j][:])
             state["rz", j] = rz
 
-        def normalise(j):
-            for k in range(4 * H):
+        def normalise(j, s0=0, s1=4):
+            for k in range(H * s0, H * s1):
                 s, h = divmod(k, H)
                 nc.scalar.activation(
                     out=p1[j][:, s, h, :],
@@ -297,13 +294,19 @@ def tile_productkeysoftmemoryplus_t_kernel(
                     scale=state["rz", j][:, k : k + 1],
                 )
 
+        rooms = [
+            keep.tile([P, 2 * SLOTS], F32, name="room%d" % r, align_bytes=64) for r in range(3)
+        ]
         sums_of_two = [keep.tile([P, 2 * SLOTS], F32, name="two%d" % r) for r in range(2)]
 
         def p1_of(n, h):
             return p1[n // 4][:, n % 4, h, :]
 
         def terms(n, g, t):
-            return state.setdefault(("terms", n, g, t), [])
+            found = []
+            for rank in range(4):
+                found = found + state.get(("terms", n, g, t, rank), [])
+            return found
 
         def e2_to_psum(q, keys):
             e2 = bank(7, [4, 2, N], "e2_ps")
@@ -335,15 +338,21 @@ def tile_productkeysoftmemoryplus_t_kernel(
                 op=ALU.mult,
             )
 
-        def add_terms(planes, n, t0, t1, g0, g1):
+        def add_terms(rank, planes, n, t0, t1, g0, g1):
             for t in range(t0, t1):
                 for g in range(g0, g1):
-                    terms(n, g, t).append(planes[:, t - t0, P * (g - g0) : P * (g - g0 + 1)])
+                    plane = planes[:, t - t0, P * (g - g0) : P * (g - g0 + 1)]
+                    state.setdefault(("terms", n, g, t, rank), []).append(plane)
+
+        def rank_of(eng, n):
+            if n < 3:
+                return 1
+            return 0 if eng is nc.vector else 3
 
         def product_into(eng, room, n, h, t0, t1, g0, g1):
             planes = room.rearrange("p (t c) -> p t c", t=t1 - t0)
             product(eng, planes, n, h, t0, t1, 16 * g0, 16 * g1)
-            add_terms(planes, n, t0, t1, g0, g1)
+            add_terms(rank_of(eng, n), planes, n, t0, t1, g0, g1)
 
         def new_product(eng, name, bufs, n, h, t0, t1, g0, g1):
             pr = work.tile([P, P * (t1 - t0) * (g1 - g0)], F32, name=name, bufs=bufs)
@@ -361,12 +370,12 @@ def tile_productkeysoftmemoryplus_t_kernel(
         def scalar_half(n, h, g):
             pr = work.tile([P, 4, P], F32, name="pr_s", bufs=5)
             scalar_rows(pr[:], n, h, 16 * g, 16 * (g + 1), 16 * g)
-            add_terms(pr[:], n, 0, 4, g, g + 1)
+            add_terms(1, pr[:], n, 0, 4, g, g + 1)
 
         def shared_head(n):
-            pr = work.tile([P, SLOTS], F32, name="pr_g", bufs=2)
+            pr = work.tile([P, SLOTS], F32, name="pr_g", bufs=3)
             planes = pr[:].rearrange("p (t c) -> p t c", t=4)
-            add_terms(planes, n, 0, 4, 0, 2)
+            add_terms(3, planes, n, 0, 4, 0, 2)
             return planes
 
         def two_heads(n, i0=0, i1=N):
@@ -396,27 +405,20 @@ def tile_productkeysoftmemoryplus_t_kernel(
                 .broadcast_to([P, rows, N, 8]),
                 op=ALU.mult,
             )
-            for r in range(rows):
-                for g in range(2):
-                    first = 2 * P * r + P * g
-                    state["last", n0 + r // 4, g, r % 4] = room[:, first : first + P]
+            for s in range(n1 - n0):
+                planes = room[:, SLOTS * s : SLOTS * (s + 1)].rearrange("p (t c) -> p t c", t=4)
+                add_terms(0 if n0 + s == 2 else 2, planes, n0 + s, 0, 4, 0, 2)
 
-        def turn(k, gate=None, after=0):
+        def turn(k, between=None, after=0):
             n, g = divmod(k, 2)
             ub = bank(2 + k % 3, [4, P], "ub_ps")
             todo = []
-            for t in range(4):
-                if ("last", n, g, t) in state:
-                    place = 0 if n == 2 else len(terms(n, g, t))
-                    state["terms", n, g, t] = (
-                        terms(n, g, t)[:place] + [state["last", n, g, t]] + terms(n, g, t)[place:]
-                    )
             for r in range(len(terms(n, g, 0))):
                 for t in range(4):
                     todo.append((t, terms(n, g, t)[r]))
             for i, (t, term) in enumerate(todo):
-                if i == after and gate is not None:
-                    gate()
+                if i == after and between is not None:
+                    between()
                 nc.tensor.matmul(
                     ub[:, t, :],
                     lhsT=term,
@@ -453,12 +455,11 @@ def tile_productkeysoftmemoryplus_t_kernel(
             u = u_of(4 * q) if k0 == 0 else state["u", q][:, D * (k0 - 1) : D * (k1 - 1)]
             quantise(uc[:, cols], us[:, cols], u)
 
-        def memory(n, passes=(0, 1)):
-            if passes[0] == 0:
-                state["mem", n] = bank(MEM_BANKS.get(n, n % 2), [D], "mem")
-            mem = state["mem", n]
+        def memory(n):
+            mem = bank(LAST_MEM_BANKS.get(n, n % 2), [D], "mem")
+            state["mem", n] = mem
             uc, us = state["uc", n // 2]
-            for g in passes:
+            for g in range(2):
                 cols = slice(P * (2 * (n % 2) + g), P * (2 * (n % 2) + g + 1))
                 nc.tensor.matmul_mx(
                     out=mem[:],
@@ -499,83 +500,44 @@ def tile_productkeysoftmemoryplus_t_kernel(
             final(n, o)
             nc.sync.dma_start(out=out_view[:, n, :], in_=o)
 
-
-        last = NT - 1
-
-        def scalar_halves(n):
-            if n == 4:
-                return []
-            if n >= last - 1:
-                return [(HEAD_D, 0), (HEAD_C, 0), (HEAD_D, 1)]
-            return [(HEAD_D, 0)] if n % 2 == 0 else []
-
-        def vector_products(n):
-            if n >= last - 1:
-                new_product(nc.vector, "pr_c", 3, n, HEAD_C, 0, 4, 1, 2)
-                return
-            new_product(nc.vector, "pr_c", 3, n, HEAD_C, 0, 4, 0, 2)
-            if n % 2 == 0:
-                new_product(nc.vector, "pr_d", 3, n, HEAD_D, 0, 4, len(scalar_halves(n)), 2)
-
         def gates(q):
             gate_matmul(2 * q)
             gate_matmul(2 * q + 1)
 
         def cycle(c):
+            even, odd = 2 * c + 2, 2 * c + 3
+            j = (c + 3) // 2
             e2_to_psum(c + 1, 3 * N)
             memory(2 * c - 2)
-            if c == NPAIR - 2:
-                memory(2 * c - 1)
-            for h, g in scalar_halves(2 * c + 2)[:1]:
-                scalar_half(2 * c + 2, h, g)
+            if c > 1:
+                scalar_half(even, HEAD_D, 0)
+            shared = shared_head(odd)
+            scalar_rows(shared, odd, HEAD_D, 0, S_ROWS, 0)
             gate_silu(2 * c)
             gate_silu(2 * c + 1)
-            if c == NPAIR - 2:
-                gates(c + 1)
             gain(4 * c)
             gain(4 * c + 1)
-            if c < NPAIR - 2:
-                times_base(2 * c + 2, 2 * c + 4)
-                n = 2 * c + 3
-                shared = shared_head(n)
-                product(nc.gpsimd, shared[:, :, 8 * S_ROWS :], n, HEAD_D, 0, 4, S_ROWS, N)
-            else:
-                times_base(last - 1, last)
-                times_base(last, NT)
-            if c % 2 == 1 and (c + 3) // 2 < NGROUP:
-                reciprocals((c + 3) // 2)
-            for h, g in scalar_halves(2 * c + 2)[1:]:
-                scalar_half(2 * c + 2, h, g)
-            if c + 2 < NPAIR:
-                two_heads(2 * c + 4)
-                two_heads(2 * c + 5)
-            for h, g in scalar_halves(2 * c + 3):
-                scalar_half(2 * c + 3, h, g)
-            if c % 2 == 1 and (c + 3) // 2 < NGROUP:
-                normalise((c + 3) // 2)
-            vector_products(2 * c + 2)
+            times_base(even, odd + 1)
+            product(nc.gpsimd, shared[:, :, 8 * S_ROWS :], odd, HEAD_D, 0, 4, S_ROWS, N)
+            if c % 2 == 1 and j < NGROUP:
+                reciprocals(j)
+            two_heads(2 * c + 4)
+            two_heads(2 * c + 5)
+            if j < NGROUP:
+                normalise(j, 2 * ((c + 3) % 2), 2 * ((c + 3) % 2) + 2)
+            new_product(nc.vector, "pr_c", 3, even, HEAD_C, 0, 4, 0, 2)
+            new_product(nc.vector, "pr_d", 3, even, HEAD_D, 0, 4, 1 if c > 1 else 0, 2)
             turn(4 * c + 2)
-            if c < NPAIR - 2:
-                turn(4 * c + 3, lambda: memory(2 * c - 1), 4)
-            else:
-                turn(4 * c + 3)
-            if c == NPAIR - 2:
-                final_pair(c - 1)
+            turn(4 * c + 3, lambda: memory(2 * c - 1), 4)
             gain(4 * c + 2)
-            vector_products(2 * c + 3)
-            if c < NPAIR - 2:
-                scalar_rows(shared, 2 * c + 3, HEAD_D, 0, S_ROWS, 0)
+            new_product(nc.vector, "pr_c", 3, odd, HEAD_C, 0, 4, 0, 2)
             gain(4 * c + 3)
-            if c % 2 == 0 and (c + 4) // 2 < NGROUP:
-                denominators((c + 4) // 2)
-            if c < NPAIR - 2:
-                final_pair(c - 1)
+            if c % 2 == 0 and j + 1 < NGROUP:
+                denominators(j + 1)
+            final_pair(c - 1)
             u_quant(c, 0, 1)
             u_quant(c, 1, 4)
-            if c < NPAIR - 2:
-                turn(4 * c + 4, lambda: gates(c + 1), 8)
-            else:
-                turn(4 * c + 4)
+            turn(4 * c + 4, lambda: gates(c + 1), 8)
             turn(4 * c + 5)
 
         def floors(q):
@@ -583,22 +545,15 @@ def tile_productkeysoftmemoryplus_t_kernel(
             floor_base(2 * q + 1)
 
         def softmax_pair(q):
-            gap_to_base(2 * q)
-            gap_to_base(2 * q + 1)
+            if q > 0:
+                gap_to_base(2 * q)
+                gap_to_base(2 * q + 1)
             exps(2 * q)
             exps(2 * q + 1)
 
-        def early_half(k):
-            h, t0 = k // 2, 2 * (k % 2)
-            new_product(nc.gpsimd, "pr_early", 4, 0, h, t0, t0 + 2, 0, 2)
-
-        rows_done = [0]
-
-        def rows_up_to(total):
-            for i in range(rows_done[0], total):
+        def early_rows(first, end):
+            for i in range(first, end):
                 two_heads(2 + i // N, i % N, i % N + 1)
-            rows_done.append(total)
-            rows_done.remove(rows_done[0])
 
         widen_first_pair()
         widen_pair(1)
@@ -607,7 +562,7 @@ def tile_productkeysoftmemoryplus_t_kernel(
         x_transpose(1)
         widen_pair(2)
         widen_pair(3)
-        quantise(wk_codes[:], wk_scales[:], wk_il)
+        quantise(wk_codes[:], wk_scales[:], wk_il[:])
         x_scale_out(0)
         x_transpose(2)
         x_quant(0, 1)
@@ -634,15 +589,16 @@ def tile_productkeysoftmemoryplus_t_kernel(
         scores(3)
         widen_group(3)
         interleave(nc.gpsimd.tensor_copy, v_il[1], v_raw[1], 0, G_COLUMNS)
-        interleave(nc.scalar.copy, v_il[1], v_raw[1], G_COLUMNS, 384)
+        interleave(nc.scalar.copy, v_il[1], v_raw[1], G_COLUMNS, 2 * G_COLUMNS)
         softmax_pair(1)
         ratios(0)
+
         for j in range(2, NGROUP):
             x_scale_out(2 * j)
             if j > 2:
                 softmax_pair(2 * j - 3)
                 ratios(j - 2)
-                rows_up_to(EARLY_ROWS * (2 * j - 4))
+                early_rows(EARLY_ROWS * (2 * j - 5), EARLY_ROWS * (2 * j - 4))
             if j + 1 < NGROUP:
                 x_transpose(2 * j + 2)
             maxima(2 * j - 2)
@@ -659,32 +615,34 @@ def tile_productkeysoftmemoryplus_t_kernel(
             maxima(2 * j - 1)
             if j == 2:
                 reciprocals(0)
-                interleave(nc.scalar.copy, v_il[1], v_raw[1], 384, D)
+                interleave(nc.scalar.copy, v_il[1], v_raw[1], 2 * G_COLUMNS, D)
                 normalise(0)
             softmax_pair(2 * j - 2)
             if j == 4:
                 normalise(1)
-            rows_up_to(EARLY_ROWS * (2 * j - 3))
-            if j == NGROUP - 3:
-                e2_to_psum(0, 8 * N)
+            early_rows(EARLY_ROWS * (2 * j - 4), EARLY_ROWS * (2 * j - 3))
             x_quant(2 * j, 2 * j + 2)
             if j + 1 < NGROUP:
                 scores(2 * j)
                 scores(2 * j + 1)
+            if j == NGROUP - 3:
+                e2_to_psum(0, 8 * N)
             if j == 3:
                 quantise(wg_codes[:], wg_scales[:], wg_il[:])
             if j in (4, 5):
                 quantise(v_codes[:, j - 4, :], v_scales[:, j - 4, :], v_il[j - 4][:])
             if j + 2 < NGROUP:
                 widen_group(j + 2)
-                early_half(j - 2)
+                h, t0 = (j - 2) // 2, 2 * (j % 2)
+                new_product(nc.gpsimd, "pr_early", 4, 0, h, t0, t0 + 2, 0, 2)
             else:
                 h = j + 2 - NGROUP
                 product_into(nc.gpsimd, x_rooms[(j - 1) % 3][:].bitcast(F32), 1, h, 0, 4, 0, 2)
             if j == NGROUP - 2:
-                new_product(nc.gpsimd, "pr_g", 2, 0, HEAD_C, 2, 4, 0, 2)
+                new_product(nc.gpsimd, "pr_g", 3, 0, HEAD_C, 2, 4, 0, 2)
             floors(2 * j - 1)
-        def last_scores_first_gates():
+
+        def last_scores_first_gate():
             scores(NPAIR - 2)
             scores(NPAIR - 1)
             gate_matmul(0)
@@ -692,9 +650,9 @@ def tile_productkeysoftmemoryplus_t_kernel(
         new_product(nc.vector, "pr_c", 3, 0, HEAD_C, 0, 2, 0, 2)
         softmax_pair(NPAIR - 3)
         ratios(NGROUP - 2)
-        rows_up_to(4 * N)
+        early_rows(EARLY_ROWS * (2 * NGROUP - 5), 4 * N)
         new_product(nc.vector, "pr_d", 3, 0, HEAD_D, 0, 4, 0, 2)
-        turn(0, last_scores_first_gates, 12)
+        turn(0, last_scores_first_gate, 12)
         turn(1)
         new_product(nc.vector, "pr_c", 3, 1, HEAD_C, 0, 4, 0, 2)
         maxima(NPAIR - 2)
@@ -713,19 +671,51 @@ def tile_productkeysoftmemoryplus_t_kernel(
         gain(1)
         times_base(2, 4)
         new_product(nc.vector, "pr_d", 3, 2, HEAD_D, 0, 4, 0, 2)
-        new_product(nc.gpsimd, "pr_g", 2, 2, HEAD_C, 2, 4, 0, 2)
+        new_product(nc.gpsimd, "pr_g", 3, 2, HEAD_C, 2, 4, 0, 2)
         new_product(nc.vector, "pr_c", 3, 2, HEAD_C, 0, 2, 0, 2)
-        new_product(nc.gpsimd, "pr_g", 2, 3, HEAD_C, 0, 4, 0, 2)
+        new_product(nc.gpsimd, "pr_g", 3, 3, HEAD_C, 0, 4, 0, 2)
         gain(2)
         new_product(nc.vector, "pr_d", 3, 3, HEAD_D, 0, 4, 0, 2)
         gain(3)
         denominators(2)
         u_quant(0, 0, 1)
         u_quant(0, 1, 4)
-        turn(4, lambda: gates(1), 0)
+        turn(4, lambda: gates(1), 4)
         turn(5)
-        for c in range(1, NPAIR - 1):
+
+        for c in range(1, NPAIR - 2):
             cycle(c)
+
+        c = NPAIR - 2
+        last = NT - 1
+        e2_to_psum(c + 1, 3 * N)
+        memory(2 * c - 2)
+        memory(2 * c - 1)
+        scalar_half(last - 1, HEAD_D, 0)
+        gate_silu(2 * c)
+        gate_silu(2 * c + 1)
+        gates(c + 1)
+        gain(4 * c)
+        gain(4 * c + 1)
+        times_base(last - 1, last)
+        times_base(last, NT)
+        scalar_half(last - 1, HEAD_C, 0)
+        scalar_half(last - 1, HEAD_D, 1)
+        scalar_half(last, HEAD_D, 0)
+        scalar_half(last, HEAD_C, 0)
+        scalar_half(last, HEAD_D, 1)
+        new_product(nc.vector, "pr_c", 3, last - 1, HEAD_C, 0, 4, 1, 2)
+        turn(4 * c + 2)
+        turn(4 * c + 3)
+        final_pair(c - 1)
+        gain(4 * c + 2)
+        new_product(nc.vector, "pr_c", 3, last, HEAD_C, 0, 4, 1, 2)
+        gain(4 * c + 3)
+        u_quant(c, 0, 1)
+        u_quant(c, 1, 4)
+        turn(4 * c + 4)
+        turn(4 * c + 5)
+
         gate_silu(last - 1)
         gate_silu(last)
         turn(2 * last)

@@ -27,7 +27,8 @@ BASE, RATIO, HEAD_C, HEAD_D = 0, 1, 2, 3
 FLOOR = -80.0
 EARLY_ROWS = 10
 G_COLUMNS = 192
-S_ROWS = 9
+S_ROWS = 12
+S_EVEN = 13
 LAST_MEM_BANKS = {NT - 2: 7, NT - 1: 3}
 
 X_CHUNKS = [(0, 2), (2, 4), (4, 8), (8, 16), (16, 24), (24, 32)]
@@ -510,7 +511,10 @@ def tile_productkeysoftmemoryplus_t_kernel(
             e2_to_psum(c + 1, 3 * N)
             memory(2 * c - 2)
             if c > 1:
-                scalar_half(even, HEAD_D, 0)
+                pr = work.tile([P, SLOTS], F32, name="pr_d", bufs=3)
+                ev = pr[:].rearrange("p (t c) -> p t c", t=4)
+                add_terms(1, ev, even, 0, 4, 0, 2)
+                scalar_rows(ev, even, HEAD_D, 0, S_EVEN, 0)
             shared = shared_head(odd)
             scalar_rows(shared, odd, HEAD_D, 0, S_ROWS, 0)
             gate_silu(2 * c)
@@ -526,7 +530,10 @@ def tile_productkeysoftmemoryplus_t_kernel(
             if j < NGROUP:
                 normalise(j, 2 * ((c + 3) % 2), 2 * ((c + 3) % 2) + 2)
             new_product(nc.vector, "pr_c", 3, even, HEAD_C, 0, 4, 0, 2)
-            new_product(nc.vector, "pr_d", 3, even, HEAD_D, 0, 4, 1 if c > 1 else 0, 2)
+            if c > 1:
+                product(nc.vector, ev[:, :, 8 * S_EVEN :], even, HEAD_D, 0, 4, S_EVEN, N)
+            else:
+                new_product(nc.vector, "pr_d", 3, even, HEAD_D, 0, 4, 0, 2)
             turn(4 * c + 2)
             turn(4 * c + 3, lambda: memory(2 * c - 1), 4)
             gain(4 * c + 2)

@@ -27,8 +27,8 @@ BASE, RATIO, HEAD_C, HEAD_D = 0, 1, 2, 3
 FLOOR = -80.0
 EARLY_ROWS = 10
 G_COLUMNS = 192
-S_ROWS = 12
-S_EVEN = 13
+S_ROWS = 10
+S_EVEN = 15
 LAST_MEM_BANKS = {NT - 2: 7, NT - 1: 3}
 
 X_CHUNKS = [(0, 2), (2, 4), (4, 8), (8, 16), (16, 24), (24, 32)]
@@ -696,6 +696,7 @@ def tile_productkeysoftmemoryplus_t_kernel(
         c = NPAIR - 2
         last = NT - 1
         e2_to_psum(c + 1, 3 * N)
+        turn(4 * c + 2)
         memory(2 * c - 2)
         memory(2 * c - 1)
         scalar_half(last - 1, HEAD_D, 0)
@@ -712,10 +713,9 @@ def tile_productkeysoftmemoryplus_t_kernel(
         scalar_half(last, HEAD_C, 0)
         scalar_half(last, HEAD_D, 1)
         new_product(nc.vector, "pr_c", 3, last - 1, HEAD_C, 0, 4, 1, 2)
-        turn(4 * c + 2)
+        gain(4 * c + 2)
         turn(4 * c + 3)
         final_pair(c - 1)
-        gain(4 * c + 2)
         new_product(nc.vector, "pr_c", 3, last, HEAD_C, 0, 4, 1, 2)
         gain(4 * c + 3)
         u_quant(c, 0, 1)

@@ -53,7 +53,7 @@ def tile_productkeysoftmemoryplus_t_kernel(
             return tile
 
         x_rooms = [
-            keep.tile([P, 4 * D], BF16, name="x_room%d" % r, align_bytes=64) for r in range(3)
+            keep.tile([P, 4 * D], BF16, name="x_room%d" % r, align_bytes=256) for r in range(3)
         ]
 
         xraw = []
@@ -89,24 +89,27 @@ def tile_productkeysoftmemoryplus_t_kernel(
         load_x(5)
         nc.sync.dma_start(out=gain_sb[:], in_=slot_gain.rearrange("(g p t) -> p g t", p=P, t=4))
 
-        ident = keep.tile([P, P], F32, name="ident")
+        ident = keep.tile([P, P], F32, name="ident", align_bytes=256)
         make_identity(nc, ident[:])
 
-        x_codes = keep.tile([P, T], U32, name="x_codes", align_bytes=64)
-        x_scales = keep.tile([P, T], U8, name="x_scales", align_bytes=64)
-        wg_codes = keep.tile([P, D], U32, name="wg_codes", align_bytes=64)
-        wg_scales = keep.tile([P, D], U8, name="wg_scales", align_bytes=64)
-        wk_codes = keep.tile([P, C], U32, name="wk_codes", align_bytes=64)
-        wk_scales = keep.tile([P, C], U8, name="wk_scales", align_bytes=64)
-        v_codes = keep.tile([P, 2, D], U32, name="v_codes", align_bytes=64)
-        v_scales = keep.tile([P, 2, D], U8, name="v_scales", align_bytes=64)
+        x_codes = keep.tile([P, T], U32, name="x_codes", align_bytes=256)
+        x_scales = keep.tile([P, T], U8, name="x_scales", align_bytes=256)
+        wg_codes = keep.tile([P, D], U32, name="wg_codes", align_bytes=256)
+        wg_scales = keep.tile([P, D], U8, name="wg_scales", align_bytes=256)
+        wk_codes = keep.tile([P, C], U32, name="wk_codes", align_bytes=256)
+        wk_scales = keep.tile([P, C], U8, name="wk_scales", align_bytes=256)
+        v_codes = keep.tile([P, 2, D], U32, name="v_codes", align_bytes=256)
+        v_scales = keep.tile([P, 2, D], U8, name="v_scales", align_bytes=256)
 
         def quantise(codes, scales, interleaved):
             nc.vector.quantize_mx(out=codes.bitcast(FP8X4), scales=scales, in_=interleaved)
 
-        wg_il = keep.tile([P, 4 * D], BF16, name="wg_il", align_bytes=64)
-        v_il = [keep.tile([P, 4 * D], BF16, name="v_il%d" % g, align_bytes=64) for g in range(2)]
-        wk_il = keep.tile([P, 4 * C], BF16, name="wk_il", align_bytes=64)
+        rooms = [
+            keep.tile([P, 2 * SLOTS], F32, name="room%d" % r, align_bytes=256) for r in range(3)
+        ]
+        wg_il = rooms[0][:, 0:SLOTS].bitcast(BF16)
+        v_il = [keep.tile([P, 4 * D], BF16, name="v_il%d" % g, align_bytes=256) for g in range(2)]
+        wk_il = rooms[2][:, 0 : 2 * C].bitcast(BF16)
 
         def interleave(copy, dst, src, c0, c1):
             copy(
@@ -116,7 +119,7 @@ def tile_productkeysoftmemoryplus_t_kernel(
 
         def wk_copy():
             src = wk_raw[:].rearrange("p j (h a k) -> p a h k j", a=2, k=N)
-            dst = wk_il[:].rearrange("p (a h k j) -> p a h k j", a=2, k=N, j=4)
+            dst = wk_il.rearrange("p (a h k j) -> p a h k j", a=2, k=N, j=4)
             nc.vector.tensor_copy(out=dst[:, 0], in_=src[:, 0])
             nc.vector.tensor_copy(
                 out=dst[:, 1].rearrange("p h (t m) j -> p h t m j", t=4),
@@ -295,10 +298,9 @@ def tile_productkeysoftmemoryplus_t_kernel(
                     scale=state["rz", j][:, k : k + 1],
                 )
 
-        rooms = [
-            keep.tile([P, 2 * SLOTS], F32, name="room%d" % r, align_bytes=64) for r in range(3)
+        sums_of_two = [
+            keep.tile([P, 2 * SLOTS], F32, name="two%d" % r, align_bytes=256) for r in range(2)
         ]
-        sums_of_two = [keep.tile([P, 2 * SLOTS], F32, name="two%d" % r) for r in range(2)]
 
         def p1_of(n, h):
             return p1[n // 4][:, n % 4, h, :]
@@ -356,7 +358,8 @@ def tile_productkeysoftmemoryplus_t_kernel(
             add_terms(rank_of(eng, n), planes, n, t0, t1, g0, g1)
 
         def new_product(eng, name, bufs, n, h, t0, t1, g0, g1):
-            pr = work.tile([P, P * (t1 - t0) * (g1 - g0)], F32, name=name, bufs=bufs)
+            width = P * (t1 - t0) * (g1 - g0)
+            pr = work.tile([P, width], F32, name=name, bufs=bufs, align_bytes=256)
             product_into(eng, pr[:], n, h, t0, t1, g0, g1)
 
         def scalar_rows(planes, n, h, i0, i1, first):
@@ -369,12 +372,12 @@ def tile_productkeysoftmemoryplus_t_kernel(
                 )
 
         def scalar_half(n, h, g):
-            pr = work.tile([P, 4, P], F32, name="pr_s", bufs=5)
+            pr = work.tile([P, 4, P], F32, name="pr_s", bufs=5, align_bytes=256)
             scalar_rows(pr[:], n, h, 16 * g, 16 * (g + 1), 16 * g)
             add_terms(1, pr[:], n, 0, 4, g, g + 1)
 
         def shared_head(n):
-            pr = work.tile([P, SLOTS], F32, name="pr_g", bufs=3)
+            pr = work.tile([P, SLOTS], F32, name="pr_g", bufs=3, align_bytes=256)
             planes = pr[:].rearrange("p (t c) -> p t c", t=4)
             add_terms(3, planes, n, 0, 4, 0, 2)
             return planes
@@ -435,7 +438,7 @@ def tile_productkeysoftmemoryplus_t_kernel(
             if k % 4 == 0:
                 return rooms[(q + 2) % 3][:, SLOTS : SLOTS + D // 2].bitcast(BF16)
             if ("u", q) not in state:
-                state["u", q] = work.tile([P, 3 * D], BF16, name="u", align_bytes=64)
+                state["u", q] = work.tile([P, 3 * D], BF16, name="u", align_bytes=256)
             return state["u", q][:, D * (k % 4 - 1) : D * (k % 4)]
 
         def gain(k):
@@ -448,8 +451,8 @@ def tile_productkeysoftmemoryplus_t_kernel(
 
         def u_quant(q, k0, k1):
             if k0 == 0:
-                uc = work.tile([P, 4 * P], U32, name="uc", align_bytes=64)
-                us = work.tile([P, 4 * P], U8, name="us", align_bytes=64)
+                uc = work.tile([P, 4 * P], U32, name="uc", align_bytes=256)
+                us = work.tile([P, 4 * P], U8, name="us", align_bytes=256)
                 state["uc", q] = (uc, us)
             uc, us = state["uc", q]
             cols = slice(P * k0, P * k1)
@@ -511,7 +514,7 @@ def tile_productkeysoftmemoryplus_t_kernel(
             e2_to_psum(c + 1, 3 * N)
             memory(2 * c - 2)
             if c > 1:
-                pr = work.tile([P, SLOTS], F32, name="pr_d", bufs=3)
+                pr = work.tile([P, SLOTS], F32, name="pr_d", bufs=3, align_bytes=256)
                 ev = pr[:].rearrange("p (t c) -> p t c", t=4)
                 add_terms(1, ev, even, 0, 4, 0, 2)
                 scalar_rows(ev, even, HEAD_D, 0, S_EVEN, 0)
@@ -529,10 +532,10 @@ def tile_productkeysoftmemoryplus_t_kernel(
             two_heads(2 * c + 5)
             if j < NGROUP:
                 normalise(j, 2 * ((c + 3) % 2), 2 * ((c + 3) % 2) + 2)
-            new_product(nc.vector, "pr_c", 3, even, HEAD_C, 0, 4, 0, 2)
             if c > 1:
                 product(nc.vector, ev[:, :, 8 * S_EVEN :], even, HEAD_D, 0, 4, S_EVEN, N)
-            else:
+            new_product(nc.vector, "pr_c", 3, even, HEAD_C, 0, 4, 0, 2)
+            if c == 1:
                 new_product(nc.vector, "pr_d", 3, even, HEAD_D, 0, 4, 0, 2)
             turn(4 * c + 2)
             turn(4 * c + 3, lambda: memory(2 * c - 1), 4)
@@ -569,7 +572,7 @@ def tile_productkeysoftmemoryplus_t_kernel(
         x_transpose(1)
         widen_pair(2)
         widen_pair(3)
-        quantise(wk_codes[:], wk_scales[:], wk_il[:])
+        quantise(wk_codes[:], wk_scales[:], wk_il)
         x_scale_out(0)
         x_transpose(2)
         x_quant(0, 1)
@@ -635,7 +638,7 @@ def tile_productkeysoftmemoryplus_t_kernel(
             if j == NGROUP - 3:
                 e2_to_psum(0, 8 * N)
             if j == 3:
-                quantise(wg_codes[:], wg_scales[:], wg_il[:])
+                quantise(wg_codes[:], wg_scales[:], wg_il)
             if j in (4, 5):
                 quantise(v_codes[:, j - 4, :], v_scales[:, j - 4, :], v_il[j - 4][:])
             if j + 2 < NGROUP:

@@ -28,6 +28,7 @@ FLOOR = -80.0
 EARLY_ROWS = 10
 G_COLUMNS = 192
 S_ROWS = 10
+MIXED = range(3, NPAIR - 1)
 S_EVEN = 15
 LAST_MEM_BANKS = {NT - 2: 7, NT - 1: 3}
 
@@ -62,7 +63,10 @@ def tile_productkeysoftmemoryplus_t_kernel(
             xraw.append(xr)
         scale_col = keep.tile([P, 4], F32, name="scale_col")
         wg_raw = keep.tile([P, 4, D], BF16, name="wg_raw")
-        wk_raw = keep.tile([P, 4, C], BF16, name="wk_raw")
+        rooms = [
+            keep.tile([P, 2 * SLOTS], F32, name="room%d" % r, align_bytes=256) for r in range(3)
+        ]
+        wk_raw = rooms[1][:, 0 : 2 * C].bitcast(BF16).rearrange("p (j c) -> p j c", j=4)
         v_raw = [keep.tile([P, 4, D], BF16, name="v_raw%d" % g) for g in range(2)]
         gain_sb = keep.tile([P, 2, 4], BF16, name="gain_sb")
 
@@ -77,7 +81,7 @@ def tile_productkeysoftmemoryplus_t_kernel(
             )
 
         load_x(0)
-        nc.sync.dma_start(out=wk_raw[:], in_=wk.rearrange("(p j) c -> p j c", j=4))
+        nc.sync.dma_start(out=wk_raw, in_=wk.rearrange("(p j) c -> p j c", j=4))
         load_x(1)
         nc.sync.dma_start(out=scale_col[:], in_=x_scale.rearrange("o (p t) -> p (o t)", t=4))
         load_x(2)
@@ -104,9 +108,6 @@ def tile_productkeysoftmemoryplus_t_kernel(
         def quantise(codes, scales, interleaved):
             nc.vector.quantize_mx(out=codes.bitcast(FP8X4), scales=scales, in_=interleaved)
 
-        rooms = [
-            keep.tile([P, 2 * SLOTS], F32, name="room%d" % r, align_bytes=256) for r in range(3)
-        ]
         wg_il = rooms[0][:, 0:SLOTS].bitcast(BF16)
         v_il = [keep.tile([P, 4 * D], BF16, name="v_il%d" % g, align_bytes=256) for g in range(2)]
         wk_il = rooms[2][:, 0 : 2 * C].bitcast(BF16)
@@ -118,7 +119,7 @@ def tile_productkeysoftmemoryplus_t_kernel(
             )
 
         def wk_copy():
-            src = wk_raw[:].rearrange("p j (h a k) -> p a h k j", a=2, k=N)
+            src = wk_raw.rearrange("p j (h a k) -> p a h k j", a=2, k=N)
             dst = wk_il.rearrange("p (a h k j) -> p a h k j", a=2, k=N, j=4)
             nc.vector.tensor_copy(out=dst[:, 0], in_=src[:, 0])
             nc.vector.tensor_copy(
@@ -207,6 +208,7 @@ def tile_productkeysoftmemoryplus_t_kernel(
         base = [keep.tile([P, 4, N], F32, name="base%d" % j) for j in range(NGROUP)]
         ratio = [keep.tile([P, 4, N], F32, name="ratio%d" % j) for j in range(NGROUP)]
         e2_cd = [keep.tile([P, 4, 2, N], F32, name="e2_cd%d" % j) for j in range(NGROUP)]
+        mixed = keep.tile([P, len(MIXED), 3, N], F32, name="mixed")
         first_b = keep.tile([P, 2, N], F32, name="first_b")
 
         def group_tiles(j):
@@ -246,7 +248,14 @@ def tile_productkeysoftmemoryplus_t_kernel(
                 return base[j][:, s, :]
             if h == RATIO:
                 return first_b[:, s, :] if n < 2 else ratio[j][:, s, :]
+            if h == HEAD_C and n // 2 in MIXED:
+                return mixed[:, n // 2 - MIXED[0], 1 + n % 2, :]
             return e2_cd[j][:, s, h - HEAD_C, :]
+
+        def p1_of(n, h):
+            if h == HEAD_D and n % 2 == 0 and n // 2 in MIXED:
+                return mixed[:, n // 2 - MIXED[0], 0, :]
+            return p1[n // 4][:, n % 4, h, :]
 
         def exps(n):
             j, s = divmod(n, 4)
@@ -260,7 +269,7 @@ def tile_productkeysoftmemoryplus_t_kernel(
                     )
                 else:
                     nc.scalar.activation(
-                        out=e2_of(n, h) if half else p1[j][:, s, h, :],
+                        out=e2_of(n, h) if half else p1_of(n, h),
                         in_=sc[:, n % 2, N * c : N * (c + 1)],
                         func=ACT.Exp,
                         bias=nm[:, n % 2, c : c + 1],
@@ -292,8 +301,8 @@ def tile_productkeysoftmemoryplus_t_kernel(
             for k in range(H * s0, H * s1):
                 s, h = divmod(k, H)
                 nc.scalar.activation(
-                    out=p1[j][:, s, h, :],
-                    in_=p1[j][:, s, h, :],
+                    out=p1_of(4 * j + s, h),
+                    in_=p1_of(4 * j + s, h),
                     func=ACT.Copy,
                     scale=state["rz", j][:, k : k + 1],
                 )
@@ -301,9 +310,6 @@ def tile_productkeysoftmemoryplus_t_kernel(
         sums_of_two = [
             keep.tile([P, 2 * SLOTS], F32, name="two%d" % r, align_bytes=256) for r in range(2)
         ]
-
-        def p1_of(n, h):
-            return p1[n // 4][:, n % 4, h, :]
 
         def terms(n, g, t):
             found = []
@@ -325,15 +331,29 @@ def tile_productkeysoftmemoryplus_t_kernel(
             for s in range(4 - first):
                 state["e2_ps", 2 * q + s] = e2[:, s, :, :]
 
+        def mixed_to_psum(q):
+            both = bank(7, [3 * N], "e2_ps")
+            nc.tensor.matmul(
+                both[:, S_EVEN:],
+                lhsT=ident[:],
+                rhs=mixed[:, q - MIXED[0], :, :].rearrange("p a k -> p (a k)")[:, S_EVEN:],
+                start=True,
+                stop=True,
+            )
+            state["mixed_ps", q] = both
+
         def product(eng, dst, n, h, t0, t1, i0, i1):
-            if eng is nc.vector:
+            a, e2 = p1_of(n, h), e2_of(n, h)
+            if eng is nc.vector and n // 2 not in MIXED:
                 e2 = state["e2_ps", n][:, h - HEAD_C, :]
-            else:
-                e2 = e2_of(n, h)
+            elif eng is nc.vector and h == HEAD_C:
+                e2 = state["mixed_ps", n // 2][:, N * (1 + n % 2) : N * (2 + n % 2)]
+            elif eng is nc.vector:
+                a = state["mixed_ps", n // 2][:, 0:N]
             nt, ni = t1 - t0, i1 - i0
             eng.tensor_tensor(
                 out=dst.rearrange("p t (i m) -> p t i m", m=8),
-                in0=p1_of(n, h)[:, i0:i1].unsqueeze(1).unsqueeze(3).broadcast_to([P, nt, ni, 8]),
+                in0=a[:, i0:i1].unsqueeze(1).unsqueeze(3).broadcast_to([P, nt, ni, 8]),
                 in1=e2[:, 8 * t0 : 8 * t1]
                 .rearrange("p (t m) -> p t m", m=8)
                 .unsqueeze(2)
@@ -511,7 +531,10 @@ def tile_productkeysoftmemoryplus_t_kernel(
         def cycle(c):
             even, odd = 2 * c + 2, 2 * c + 3
             j = (c + 3) // 2
-            e2_to_psum(c + 1, 3 * N)
+            if c > 1:
+                mixed_to_psum(c + 1)
+            else:
+                e2_to_psum(c + 1, 3 * N)
             memory(2 * c - 2)
             if c > 1:
                 pr = work.tile([P, SLOTS], F32, name="pr_d", bufs=3, align_bytes=256)

from contextlib import ExitStack

import concourse.mybir as mybir
from concourse.masks import make_identity

F32 = mybir.dt.float32
BF16 = mybir.dt.bfloat16
U32 = mybir.dt.uint32
U8 = mybir.dt.uint8
FP8 = mybir.dt.float8_e4m3fn
FP8X4 = mybir.dt.float8_e4m3fn_x4
ACT = mybir.ActivationFunctionType
ALU = mybir.AluOpType
AX = mybir.AxisListType

T, D, H, N = 4096, 512, 4, 32
C = H * 2 * N
SLOTS = N * N
P = 128
NT = T // P
NPAIR = NT // 2
NGROUP = NT // 4

FLOPS = 2 * T * D * C + 2 * T * SLOTS * D + 2 * T * D * D

BASE, RATIO, HEAD_C, HEAD_D = 0, 1, 2, 3
FLOOR = -80.0
EARLY_ROWS = 10
G_COLUMNS = 192
S_ROWS = 10
MIXED = range(3, NPAIR - 1)
S_EVEN = 15
LAST_MEM_BANKS = {NT - 2: 7, NT - 1: 3}

X_CHUNKS = [(0, 2), (2, 4), (4, 8), (8, 16), (16, 24), (24, 32)]


def tile_productkeysoftmemoryplus_t_kernel(
    tc, x_bytes, x_scale, wk, slot_gain, values, wg, out
):
    nc = tc.nc
    x_view = x_bytes.rearrange("(p n) d -> p n d", n=NT)
    out_view = out.rearrange("(p n) d -> p n d", n=NT)

    with ExitStack() as ctx:
        keep = ctx.enter_context(tc.tile_pool(name="keep", bufs=1))
        work = ctx.enter_context(tc.tile_pool(name="work", bufs=2))
        psum = ctx.enter_context(tc.psum_pool(name="psum", bufs=1))
        ctx.enter_context(tc.manual_schedule())
        state = {}

        def bank(b, shape, name):
            tile = psum.tile([P] + shape, F32, name=name, tag="bank%d" % b, bufs=1)
            return tile

        x_rooms = [
            keep.tile([P, 4 * D], BF16, name="x_room%d" % r, align_bytes=256) for r in range(3)
        ]

        xraw = []
        for a, b in X_CHUNKS:
            xr = keep.tile([P, b - a, D], U8, name="xraw%d" % a, align_bytes=64)
            xraw.append(xr)
        scale_col = keep.tile([P, 4], F32, name="scale_col")
        wg_raw = keep.tile([P, 4, D], BF16, name="wg_raw")
        rooms = [
            keep.tile([P, 2 * SLOTS], F32, name="room%d" % r, align_bytes=256) for r in range(3)
        ]
        wk_raw = rooms[1][:, 0 : 2 * C].bitcast(BF16).rearrange("p (j c) -> p j c", j=4)
        v_raw = [keep.tile([P, 4, D], BF16, name="v_raw%d" % g) for g in range(2)]
        gain_sb = keep.tile([P, 2, 4], BF16, name="gain_sb")

        def load_x(i):
            a, b = X_CHUNKS[i]
            nc.sync.dma_start(out=xraw[i][:], in_=x_view[:, a:b, :])

        def load_values(g):
            nc.sync.dma_start(
                out=v_raw[g][:],
                in_=values[512 * g : 512 * (g + 1), :].rearrange("(p j) c -> p j c", j=4),
            )

        load_x(0)
        nc.sync.dma_start(out=wk_raw, in_=wk.rearrange("(p j) c -> p j c", j=4))
        load_x(1)
        nc.sync.dma_start(out=scale_col[:], in_=x_scale.rearrange("o (p t) -> p (o t)", t=4))
        load_x(2)
        nc.sync.dma_start(out=wg_raw[:], in_=wg.rearrange("(p j) c -> p j c", j=4))
        load_x(3)
        load_values(0)
        load_values(1)
        load_x(4)
        load_x(5)
        nc.sync.dma_start(out=gain_sb[:], in_=slot_gain.rearrange("(g p t) -> p g t", p=P, t=4))

        ident = keep.tile([P, P], F32, name="ident", align_bytes=256)
        make_identity(nc, ident[:])

        x_codes = keep.tile([P, T], U32, name="x_codes", align_bytes=256)
        x_scales = keep.tile([P, T], U8, name="x_scales", align_bytes=256)
        wg_codes = keep.tile([P, D], U32, name="wg_codes", align_bytes=256)
        wg_scales = keep.tile([P, D], U8, name="wg_scales", align_bytes=256)
        wk_codes = keep.tile([P, C], U32, name="wk_codes", align_bytes=256)
        wk_scales = keep.tile([P, C], U8, name="wk_scales", align_bytes=256)
        v_codes = keep.tile([P, 2, D], U32, name="v_codes", align_bytes=256)
        v_scales = keep.tile([P, 2, D], U8, name="v_scales", align_bytes=256)

        def quantise(codes, scales, interleaved):
            nc.vector.quantize_mx(out=codes.bitcast(FP8X4), scales=scales, in_=interleaved)

        wg_il = rooms[0][:, 0:SLOTS].bitcast(BF16)
        v_il = [keep.tile([P, 4 * D], BF16, name="v_il%d" % g, align_bytes=256) for g in range(2)]
        wk_il = rooms[2][:, 0 : 2 * C].bitcast(BF16)

        def interleave(copy, dst, src, c0, c1):
            copy(
                out=dst[:, 4 * c0 : 4 * c1].rearrange("p (c i j) -> p c j i", i=4, j=4),
                in_=src[:, :, c0:c1].rearrange("p j (c i) -> p c j i", i=4),
            )

        def wk_copy():
            src = wk_raw.rearrange("p j (h a k) -> p a h k j", a=2, k=N)
            dst = wk_il.rearrange("p (a h k j) -> p a h k j", a=2, k=N, j=4)
            nc.vector.tensor_copy(out=dst[:, 0], in_=src[:, 0])
            nc.vector.tensor_copy(
                out=dst[:, 1].rearrange("p h (t m) j -> p h t m j", t=4),
                in_=src[:, 1].rearrange("p h (m t) j -> p h t m j", t=4),
            )

        def raw_tiles(n0, n1):
            i = [k for k, (a, b) in enumerate(X_CHUNKS) if a <= n0 < b][0]
            rows = xraw[i][:, n0 - X_CHUNKS[i][0] : n1 - X_CHUNKS[i][0], :]
            return rows.rearrange("p s d -> p (s d)").bitcast(FP8)

        def widened(q):
            return x_rooms[q // 2 % 3][:, 2 * D * (q % 2) : 2 * D * (q % 2 + 1)]

        def widen_pair(q):
            nc.scalar.copy(out=widened(q), in_=raw_tiles(2 * q, 2 * q + 2))

        def widen_first_pair():
            nc.vector.tensor_copy(out=widened(0)[:, 0:D], in_=raw_tiles(0, 1))
            nc.scalar.copy(out=widened(0)[:, D:], in_=raw_tiles(1, 2))

        def widen_group(j):
            nc.gpsimd.tensor_copy(out=x_rooms[j % 3][:], in_=raw_tiles(4 * j, 4 * j + 4))

        def x_transpose(q):
            words = widened(q).bitcast(F32)
            xt = bank(q % 2, [2, 2, P], "xt")
            for s in range(2):
                for u in range(2):
                    nc.tensor.transpose(
                        xt[:, u, s, :], words[:, 256 * s + u : 256 * (s + 1) : 2], ident[:]
                    )
            state["xt", q] = xt

        def scaled(q0, q1):
            room = x_rooms[(q0 // 2 - 1) % 3]
            return room[:, 2 * D * (q0 % 2) : 2 * D * (q0 % 2 + q1 - q0)]

        def x_scale_out(q):
            pairs = state["xt", q][:].rearrange("p u s k -> p (u s k)").bitcast(BF16)
            nc.vector.tensor_tensor(
                out=scaled(q, q + 1).rearrange("p (k u e) -> p k u e", u=2, e=2),
                in0=pairs.rearrange("p (u k e) -> p k u e", u=2, e=2),
                in1=scale_col[:]
                .rearrange("p (u e) -> p u e", e=2)
                .unsqueeze(1)
                .broadcast_to([P, 2 * P, 2, 2]),
                op=ALU.mult,
            )

        def x_quant(q0, q1):
            cols = slice(256 * q0, 256 * q1)
            quantise(x_codes[:, cols], x_scales[:, cols], scaled(q0, q1))

        def mx_x(dst, n, codes, scales):
            cols = slice(P * n, P * (n + 1))
            nc.tensor.matmul_mx(
                out=dst,
                lhsT=x_codes[:, cols].bitcast(FP8X4),
                lhsT_scale=x_scales[:, cols],
                rhs=codes[:].bitcast(FP8X4),
                rhs_scale=scales[:],
                start=True,
                stop=True,
            )

        def scores(q):
            sc = bank(2 + (q + 4) % 5, [2, C], "sc_ps")
            for s in range(2):
                mx_x(sc[:, s, :], 2 * q + s, wk_codes, wk_scales)
            state["sc", q] = sc

        def maxima(q):
            nm = work.tile([P, 2, 2 * H], F32, name="nm", bufs=5)
            nc.vector.tensor_reduce(
                out=nm[:].rearrange("p s c -> p (s c)"),
                in_=state["sc", q][:].rearrange("p s (c k) -> p (s c) k", k=N),
                axis=AX.X,
                op=ALU.max,
                negate=True,
            )
            state["nm", q] = nm

        p1 = [keep.tile([P, 4, H, N], F32, name="p1_%d" % j) for j in range(NGROUP)]
        base = [keep.tile([P, 4, N], F32, name="base%d" % j) for j in range(NGROUP)]
        ratio = [keep.tile([P, 4, N], F32, name="ratio%d" % j) for j in range(NGROUP)]
        e2_cd = [keep.tile([P, 4, 2, N], F32, name="e2_cd%d" % j) for j in range(NGROUP)]
        mixed = keep.tile([P, len(MIXED), 3, N], F32, name="mixed")
        first_b = keep.tile([P, 2, N], F32, name="first_b")

        def group_tiles(j):
            state["low", j] = work.tile([P, 4, N], F32, name="low", bufs=3)
            state["gap", j] = work.tile([P, 4, N], F32, name="gap", bufs=3)
            state["z", j] = work.tile([P, 4, H, 2], F32, name="z", bufs=NGROUP)

        def floor_base(n):
            j, s = divmod(n, 4)
            if s == 0:
                group_tiles(j)
            c = H + BASE
            nc.vector.tensor_scalar(
                out=state["low", j][:, s, :],
                in0=state["sc", n // 2][:, n % 2, N * c : N * (c + 1)],
                scalar1=state["nm", n // 2][:, n % 2, c : c + 1],
                scalar2=FLOOR,
                op0=ALU.add,
                op1=ALU.max,
            )

        def gap_to_base(n):
            j, s = divmod(n, 4)
            c = H + RATIO
            nc.vector.scalar_tensor_tensor(
                out=state["gap", j][:, s, :],
                in0=state["sc", n // 2][:, n % 2, N * c : N * (c + 1)],
                scalar=state["nm", n // 2][:, n % 2, c : c + 1],
                in1=state["low", j][:, s, :],
                op0=ALU.add,
                op1=ALU.subtract,
            )

        def e2_of(n, h):
            j, s = divmod(n, 4)
            if h == BASE:
                return base[j][:, s, :]
            if h == RATIO:
                return first_b[:, s, :] if n < 2 else ratio[j][:, s, :]
            if h == HEAD_C and n // 2 in MIXED:
                return mixed[:, n // 2 - MIXED[0], 1 + n % 2, :]
            return e2_cd[j][:, s, h - HEAD_C, :]

        def p1_of(n, h):
            if h == HEAD_D and n % 2 == 0 and n // 2 in MIXED:
                return mixed[:, n // 2 - MIXED[0], 0, :]
            return p1[n // 4][:, n % 4, h, :]

        def exps(n):
            j, s = divmod(n, 4)
            sc, nm, z = state["sc", n // 2], state["nm", n // 2], state["z", j]
            for c in range(2 * H):
                half, h = divmod(c, H)
                total = z[:, s, h, half : half + 1]
                if c == H + BASE:
                    nc.scalar.activation(
                        out=e2_of(n, h), in_=state["low", j][:, s, :], func=ACT.Exp, accum_out=total
                    )
                else:
                    nc.scalar.activation(
                        out=e2_of(n, h) if half else p1_of(n, h),
                        in_=sc[:, n % 2, N * c : N * (c + 1)],
                        func=ACT.Exp,
                        bias=nm[:, n % 2, c : c + 1],
                        accum_out=total,
                    )

        def ratios(j):
            first = 2 if j == 0 else 0
            nc.scalar.activation(
                out=ratio[j][:, first:, :], in_=state["gap", j][:, first:, :], func=ACT.Exp
            )

        def denominators(j):
            zz = work.tile([P, 4 * H], F32, name="zz", bufs=2)
            nc.vector.tensor_reduce(
                out=zz[:],
                in_=state["z", j][:].rearrange("p s h a -> p (s h) a"),
                axis=AX.X,
                op=ALU.mult,
            )
            state["zz", j] = zz

        def reciprocals(j):
            rz = work.tile([P, 4 * H], F32, name="rz", bufs=NGROUP)
            nc.vector.reciprocal(out=rz[:], in_=state["zz", j][:])
            state["rz", j] = rz

        def normalise(j, s0=0, s1=4):
            for k in range(H * s0, H * s1):
                s, h = divmod(k, H)
                nc.scalar.activation(
                    out=p1_of(4 * j + s, h),
                    in_=p1_of(4 * j + s, h),
                    func=ACT.Copy,
                    scale=state["rz", j][:, k : k + 1],
                )

        sums_of_two = [
            keep.tile([P, 2 * SLOTS], F32, name="two%d" % r, align_bytes=256) for r in range(2)
        ]

        def terms(n, g, t):
            found = []
            for rank in range(4):
                found = found + state.get(("terms", n, g, t, rank), [])
            return found

        def e2_to_psum(q, keys):
            e2 = bank(7, [4, 2, N], "e2_ps")
            first = 2 * (q % 2)
            second = e2_cd[q // 2][:, first:, :, :].rearrange("p s h k -> p (s h k)")
            nc.tensor.matmul(
                e2[:].rearrange("p s h k -> p (s h k)")[:, 0:keys],
                lhsT=ident[:],
                rhs=second[:, 0:keys],
                start=True,
                stop=True,
            )
            for s in range(4 - first):
                state["e2_ps", 2 * q + s] = e2[:, s, :, :]

        def mixed_to_psum(q):
            both = bank(7, [3 * N], "e2_ps")
            nc.tensor.matmul(
                both[:, S_EVEN:],
                lhsT=ident[:],
                rhs=mixed[:, q - MIXED[0], :, :].rearrange("p a k -> p (a k)")[:, S_EVEN:],
                start=True,
                stop=True,
            )
            state["mixed_ps", q] = both

        def product(eng, dst, n, h, t0, t1, i0, i1):
            a, e2 = p1_of(n, h), e2_of(n, h)
            if eng is nc.vector and n // 2 not in MIXED:
                e2 = state["e2_ps", n][:, h - HEAD_C, :]
            elif eng is nc.vector and h == HEAD_C:
                e2 = state["mixed_ps", n // 2][:, N * (1 + n % 2) : N * (2 + n % 2)]
            elif eng is nc.vector:
                a = state["mixed_ps", n // 2][:, 0:N]
            nt, ni = t1 - t0, i1 - i0
            eng.tensor_tensor(
                out=dst.rearrange("p t (i m) -> p t i m", m=8),
                in0=a[:, i0:i1].unsqueeze(1).unsqueeze(3).broadcast_to([P, nt, ni, 8]),
                in1=e2[:, 8 * t0 : 8 * t1]
                .rearrange("p (t m) -> p t m", m=8)
                .unsqueeze(2)
                .broadcast_to([P, nt, ni, 8]),
                op=ALU.mult,
            )

        def add_terms(rank, planes, n, t0, t1, g0, g1):
            for t in range(t0, t1):
                for g in range(g0, g1):
                    plane = planes[:, t - t0, P * (g - g0) : P * (g - g0 + 1)]
                    state.setdefault(("terms", n, g, t, rank), []).append(plane)

        def rank_of(eng, n):
            if n < 3:
                return 1
            return 0 if eng is nc.vector else 3

        def product_into(eng, room, n, h, t0, t1, g0, g1):
            planes = room.rearrange("p (t c) -> p t c", t=t1 - t0)
            product(eng, planes, n, h, t0, t1, 16 * g0, 16 * g1)
            add_terms(rank_of(eng, n), planes, n, t0, t1, g0, g1)

        def new_product(eng, name, bufs, n, h, t0, t1, g0, g1):
            width = P * (t1 - t0) * (g1 - g0)
            pr = work.tile([P, width], F32, name=name, bufs=bufs, align_bytes=256)
            product_into(eng, pr[:], n, h, t0, t1, g0, g1)

        def scalar_rows(planes, n, h, i0, i1, first):
            for i in range(i0, i1):
                nc.scalar.activation(
                    out=planes[:, :, 8 * (i - first) : 8 * (i - first + 1)],
                    in_=e2_of(n, h).rearrange("p (t m) -> p t m", t=4),
                    func=ACT.Copy,
                    scale=p1_of(n, h)[:, i : i + 1],
                )

        def scalar_half(n, h, g):
            pr = work.tile([P, 4, P], F32, name="pr_s", bufs=5, align_bytes=256)
            scalar_rows(pr[:], n, h, 16 * g, 16 * (g + 1), 16 * g)
            add_terms(1, pr[:], n, 0, 4, g, g + 1)

        def shared_head(n):
            pr = work.tile([P, SLOTS], F32, name="pr_g", bufs=3, align_bytes=256)
            planes = pr[:].rearrange("p (t c) -> p t c", t=4)
            add_terms(3, planes, n, 0, 4, 0, 2)
            return planes

        def two_heads(n, i0=0, i1=N):
            two = sums_of_two[n // 2 % 2][:, SLOTS * (n % 2) : SLOTS * (n % 2 + 1)]
            planes = two.rearrange("p (t c) -> p t c", t=4)
            for i in range(i0, i1):
                nc.scalar.activation(
                    out=planes[:, :, 8 * i : 8 * (i + 1)],
                    in_=ratio[n // 4][:, n % 4, :].rearrange("p (t m) -> p t m", t=4),
                    func=ACT.Identity,
                    scale=p1_of(n, RATIO)[:, i : i + 1],
                    bias=p1_of(n, BASE)[:, i : i + 1],
                )

        def times_base(n0, n1):
            q, rows = n0 // 2, 4 * (n1 - n0)
            cols = slice(SLOTS * (n0 % 2), SLOTS * (n0 % 2 + n1 - n0))
            room = rooms[q % 3][:]
            if n1 - n0 == 1:
                room = room[:, SLOTS * (1 - n0 % 2) : SLOTS * (2 - n0 % 2)]
            factor = base[n0 // 4][:, n0 % 4 : n0 % 4 + n1 - n0, :]
            nc.gpsimd.tensor_tensor(
                out=room.rearrange("p (r i m) -> p r i m", r=rows, m=8),
                in0=sums_of_two[q % 2][:, cols].rearrange("p (r i m) -> p r i m", r=rows, m=8),
                in1=factor.rearrange("p s (t m) -> p (s t) m", m=8)
                .unsqueeze(2)
                .broadcast_to([P, rows, N, 8]),
                op=ALU.mult,
            )
            for s in range(n1 - n0):
                planes = room[:, SLOTS * s : SLOTS * (s + 1)].rearrange("p (t c) -> p t c", t=4)
                add_terms(0 if n0 + s == 2 else 2, planes, n0 + s, 0, 4, 0, 2)

        def turn(k, between=None, after=0):
            n, g = divmod(k, 2)
            ub = bank(2 + k % 3, [4, P], "ub_ps")
            todo = []
            for r in range(len(terms(n, g, 0))):
                for t in range(4):
                    todo.append((t, terms(n, g, t)[r]))
            for i, (t, term) in enumerate(todo):
                if i == after and between is not None:
                    between()
                nc.tensor.matmul(
                    ub[:, t, :],
                    lhsT=term,
                    rhs=ident[:],
                    start=(i == 0),
                    stop=(i == len(todo) - 1),
                    is_transpose=True,
                )
            state["ub", k] = ub

        def u_of(k):
            q = k // 4
            if k % 4 == 0:
                return rooms[(q + 2) % 3][:, SLOTS : SLOTS + D // 2].bitcast(BF16)
            if ("u", q) not in state:
                state["u", q] = work.tile([P, 3 * D], BF16, name="u", align_bytes=256)
            return state["u", q][:, D * (k % 4 - 1) : D * (k % 4)]

        def gain(k):
            nc.vector.tensor_tensor(
                out=u_of(k).rearrange("p (k t) -> p k t", t=4),
                in0=state["ub", k][:].rearrange("p t k -> p k t"),
                in1=gain_sb[:, k % 2, :].unsqueeze(1).broadcast_to([P, P, 4]),
                op=ALU.mult,
            )

        def u_quant(q, k0, k1):
            if k0 == 0:
                uc = work.tile([P, 4 * P], U32, name="uc", align_bytes=256)
                us = work.tile([P, 4 * P], U8, name="us", align_bytes=256)
                state["uc", q] = (uc, us)
            uc, us = state["uc", q]
            cols = slice(P * k0, P * k1)
            u = u_of(4 * q) if k0 == 0 else state["u", q][:, D * (k0 - 1) : D * (k1 - 1)]
            quantise(uc[:, cols], us[:, cols], u)

        def memory(n):
            mem = bank(LAST_MEM_BANKS.get(n, n % 2), [D], "mem")
            state["mem", n] = mem
            uc, us = state["uc", n // 2]
            for g in range(2):
                cols = slice(P * (2 * (n % 2) + g), P * (2 * (n % 2) + g + 1))
                nc.tensor.matmul_mx(
                    out=mem[:],
                    lhsT=uc[:, cols].bitcast(FP8X4),
                    lhsT_scale=us[:, cols],
                    rhs=v_codes[:, g, :].bitcast(FP8X4),
                    rhs_scale=v_scales[:, g, :],
                    start=(g == 0),
                    stop=(g == 1),
                )

        def gate_matmul(n):
            a_ps = bank((5 if n > 1 else 0) + n % 2, [D], "a_ps")
            mx_x(a_ps[:], n, wg_codes, wg_scales)
            state["a", n] = a_ps

        def gate_of(n):
            if n < NT - 2:
                room = rooms[n // 2 % 3][:]
            else:
                room = x_rooms[1][:].bitcast(F32)
            return room[:, D * (n % 2) : D * (n % 2 + 1)]

        def gate_silu(n):
            nc.scalar.activation(out=gate_of(n), in_=state["a", n][:], func=ACT.Silu)

        def final(n, o):
            nc.vector.tensor_tensor(out=o, in0=state["mem", n][:], in1=gate_of(n), op=ALU.mult)

        def final_pair(q):
            o = work.tile([P, 2, D], F32, name="o_pair")
            final(2 * q + 1, o[:, 1, :])
            final(2 * q, o[:, 0, :])
            nc.sync.dma_start(out=out_view[:, 2 * q : 2 * q + 2, :], in_=o[:])

        def final_tile(n):
            o = sums_of_two[1][:, D * (n % 4) : D * (n % 4 + 1)]
            final(n, o)
            nc.sync.dma_start(out=out_view[:, n, :], in_=o)

        def gates(q):
            gate_matmul(2 * q)
            gate_matmul(2 * q + 1)

        def cycle(c):
            even, odd = 2 * c + 2, 2 * c + 3
            j = (c + 3) // 2
            if c > 1:
                mixed_to_psum(c + 1)
            else:
                e2_to_psum(c + 1, 3 * N)
            memory(2 * c - 2)
            if c > 1:
                pr = work.tile([P, SLOTS], F32, name="pr_d", bufs=3, align_bytes=256)
                ev = pr[:].rearrange("p (t c) -> p t c", t=4)
                add_terms(1, ev, even, 0, 4, 0, 2)
                scalar_rows(ev, even, HEAD_D, 0, S_EVEN, 0)
            shared = shared_head(odd)
            scalar_rows(shared, odd, HEAD_D, 0, S_ROWS, 0)
            gate_silu(2 * c)
            gate_silu(2 * c + 1)
            gain(4 * c)
            gain(4 * c + 1)
            times_base(even, odd + 1)
            product(nc.gpsimd, shared[:, :, 8 * S_ROWS :], odd, HEAD_D, 0, 4, S_ROWS, N)
            if c % 2 == 1 and j < NGROUP:
                reciprocals(j)
            two_heads(2 * c + 4)
            two_heads(2 * c + 5)
            if j < NGROUP:
                normalise(j, 2 * ((c + 3) % 2), 2 * ((c + 3) % 2) + 2)
            if c > 1:
                product(nc.vector, ev[:, :, 8 * S_EVEN :], even, HEAD_D, 0, 4, S_EVEN, N)
            new_product(nc.vector, "pr_c", 3, even, HEAD_C, 0, 4, 0, 2)
            if c == 1:
                new_product(nc.vector, "pr_d", 3, even, HEAD_D, 0, 4, 0, 2)
            turn(4 * c + 2)
            turn(4 * c + 3, lambda: memory(2 * c - 1), 4)
            gain(4 * c + 2)
            new_product(nc.vector, "pr_c", 3, odd, HEAD_C, 0, 4, 0, 2)
            gain(4 * c + 3)
            if c % 2 == 0 and j + 1 < NGROUP:
                denominators(j + 1)
            final_pair(c - 1)
            u_quant(c, 0, 1)
            u_quant(c, 1, 4)
            turn(4 * c + 4, lambda: gates(c + 1), 8)
            turn(4 * c + 5)

        def floors(q):
            floor_base(2 * q)
            floor_base(2 * q + 1)

        def softmax_pair(q):
            if q > 0:
                gap_to_base(2 * q)
                gap_to_base(2 * q + 1)
            exps(2 * q)
            exps(2 * q + 1)

        def early_rows(first, end):
            for i in range(first, end):
                two_heads(2 + i // N, i % N, i % N + 1)

        widen_first_pair()
        widen_pair(1)
        wk_copy()
        x_transpose(0)
        x_transpose(1)
        widen_pair(2)
        widen_pair(3)
        quantise(wk_codes[:], wk_scales[:], wk_il)
        x_scale_out(0)
        x_transpose(2)
        x_quant(0, 1)
        scores(0)
        x_scale_out(1)
        x_transpose(3)
        x_quant(1, 2)
        maxima(0)
        scores(1)
        widen_group(2)
        interleave(nc.gpsimd.tensor_copy, v_il[0], v_raw[0], 0, G_COLUMNS)
        interleave(nc.scalar.copy, wg_il, wg_raw, 0, D)
        interleave(nc.scalar.copy, v_il[0], v_raw[0], G_COLUMNS, D)
        x_scale_out(2)
        x_transpose(4)
        floors(0)
        maxima(1)
        softmax_pair(0)
        x_scale_out(3)
        x_transpose(5)
        floors(1)
        x_quant(2, 4)
        scores(2)
        scores(3)
        widen_group(3)
        interleave(nc.gpsimd.tensor_copy, v_il[1], v_raw[1], 0, G_COLUMNS)
        interleave(nc.scalar.copy, v_il[1], v_raw[1], G_COLUMNS, 2 * G_COLUMNS)
        softmax_pair(1)
        ratios(0)

        for j in range(2, NGROUP):
            x_scale_out(2 * j)
            if j > 2:
                softmax_pair(2 * j - 3)
                ratios(j - 2)
                early_rows(EARLY_ROWS * (2 * j - 5), EARLY_ROWS * (2 * j - 4))
            if j + 1 < NGROUP:
                x_transpose(2 * j + 2)
            maxima(2 * j - 2)
            if j == 4:
                denominators(1)
            x_scale_out(2 * j + 1)
            if j == 2:
                denominators(0)
            if j + 1 < NGROUP:
                x_transpose(2 * j + 3)
            floors(2 * j - 2)
            if j == 4:
                reciprocals(1)
            maxima(2 * j - 1)
            if j == 2:
                reciprocals(0)
                interleave(nc.scalar.copy, v_il[1], v_raw[1], 2 * G_COLUMNS, D)
                normalise(0)
            softmax_pair(2 * j - 2)
            if j == 4:
                normalise(1)
            early_rows(EARLY_ROWS * (2 * j - 4), EARLY_ROWS * (2 * j - 3))
            x_quant(2 * j, 2 * j + 2)
            if j + 1 < NGROUP:
                scores(2 * j)
                scores(2 * j + 1)
            if j == NGROUP - 3:
                e2_to_psum(0, 8 * N)
            if j == 3:
                quantise(wg_codes[:], wg_scales[:], wg_il)
            if j in (4, 5):
                quantise(v_codes[:, j - 4, :], v_scales[:, j - 4, :], v_il[j - 4][:])
            if j + 2 < NGROUP:
                widen_group(j + 2)
                h, t0 = (j - 2) // 2, 2 * (j % 2)
                new_product(nc.gpsimd, "pr_early", 4, 0, h, t0, t0 + 2, 0, 2)
            else:
                h = j + 2 - NGROUP
                product_into(nc.gpsimd, x_rooms[(j - 1) % 3][:].bitcast(F32), 1, h, 0, 4, 0, 2)
            if j == NGROUP - 2:
                new_product(nc.gpsimd, "pr_g", 3, 0, HEAD_C, 2, 4, 0, 2)
            floors(2 * j - 1)

        def last_scores_first_gate():
            scores(NPAIR - 2)
            scores(NPAIR - 1)
            gate_matmul(0)

        new_product(nc.vector, "pr_c", 3, 0, HEAD_C, 0, 2, 0, 2)
        softmax_pair(NPAIR - 3)
        ratios(NGROUP - 2)
        early_rows(EARLY_ROWS * (2 * NGROUP - 5), 4 * N)
        new_product(nc.vector, "pr_d", 3, 0, HEAD_D, 0, 4, 0, 2)
        turn(0, last_scores_first_gate, 12)
        turn(1)
        new_product(nc.vector, "pr_c", 3, 1, HEAD_C, 0, 4, 0, 2)
        maxima(NPAIR - 2)
        maxima(NPAIR - 1)
        floors(NPAIR - 2)
        floors(NPAIR - 1)
        softmax_pair(NPAIR - 2)
        softmax_pair(NPAIR - 1)
        ratios(NGROUP - 1)
        new_product(nc.vector, "pr_d", 3, 1, HEAD_D, 0, 4, 0, 2)
        turn(2, lambda: gate_matmul(1), 0)
        gate_silu(0)
        gate_silu(1)
        gain(0)
        turn(3)
        gain(1)
        times_base(2, 4)
        new_product(nc.vector, "pr_d", 3, 2, HEAD_D, 0, 4, 0, 2)
        new_product(nc.gpsimd, "pr_g", 3, 2, HEAD_C, 2, 4, 0, 2)
        new_product(nc.vector, "pr_c", 3, 2, HEAD_C, 0, 2, 0, 2)
        new_product(nc.gpsimd, "pr_g", 3, 3, HEAD_C, 0, 4, 0, 2)
        gain(2)
        new_product(nc.vector, "pr_d", 3, 3, HEAD_D, 0, 4, 0, 2)
        gain(3)
        denominators(2)
        u_quant(0, 0, 1)
        u_quant(0, 1, 4)
        turn(4, lambda: gates(1), 4)
        turn(5)

        for c in range(1, NPAIR - 2):
            cycle(c)

        c = NPAIR - 2
        last = NT - 1
        e2_to_psum(c + 1, 3 * N)
        turn(4 * c + 2)
        memory(2 * c - 2)
        memory(2 * c - 1)
        scalar_half(last - 1, HEAD_D, 0)
        gate_silu(2 * c)
        gate_silu(2 * c + 1)
        gates(c + 1)
        gain(4 * c)
        gain(4 * c + 1)
        times_base(last - 1, last)
        times_base(last, NT)
        scalar_half(last - 1, HEAD_C, 0)
        scalar_half(last - 1, HEAD_D, 1)
        scalar_half(last, HEAD_D, 0)
        scalar_half(last, HEAD_C, 0)
        scalar_half(last, HEAD_D, 1)
        new_product(nc.vector, "pr_c", 3, last - 1, HEAD_C, 0, 4, 1, 2)
        gain(4 * c + 2)
        turn(4 * c + 3)
        final_pair(c - 1)
        new_product(nc.vector, "pr_c", 3, last, HEAD_C, 0, 4, 1, 2)
        gain(4 * c + 3)
        u_quant(c, 0, 1)
        u_quant(c, 1, 4)
        turn(4 * c + 4)
        turn(4 * c + 5)

        gate_silu(last - 1)
        gate_silu(last)
        turn(2 * last)
        gain(2 * last - 2)
        turn(2 * last + 1)
        gain(2 * last - 1)
        memory(last - 3)
        memory(last - 2)
        u_quant(NPAIR - 1, 0, 1)
        gain(2 * last)
        u_quant(NPAIR - 1, 1, 2)
        gain(2 * last + 1)
        memory(last - 1)
        final_tile(last - 3)
        u_quant(NPAIR - 1, 2, 4)
        memory(last)
        final_tile(last - 2)
        final_tile(last - 1)
        final_tile(last)
